import numpy as np, ml_dtypes
CORES = [13,21,141,149]
N = 4
BF = ml_dtypes.bfloat16
def gentries(a):
    return np.ascontiguousarray(a.reshape(8, 16, -1).transpose(0, 2, 1)).reshape(8, -1)
def gtable(e):
    e = np.asarray(e); return np.ascontiguousarray(e.reshape(8, -1, 16).transpose(0, 2, 1)).reshape(128, -1).astype(np.int32)
V, C, S, RO = 2048, 512, 256, 3
Q, B = 8, 64
def parts(rng):
    X = rng.integers(0, 160, (N, 8, 16, V)) + 96 * rng.integers(0, 2, (N, 8, 1, V))
    p = rng.integers(0, 160, (N, 8, 16, S)) + 96 * rng.integers(0, 2, (N, 8, 1, S))
    return X, rng.integers(0, V, (N, 8, 16, C)), rng.integers(0, V, (N, 8, 16, S)), p, rng.integers(0, C, (N, 8, S))
def pack(X, K, M, p, c):
    return {"tx": np.ascontiguousarray(X.reshape(N, 128, V)).astype(BF), "kt": np.ascontiguousarray(K.reshape(N, 128, C)).astype(np.int32),
            "ms": np.ascontiguousarray(M.reshape(N, 128, S)).astype(np.int32), "z": np.ascontiguousarray(p.reshape(N, 128, S)).astype(BF), "cp": np.stack([gtable(a) for a in c])}
def setup_inputs(rng):
    return pack(*parts(rng))
def setup_inputs_spread(rng):
    X, K, M, p, c = parts(rng)
    X = np.minimum((np.exp2(8 * rng.random((N, 8, 1, V))) * rng.random((N, 8, 16, V))).astype(np.int64), 255)
    p = np.minimum((np.exp2(8 * rng.random((N, 8, 1, S))) * rng.random((N, 8, 16, S))).astype(np.int64), 255)
    K = np.minimum((V * rng.random((N, 8, 16, C)) ** 3).astype(np.int64), V - 1)
    M = np.minimum((V * rng.random((N, 8, 16, S)) ** 2).astype(np.int64), V - 1)
    c = np.minimum((C * rng.random((N, 8, S)) ** 2).astype(np.int64), C - 1)
    return pack(X, K, M, p, c)
def setup_inputs_ends(rng):
    half = (np.arange(16) >> 3)[:, None]
    X = 255 * rng.integers(0, 2, (N, 8, 16, V)); lo = 255 * rng.integers(0, 2, (N, 8, 1)); lo[:, 0] = 0; lo[:, 7] = 0
    for g in (0, 2, 4, 7):
        X[:, g, :, 0] = lo[:, g]; X[:, g, :, V - 1] = 255 - lo[:, g]
    p = 255 * rng.integers(0, 2, (N, 8, 16, S)); r = rng.integers(0, 4, (N, 8, 1, S)); p = np.where(r == 0, 0, np.where(r == 1, 255, p))
    K = rng.integers(0, 2, (N, 8, 16, C)); r = rng.integers(0, 5, (N, 8, 1, C))
    K = (V - 1) * np.where(r == 0, half, np.where(r == 1, 1 - half, np.where(r == 2, K[:, :, :1], K)))
    M = rng.integers(0, 2, (N, 8, 16, S)); r = rng.integers(0, 5, (N, 8, 1, S))
    M = (V - 1) * np.where(r == 0, half, np.where(r == 1, 1 - half, np.where(r == 2, M[:, :, :1], M)))
    c = np.where(rng.random((N, 8, S)) < 0.75, (C - 1) * rng.integers(0, 2, (N, 8, S)), rng.integers(0, C, (N, 8, S)))
    K[:, 7, :, C - 1] = V - 1; K[:, 0, :8, C - 1] = V - 1; K[:, 0, 8:, C - 1] = 0
    for g in (0, 7):
        for i in (0, 1, S - 1):
            p[:, g, :, i] = 0; c[:, g, i] = C - 1; M[:, g, :, i] = 0
        for i in (3, S - 5):
            p[:, g, :, i] = 0; c[:, g, i] = C - 1; M[:, g, :8, i] = 0; M[:, g, 8:, i] = V - 1
        for i in (2, S - 2):
            p[:, g, :, i] = 0; c[:, g, i] = C - 1; M[:, g, :, i] = V - 1
        for i in (4, S - 3):
            p[:, g, :, i] = 255; c[:, g, i] = C - 1; M[:, g, :, i] = 0
        for i in (5, S - 4):
            p[:, g, :, i] = 255; c[:, g, i] = C - 1; M[:, g, :8, i] = V - 1; M[:, g, 8:, i] = 0
    return pack(X, K, M, p, c)
def setup_inputs_corners(rng):
    X, K, M, p, c = parts(rng)
    c = rng.choice(np.array([0, 1, C // 2 - 1, C // 2, C - 2, C - 1]), (N, 8, S)); c[:, ::2] = (C - 1) * rng.integers(0, 2, (N, 4, S))
    X[:, 2] = rng.integers(0, 4, (N, 16, V)); p[:, 2] = rng.integers(0, 4, (N, 16, S))
    X[:, 5] = 8 * rng.integers(0, 32, (N, 16, V)); p[:, 5] = 8 * rng.integers(0, 32, (N, 16, S)); c[:, 5] = rng.integers(0, C, (N, S))
    K[:, 0] = rng.choice(np.array([0, 1, V - 1]), (N, 16, C)); M[:, 0, :, ::2] = 0; M[:, 0, :, 1::2] = V - 1
    M[:, 1] = Q * np.arange(S) + np.arange(16)[:, None] % Q
    M[:, 3] = np.take_along_axis(K[:, 3], c[:, 3][:, None, :], 2)
    K[:, 4] = K[:, 4, :1].copy(); M[:, 4, :, ::2] = M[:, 4, :1, ::2].copy()
    K[:, 6, 8:] = K[:, 6, :8].copy()
    kc = np.take_along_axis(K[:, 6, :1], c[:, 6][:, None, :], 2); near = np.take_along_axis(X[:, 6], kc, 2); p[:, 6, :, ::3] = near[:, :, ::3]
    p[:, 7] = np.take_along_axis(X[:, 7], M[:, 7, :1], 2)
    return pack(X, K, M, p, c)
def setup_inputs_crowd(rng):
    X, K, M, p, c = parts(rng); far1 = Q * B + 1
    for q in range(N):
        for g in range(7):
            o = rng.permutation(V)
            if g == 4:
                j = int(np.flatnonzero(o == far1)[0]); o[j] = o[B]; o[B] = far1
                X[q, g, :, far1] = 255 * (q & 1); X[q, g, 0, far1 + 1] = 0
                X[q, g, :, far1 + 2] = X[q, g, :, far1 + 1]; X[q, g, 0, far1 + 2] = S - 1
            own, far = o[:S], o[S:]
            M[q, g] = own[None, :]; p[q, g] = np.minimum(X[q, g][:, own] + rng.integers(0, 8, (16, S)), 255)
            two = rng.permutation(C)[:2]
            if g == 3: two = np.array([C - 1, C - 1])
            if g == 4:
                two = 1 + rng.permutation(C - 1)[:2]
                p[q, g, :, B] = X[q, g, :, far1]; K[q, g, :8, 0] = far1 + 1; K[q, g, 8:, 0] = far1 + 2
            if g in (2, 6):
                c[q, g] = two[rng.integers(0, 2, S)]; K[q, g, :, two[0]] = far[:16]; K[q, g, :, two[1]] = far[16:32]
            else:
                c[q, g] = two[0]; K[q, g, :, two[0]] = np.concatenate([far[:8], far[:8]])
            if g in (1, 5):
                i = 0 if g == 1 else S - 1
                M[q, g, :, i] = K[q, g, :, two[0]]
        full, near, home = [int(v) for v in rng.permutation(V)[:3]]
        X[q, 7, :, full] = 255; X[q, 7, :, near] = 255; X[q, 7, int(rng.integers(0, 16)), near] = 254; X[q, 7, :, home] = rng.integers(0, 8, 16)
        c[q, 7] = rng.integers(1, C // 2 - 1, S) + (C // 2) * rng.integers(0, 2, S)
        for i in (0, S - 2, S - 1): p[q, 7, :, i] = 0
        c[q, 7, 0] = 0; M[q, 7, :, 0] = home; K[q, 7, :8, 0] = full; K[q, 7, 8:, 0] = near
        c[q, 7, S - 1] = C - 1; M[q, 7, :, S - 1] = home; K[q, 7, :8, C - 1] = near; K[q, 7, 8:, C - 1] = full
        c[q, 7, S - 2] = C // 2; M[q, 7, :, S - 2] = near; M[q, 7, 0, S - 2] = full; K[q, 7, :, C // 2] = home
    return pack(X, K, M, p, c)
def check_inputs(d):
    bad = []
    for k, hi in (("tx", 255), ("kt", V - 1), ("ms", V - 1), ("z", 255), ("cp", C - 1)):
        v = np.asarray(d[k]).astype(np.float64)
        if not (np.min(v) >= 0 and np.max(v) <= hi): bad.append("range of " + k)
        elif np.any(v != np.floor(v)): bad.append("whole numbers of " + k)
    return bad
def mixed(p):
    return np.add.reduce(p * (2 * np.arange(16) + 1)[:, None], axis=-2)
def travel(v):
    w = v.reshape(v.shape[:-1] + (N, B)); o = np.empty_like(w)
    for h in range(N): o[..., (h + 1) % N, :] = np.roll(w[..., h, :], h, axis=0)
    return o.reshape(v.shape)
def reference(tx, kt, ms, z, cp):
    X = tx.astype(np.float32).astype(np.int64).reshape(N, 8, 16, V); K = kt.astype(np.int64).reshape(N, 8, 16, C); M = ms.astype(np.int64).reshape(N, 8, 16, S)
    p = z.astype(np.float32).astype(np.int64).reshape(N, 8, 16, S); c = np.stack([gentries(a) for a in cp]).astype(np.int64)
    A = np.zeros((N, 8), np.int64); row = np.arange(16)[:, None]; slot = np.arange(S)
    for rnd in range(RO):
        kc = np.take_along_axis(K, c[:, :, None, :], 3)
        x = np.take_along_axis(X, kc.reshape(N, 8, 1, 16 * S), 3).reshape(N, 8, 16, 16, S)
        m = np.take_along_axis(X, M.reshape(N, 8, 1, 16 * S), 3).reshape(N, 8, 16, 16, S)
        d = np.add.reduce(np.abs(x - p[:, :, :, None, :]), axis=2); dm = np.add.reduce(np.abs(m - p[:, :, :, None, :]), axis=2)
        s0, s1 = np.add.reduce(d[:, :, :8], axis=2), np.add.reduce(d[:, :, 8:], axis=2)
        t0, t1 = np.add.reduce(dm[:, :, :8], axis=2), np.add.reduce(dm[:, :, 8:], axis=2)
        b = (s1 < s0).astype(np.int64); e = np.argmin(dm, axis=2); a = np.argmax(d, axis=2)
        db = np.where(b[:, :, None, :] == 1, d[:, :, 8:], d[:, :, :8]); w = 8 * b + np.argmin(db, axis=2)
        trust = np.abs(s1 - s0) >= np.abs(t1 - t0) + 8 * A[:, :, None]
        contra = trust & (np.min(dm, axis=2) < np.min(db, axis=2)); agree = trust & ~contra
        me = np.take_along_axis(m, e[:, :, None, None, :], 3)[:, :, :, 0]; xw = np.take_along_axis(x, w[:, :, None, None, :], 3)[:, :, :, 0]
        name = np.take_along_axis(M, e[:, :, None, :], 2)[:, :, 0]; u = mixed(p)
        take = agree[:, :, None, :] & ((row >> 3) == b[:, :, None, :]) & (d < dm)
        fresh = ~trust[:, :, None, :] & (16 * dm > (t0 + t1)[:, :, None, :])
        M = np.where(take, kc, np.where(fresh, (kc + u[:, :, None, :] + 37 * row) & (V - 1), M))
        t = (2 * c + 1 - b) & (C - 1)
        for q in range(N):
            for g in range(8):
                i = np.flatnonzero(contra[q, g]); col, first = np.unique(t[q, g, i], return_index=True); i = i[first]
                K[q, g, a[q, g, i], col] = name[q, g, i]
        p = np.where(agree[:, :, None, :], (p + xw) >> 1, np.abs(p - me)); u = mixed(p)
        own = np.repeat((Q * slot + (u & (Q - 1)))[:, :, None, :], 16, axis=2)
        np.put_along_axis(X, own, (np.take_along_axis(X, own, 3) + p) >> 1, 3)
        if rnd < RO - 1:
            A = np.add.reduce(contra.astype(np.int64), axis=2)
            c = np.where(agree, (2 * c + b) & (C - 1), u & (C - 1))
            p = travel(p); M = travel(M); c = travel(c)
    return {"ytx": X.reshape(N, 128, V).astype(BF), "ykt": K.reshape(N, 128, C).astype(np.float32), "yms": M.reshape(N, 128, S).astype(np.float32), "yz": p.reshape(N, 128, S).astype(BF)}

@@ -1,0 +1,836 @@
+from concourse.bass import DstId, RemoteDMATransfer
+from concourse.mybir import AluOpType as A, AxisListType, ActivationFunctionType as F
+
+N, RO = 4, 3
+H = "float16"
+U = 2.0 ** -24
+SU = 2.0 ** -16
+CFG = {"oh": "SSS", "ohl": "SVS", "zg": 8, "zs": 0, "rs": 640, "h0": 4, "h1": 6, "hv": 5, "xabs": False, "ex2": "VVV"}
+
+SCRATCH = {}
+
+
+def _decl(where, dtype, spec):
+    for item in spec.split():
+        name, shape = item.split(":")
+        SCRATCH[name] = (where, [128] + [int(v) for v in shape.split("x")], dtype)
+
+
+F16 = "df nf thr nthr ts ts2 tT Tt a8 m1 win nt P tA tB tC tD sd ek".split()
+I16 = "wi32 ix ai a15 uq ow c2 c2a u9 im vv ci ui".split()
+_decl("sbuf", "bfloat16", "X:2048 zi:768 zo:768 W:8192 R:4096 G:4096 ZR:8192 "
+      "I:128 nI:128 BO:128 E:528 H0:528 H1:528 EA:16 um:256 Rx:64 Wu:128 irow:128 irw:128 one:128 "
+      "xa:32x16 xb:32x16 xk:32x16 mb:32x16 crow:16 srow:512 arow:16 aw:128 rr:256 hz:64 ltb:256 c2b:256 oa:256 Fw:32 "
+      "oh:768 L1:256 L2:256 Oh:512 t0:512 t1:512 r8:288 r16:256 ra:288 ru:256")
+_decl("sbuf", H, "If:128 nIf:128 BOf:128 onef:128 vrow:128 drow:128 Mf:256 kcf:256 p1m:256 p2:256 EM:256")
+_decl("sbuf", "float32", "K:528 Mof:256 pm:8 sel8:8 hm:64 xs:288 msn:256 kxs:288 "
+      "asn:288 kms:256 tt:32 pf:304 bad:32 cand:32 hs:64 ex:256 ex2:256 nkx:256 tbc:256 g1:256 sx:256 us:256 ry:256 Kt:256 "
+      "nIq:128 Q:256 Wd:272 tb:512 tg:128 rc:64 ra2:64 om:32 wc:2 wi:4 sl:4 s1:16 s2:16")
+_decl("sbuf", "int32", "Ki:512 pn:208 o8:48 si:256 sh:256 li:48 l4:32 oi:32")
+_decl("sbuf", "uint16", "Mu:768 Mo:512 cu:48 co:32 kcu:256 b16:16 dl:8 il:16 ol:16 el:32 tl:16 wl:32")
+_decl("psum", "float32", "BX:32x16 BM:32x16 D0:512 D1:512 BA:512 BB:512 BL:512 BK:512")
+
+MSGS = [k + str(r) for r in (1, 2) for k in "zMc"]
+SEMAPHORES = ["V", "S", "P", "C", "sent"] + ["d%d" % i for i in range(26)] + [m + "l%d" % l for m in MSGS for l in range(N)]
+
+
+def piece(T, kind, side, r, l0=0, n=N):
+    w = 4 if kind == "c" else 64
+    b = T[{"z": ("zi", "zo"), "M": ("Mu", "Mo"), "c": ("cu", "co")}[kind][side]]
+    return b[:, w * (N * r + l0):w * (N * r + l0 + n)]
+
+
+def block(l, r):
+    return (l // 2 + 2 * (l % 2) + r) % N
+
+
+def home(r):
+    return [l for l in range(N) if block(l, r) == 0][0]
+
+
+def routes(T, topo, rank, r):
+    me, out, used = T.cores[rank], [], []
+    for l in range(N):
+        h = block(l, r - 1)
+        if h == 0:
+            continue
+        dst = T.cores[(rank + h) % N]
+        if topo.may_write(me, dst):
+            out.append((l, dst, None))
+            continue
+        can = [c for c in topo.cores_of(me) if c != me and T.rank_of(c) is None and topo.may_write(c, dst) and c not in used]
+        can.sort(key=lambda c: topo.die(c) != topo.die(me))
+        used.append(can[0])
+        out.append((l, dst, can[0]))
+    return out
+
+
+def engine_split(topo, me, rt):
+    off = 0
+    for l, dst, via in rt:
+        if via is None:
+            off |= topo.mask(me, dst)
+    vias = [x[0] for x in rt if x[2] is not None]
+    res = {}
+    for l, dst, via in rt:
+        if via is None:
+            res[l] = topo.engines(me, dst)
+        else:
+            free = [e for e in topo.engines(me, via) if not off >> e & 1]
+            n = len(free) // len(vias)
+            res[l] = free[vias.index(l) * n:(vias.index(l) + 1) * n]
+    return res
+
+
+PLAN = {}
+ORDER = """2 29 -28 6 -5 1 7 7 -9 7 -2 8 -3 64 2 -62 -3 -10 7 4 -6 30 -32 28 -17 1 1 1 1 1 21 -38 78 -90 7 25 38 2 -67 1 25 2 4 36 1 -9 -27 31 -35 2 90 -59 -1 57 1 3 3 -31 -64 42 -9 57 8 -35 -59 32 4 7 -1 -5 63 -11 1 3 -1 5 4 -61 43 -22 34 38 -126 91 38 -87 53 -61 -2 -30 14 -1 -9 -5 64 24 42 -39 4 31 3 -58 56 -78 -41 -13 14 51 -67 47 34 -24 81 -115 1 117 -62 64 -39 38 -3 5 -81 9 -26 15 9 -2 -51 -13 16 120 -64 -14 83 -92 21 -55 130 -85 -61 41 66 -5 4 38 4 -74 -26 24 77 -41 42 -101 102 1 -37 49 -55 45 -1 -101 103 -78 26 54 -91 4 -62 148 2 14 -166 4 149 1 -149 4 146 10 -8 -53 1 5 58 16 -85 -1 58 11 9 10 -9 8 -48 -26 1 1 1 -8 1 1 7 1 -22 23 1 1 1 1 1 37 1 18 1 8 -48 49 -27 8 -129 101 48 1 -8 15 -6 1 1 -13 1 -11 24 -11 16 13 -48 51 -15 -37 54 -55 39 2 16 -17 -31 27 27 -12 -9 32 -31 -31 50 2 -54 1 33 8 24 1 -23 2 -11 1 1 1 1 10 6 -32 1 32 -6 7 21 -20 1 1 19 -18 1 1 2 -17 20 -17 18 17 -11 -1 6 -10 -186 192 -203 209 -1 12 1 -11 12 -8 -202 186 6 11 -85 82 -1 8 -2 -18 1 18 15 -9 8 -16 23 -14 1 1 7 -6 7 -6 -6 38 -1 2 -26 -6 18 -17 33 3 -15 -3 17 3 -6 2 8 -3 -33 1 38 -8 9 -32 -2 1 30 31 -52 -3 8 13 1 30 -27 4 -1 -36 -2 67 -4 -62 6 -1 60 -2 -45 53 -4 3 -2 1 3 -62 64 -60 59 -60 34 1 -9 37 2 1 -4 6 -66 62 6 -1 -2 4 1 37 -36 1 1 1 1 1 1 1 1 10 -8 9 -89 91 -67 1 1 1 54 -2 11 9 -71 1 1 3 1 1 1 1 1 1 1 1 1 1 1 38 1 17 5 -21 23 1 -7 1 1 1 -12 -7 24 -23 7 1 -7 10 57 -34 -22 23 2 2 2 -16 3 -2 -2 3 -18 1 26 33 -40 1 1 1 1 14 -1 2 -10 11 1 20 -11 -19 33 -1 3 -1 -23 1 -9 10 1 1 1 1 -15 16 -14 32 -31 15 1 1 9 -8 24 -7 6 -7 -15 17 -16 1 1 21 -11 1 6 1 -2 -1 9 10 -2 7 -17 38 1 -28 31 3 -4 -38 1 1 35 -39 13 -8 1 20 -19 5 -4 35 -1 4 4 -3 -33 11 -10 38 -8 6 3 28 -59 -1 -2 4 5 2 -4 8 14 -1 7 -3 29 -2 -62 4 63 -28 24 3 2 -66 -1 10 5 3 52 1 -3 -52 -4 60 -3 4 2 -61 60 2 -29 30 2 -1 3 -42 43 -2 -40 1 42 1 1 2 -1 -44 1 1 53 -9 1 1 1 1 1 1 10 -8 9 -10 11 1 -5 -57 1 2 1 1 1 1 1 1 1 1 1 1 1 1 57 -19 1 19 3 3 -24 23 -4 -11 -7 24 -16 11 -10 1 1 45 -31 1 2 29 -27 28 -26 -5 7 2 1 23 1 -26 3 1 1 -11 -27 39 -10 11 1 1 1 17 1 1 -43 46 14 -48 26 -4 18 1 -28 19 -18 1 27 2 -11 13 1 -2 5 -1 -68 70 1 1 -37 1 1 1 1 1 14 -55 2 -3 75 -11 -4 -1 -2 1 18 2 -1 2"""
+
+
+def issue_order(ops):
+    out = [-1]
+    for d in ORDER.split():
+        out.append(out[-1] + int(d))
+    out = out[1:]
+    if sorted(out) != list(range(len(ops))):
+        return list(range(len(ops)))
+    pos = {i: p for p, i in enumerate(out)}
+    wr, rd = {}, {}
+    for i, o in enumerate(ops):
+        for k in o[1] + o[2]:
+            assert pos[wr.get(k, i)] <= pos[i]
+        for k in o[2]:
+            assert all(pos[j] <= pos[i] for j in rd.get(k, []))
+        for k in o[1]:
+            rd.setdefault(k, []).append(i)
+        for k in o[2]:
+            wr[k], rd[k] = i, []
+    return out
+
+
+def relay_program(g, core, T, topo):
+    total = 0
+    for m in MSGS:
+        for rank in range(N):
+            rt = routes(T, topo, rank, int(m[1]))
+            sp = engine_split(topo, T.cores[rank], rt)
+            for l, dst, via in rt:
+                if via != core:
+                    continue
+                sem = T.sem[m + "l%d" % l]
+                g.wait_ge(sem, len(sp[l]))
+                rid, pid = topo.addr(dst, core)
+                ap = piece(T, m[0], 0, int(m[1]), l, 1)
+                g.remote_dma(ap, ap, sem, T.sem.sent, pid, rid, topo.mask(core, dst))
+                total += len(topo.engines(core, dst))
+    if total:
+        g.wait_ge(T.sem.sent, total)
+
+
+def rank_program(g, core, T, topo):
+    rank = T.rank_of(core)
+    if rank is None:
+        relay_program(g, core, T, topo)
+        return
+    Qs = {"V": g.vector, "S": g.scalar, "P": g.tensor, "C": g, "Y": g.sync}
+    cnt = {"V": 0, "S": 0, "P": 0, "C": 0}
+    seen = {q: {} for q in Qs}
+    wr, rd, final, nd, sent = {}, {}, {}, [0], [0]
+    BANK = ("BX", "BM", "D0", "D1", "BA", "BB", "BL", "BK")
+    s = {n: T.pf[:, 16 * j:16 * j + 16] for j, n in enumerate(F16)}
+    s.update({n: T.pn[:, 16 * j:16 * j + 16] for j, n in enumerate(I16)})
+
+    def need(q, tok):
+        if seen[q].get(tok[0], 0) < tok[1]:
+            Qs[q].wait_ge(T.sem[tok[0]], tok[1])
+            seen[q][tok[0]] = tok[1]
+
+    def order(q, r, w):
+        toks = {}
+        for k in r + w:
+            deps = [wr[k]] if k in wr else []
+            if k in w or k in BANK:
+                deps = deps + [t for t in rd.get(k, []) if k in w or t[0] != q]
+            for t in deps:
+                if not (q == "P" and t[0] == "P"):
+                    toks[t[0]] = max(toks.get(t[0], 0), t[1])
+        for n in toks:
+            need(q, (n, toks[n]))
+
+    def mark(tok, r, w):
+        for k in r:
+            rd.setdefault(k, []).append(tok)
+        for k in w:
+            wr[k], rd[k] = tok, []
+        final[tok[0]] = tok[1]
+
+    ops = []
+
+    def op(q, r, w, f, kind, n):
+        r, w = r.split(), w.split()
+
+        def emit():
+            order(q, r, w)
+            cnt[q] += 1
+            f().then_inc(T.sem[q], 1)
+            mark((q, cnt[q]), r, w)
+        if q == "P" and ops[-1][:3] == (q, r, w):
+            a = ops.pop()
+            ops.append((q, r, w, lambda: (a[3](), emit()), kind, n + a[5], {}))
+        elif q == "V" and w[0][:2] == "ZR" and int(w[0][5:]) % 4 and ops[-1][:2] == (q, r):
+            a = ops.pop()
+            ops.append((q, r, a[2] + w, lambda: (a[3](), emit()), kind, n + a[5], {}))
+        else:
+            ops.append((q, r, w, emit, kind, n, {}))
+
+    def dma(q, out, in_, r, w):
+        r, w = r.split(), w.split()
+
+        def emit():
+            order(q, r, w)
+            n = "d%d" % nd[0]
+            nd[0] += 1
+            Qs[q].dma_start(out, in_).then_inc(T.sem[n], 16)
+            mark((n, 16), r, w)
+        ops.append((q, r, w, emit, "dma", size(out) * (2 if "16" in str(out.dtype) else 4), {}))
+
+    def size(a):
+        n = 1
+        for d in a.shape[1:]:
+            n *= d
+        return n
+
+    def kind_of(r, w, out, a, base):
+        if "X.a" in w.split():
+            return "scatter", size(a)
+        if set(r.split()) & set("b16 bH il ol el tl dl wl".split()) or w[:3] == "kcu" or w[:2] == "G." or w[:3] == "W.x":
+            return "gather", size(out)
+        if base == "half":
+            return "plain", size(a) * (0.5 if "16" in str(out.dtype) and "16" in str(a.dtype) else 1)
+        return "plain", size(a) * base
+
+    v, sc, pe = g.vector, g.scalar, g.tensor
+
+    def TT(r, w, out, a, b, o):
+        op("V", r, w, lambda: v.tensor_tensor(out, a, b, o), *kind_of(r, w, out, a, 1 if set(r.split()) & set(BANK) else 2))
+
+    def TS(r, w, out, a, s1, o0, s2=None, o1=None):
+        if o1 is None:
+            op("V", r, w, lambda: v.tensor_scalar(out, a, s1, None, o0), *kind_of(r, w, out, a, "half"))
+        else:
+            op("V", r, w, lambda: v.tensor_scalar(out, a, s1, s2, o0, o1), *kind_of(r, w, out, a, "half"))
+
+    def tt(out, a, b, o):
+        TT(a + " " + b, out, s[out], s[a], s[b], o)
+
+    def ts(out, a, s1, o0, s2=None, o1=None):
+        TS(a, out, s[out], s[a], s1, o0, s2, o1)
+
+    def CP(r, w, out, a):
+        op("V", r, w, lambda: v.tensor_copy(out, a), *kind_of(r, w, out, a, "half"))
+
+    def MS(w, out, c):
+        op("V", "", w, lambda: v.memset(out, c), *kind_of("", w, out, out, "half"))
+
+    def SCAN(r, w, out, d0, d1, o0, o1, init=0.0):
+        op("V", r, w, lambda: v.tensor_tensor_scan(out, d0, d1, init, o0, o1), "plain", size(out))
+
+    def ACT(r, w, out, a, f=F.Copy, **kw):
+        op("S", r, w, lambda: sc.activation(out, a, f, **kw), *kind_of(r, w, out, a, 1))
+
+    def MM(r, w, out, l, rh, st, sp, fence=False):
+        def f():
+            if fence:
+                need("P", ("P", cnt["P"] - 1))
+            return pe.matmul(out, l, rh, st, sp)
+        op("P", r, w, f, "mm", max(min(64, size(l)), size(rh)) * (4 if "32" in str(l.dtype) else 1))
+
+    def IO(w, out, pat, base=0, cm=0, flt=True):
+        if flt:
+            op("C", "", w, lambda: g.iota(out, pat, base, cm, allow_small_or_imprecise_dtypes=True), "pool", size(out))
+        else:
+            op("C", "", w, lambda: g.iota(out, pat, base, cm), "pool", size(out))
+
+    def SEL(r, w, out, a, pat, o, base, cm, fill=0.0):
+        op("C", r, w, lambda: g.affine_select(out, a, pat, o, fill, base, cm), "pool", size(out))
+
+    def send(kind, r, src):
+        hops = {"%s%d.%d" % (kind, r, l): 1 if via is None else 2 for l, dst, via in routes(T, topo, rank, r)}
+        ops.append(("C", [src], list(hops), lambda: send_now(kind, r, src), "send", 0, hops))
+
+    def send_now(kind, r, src):
+        m = kind + str(r)
+        rt = routes(T, topo, rank, r)
+        sp = engine_split(topo, core, rt)
+        order("C", [src], [])
+        trs = []
+        for l, dst, via in rt:
+            rid, pid = topo.addr(dst if via is None else via, core)
+            trs.append(RemoteDMATransfer(dst_ids=[DstId(rid=rid, pnc=pid)], dma_engine_mask=sum(1 << e for e in sp[l]),
+                                         remote_sem=T.sem[m + "l%d" % l], src=piece(T, kind, 1, r - 1, l, 1), dst=piece(T, kind, 0, r, l, 1)))
+            sent[0] += len(sp[l])
+        g.remote_dma_fused(trs, local_sem=T.sem.sent)
+        for l in range(N):
+            h = block(l, r - 1)
+            if h:
+                frm = (rank - h) % N
+                via = [x[2] for x in routes(T, topo, frm, r) if x[0] == l][0]
+                n = len(topo.engines(T.cores[frm] if via is None else via, core))
+                mark((m + "l%d" % l, n), [], ["%s.%d" % (m, l)])
+
+    def lanes(m, ls=range(N)):
+        return " ".join("%s.%d" % (m, l) for l in ls)
+
+    def tile(b, t, w=128):
+        return b[:, w * t:w * t + w]
+
+    dma("Y", T.si[:], T.ms[:], "", "si")
+    dma("S", T.X[:, 0:1024], T.tx[:, 0:1024], "", "X.a")
+    dma("Y", T.X[:, 1024:2048], T.tx[:, 1024:2048], "", "X.b")
+    for l in range(N):
+        dma("SY"[l // 2], piece(T, "z", 0, 0, l, 1), tile(T.z, block(l, 0), 64), "", "z0.%d" % l)
+    dma("Y", s["ci"], T.cp[:], "", "ci")
+    dma("S", T.Ki[:], T.kt[:], "", "Ki")
+    XX = "X.a X.b"
+
+    def consts_first():
+        IO("one", T.one[:], [[0, 128]], 1)
+        SEL("one", "I", T.I[:], T.one[:], [[-1, 128]], A.is_equal, 0, 1)
+        IO("xk", T.xk[0:32, :, 0:9], [[0, 16], [8, 2], [1, 9]])
+        IO("irow", T.irow[0:32, :], [[1, 128]])
+        IO("irow16", T.irw[0:32, :], [[16, 128]])
+        SEL("one", "s1", T.s1[:, 0:8], T.one[:, 0:8], [[-16, 8]], A.is_ge, 0, 1)
+        SEL("s1", "sel8", T.sel8[:], T.s1[:, 0:8], [[16, 8]], A.is_ge, 15, -1)
+        IO("sh", T.sh[:, 0:1], [[0, 1]], 0, 1, False)
+        ACT("I", "nI", T.nI[:], T.I[:], scale=-1.0)
+        xk = T.xk[0:32, :, 0:9]
+        ACT("xk", "xb", T.xb[0:32, :, 0:9], xk, scale=U)
+        ACT("xk", "mb", T.mb[0:32, :, 0:9], xk, F.Identity, scale=128 * U, bias=2048 * U)
+        ACT("xk", "xa", T.xa[0:32, :, 0:9], xk, F.Identity, scale=0.0, bias=U)
+        for b, c in (("xa", 0.0), ("xb", -2.0), ("mb", 0.0)):
+            ACT("xk", b, T[b][0:32, :, 8], T.xk[0:32, :, 8], F.Identity, scale=0.0, bias=c)
+        for j, c in enumerate((-1.0, 2.0, 1.0, 0.5)):
+            if j != 2 or CFG["xabs"]:
+                ACT("sel8", "Rx", T.Rx[:, 16 * j:16 * j + 16:2], T.sel8[:], scale=c * 2.0 ** -12)
+                ACT("sel8", "Rx", T.Rx[:, 16 * j + 1:16 * j + 16:2], T.sel8[:], scale=c * SU)
+
+    def consts_iota():
+        IO("t1", T.t1[:], [[0, 32], [1, 16]])
+        SEL("one", "um", T.um[:, 0:128], T.one[:], [[-16, 8], [0, 16]], A.is_ge, 0, 1)
+        SEL("um", "BO", T.BO[:], T.um[:, 0:128], [[16, 8], [0, 16]], A.is_ge, 15, -1)
+        IO("sx", T.sx[0:32, 0:128], [[0, 8], [37, 16]])
+        IO("li.a", T.li[:, 0:16], [[1, 16]], 0, 0, False)
+        for r in range(RO):
+            IO("o8", tile(T.o8, r, 16), [[512, 2], [1024, 2], [128, 4]], 512 * r, 0, False)
+        IO("s2", T.s2[:], [[-1, 16]], 14, 0)
+        IO("hz hz1 hz2", T.hz[:], [[0, 64]])
+        IO("crow", T.crow[:], [[4096, 2], [0, 8]])
+        IO("Wd", T.Wd[:, 256:272], [[0, 16]])
+        for b in ("E", "H0", "H1"):
+            IO(b, T[b][:, 512:528], [[0, 16]])
+        for j, c in enumerate((0, 2, 512, 16)):
+            IO("hm", T.hm[:, j::4], [[0, 16]], c)
+        IO("t0", T.t0[:], [[1, 32], [0, 16]])
+        IO("oi", T.oi[:, 0:8], [[64, 8]], 0, 0, False)
+        IO("oi2", T.oi[:, 8:12], [[64, 4]], 0, 1, False)
+        IO("ZR.y", T.ZR[:, 2048:3072], [[0, 1024]])
+        dma("Y", T.ZR[:, 3072:4096], T.ZR[:, 2048:3072], "ZR.y", "ZR.x")
+        dma("Y", T.ZR[:, 6144:8192], T.ZR[:, 2048:4096], "ZR.y ZR.x", "ZR.z")
+
+    def consts_later():
+        p16 = T.pm[:, 0:1]
+        TS("sh", "ai", T.pn[:, 32:33], T.sh[:, 0:1], 15, A.bitwise_and)
+        CP("I", "If", T.If[:], T.I[:])
+        CP("ai", "pm", p16, T.pn[:, 32:33])
+        CP("nI", "nIf", T.nIf[:], T.nI[:])
+        TS("t1 pm", "E", T.E[:, 0:512], T.t1[:], p16, A.is_equal)
+        TS("pm", "pm1", T.pm[:, 1:2], p16, 2.0, A.mult, 1.0, A.add)
+        TS("pm", "pm3", T.pm[:, 3:4], p16, 16.0, A.add)
+        TS("pm", "pm4", T.pm[:, 4:5], p16, 8.0, A.mult)
+        TS("sx", "vrow", T.vrow[0:32, :], T.sx[0:32, 0:128], -1023.5, A.add)
+        CP("sx", "drow", T.drow[0:32, :], T.sx[0:32, 0:128])
+        MS("onef", T.onef[0:32, :], 1.0)
+        CP("BO", "BOf", T.BOf[:], T.BO[:])
+        CP("li.a", "b16", T.b16[:], T.li[:, 0:16])
+        TS("s2", "s1", T.s1[:], T.s2[:], 0.0, A.is_lt, 16.0, A.mult)
+        TT("s1 s2", "s2", T.s2[:], T.s2[:], T.s1[:], A.add)
+        TS("sh", "a15", T.pn[:, 48:49], T.sh[:, 0:1], 63, A.bitwise_and)
+        TS("sh", "uq", T.pn[:, 64:65], T.sh[:, 0:1], 64, A.bitwise_and)
+        CP("uq", "pm6", T.pm[:, 6:7], T.pn[:, 64:65])
+        TS("oi2 pm6", "oi2", T.oi[:, 8:12], T.oi[:, 8:12], T.pm[:, 6:7], A.add)
+        TS("oi2", "oi3", T.oi[:, 16:20], T.oi[:, 8:12], 255, A.bitwise_and)
+        CP("a15", "pm5", T.pm[:, 5:6], T.pn[:, 48:49])
+        CP("oi3", "sl", T.sl[:], T.oi[:, 16:20])
+        TS("oi pm5", "dl", T.dl[:], T.oi[:, 0:8], T.pm[:, 5:6], A.add)
+        TS("s2 pm", "EA", T.EA[:], T.s2[:], p16, A.is_equal)
+        zero = T.ZR[:, 2048:2336]
+        SEL("ZR.y", "r16", T.r16[:], T.ZR[:, 2048:2304], [[0, 16], [1, 16]], A.not_equal, 0, 0, 4.0)
+        SEL("ZR.y", "r8", T.r8[:], zero, [[0, 32], [1, 9]], A.not_equal, 0, 0, 8.0)
+        SEL("ZR.y", "ra", T.ra[:], zero, [[0, 32], [1, 9]], A.is_equal, -8, 0, 2 * U)
+        SEL("ZR.y", "ru", T.ru[:], T.ZR[:, 2048:2304], [[0, 16], [1, 16]], A.not_equal, 0, 0, -2.0 ** 18)
+        TS("o8 pm4", "o8", T.o8[:], T.o8[:], T.pm[:, 4:5], A.add)
+        TS("o8", "o8", T.o8[:], T.o8[:], 2047, A.bitwise_and)
+        IO("ra", T.ra[:, 0::18], [[0, 16]], -8)
+
+    def consts_scalar():
+        ACT("nI", "nIq", T.nIq[:], T.nI[:])
+        ACT("E BO", "um", T.um[:], T.E[:, 0:256], F.Identity, scale=2.0 ** 17, bias=-2.0 ** 17)
+        ACT("BO pm1", "Wu", T.Wu[:], T.BO[:], scale=T.pm[:, 1:2])
+        ACT("E", "srow", T.srow[0:32, 0:256], T.E[0:32, 0:256], F.Identity, scale=0.0, bias=2.0 ** -125)
+        ACT("E", "srow", T.srow[0:32, 256:512], T.E[0:32, 0:256], F.Identity, scale=0.0, bias=2.0 ** -117)
+        ACT("one", "arow", T.arow[:], T.one[:, 0:16], scale=2048 * SU)
+        ACT("one", "aw", T.aw[:], T.one[:], scale=-8 * SU)
+
+    def consts_last():
+        TS("t0 pm", "H0", T.H0[:, 0:512], T.t0[:], T.pm[:, 0:1], A.is_equal)
+        TS("t0 pm3", "H1", T.H1[:, 0:512], T.t0[:], T.pm[:, 3:4], A.is_equal)
+        MS("t1", T.t1[0:32, 0:128], 0.25)
+        MS("L2", T.L2[0:32, 0:128], 0.0)
+        MS("t1", T.t1[0:32, 5:116:5], 0.5)
+        MS("t1", T.t1[0:32, 0:1], 2.0 ** 58)
+        SCAN("t1 L2", "Q", T.Q[0:32, 0:128], T.t1[0:32, 0:128], T.L2[0:32, 0:128], A.mult, A.add, 2.0 ** 59)
+        for j in range(4):
+            ACT("Q", "L1", T.L1[0:32, 64 * j:64 * j + 64], T.Q[0:32, 64 * (j // 2):64 * (j // 2) + 64])
+        for j in (0, 1):
+            MM("L1 one", "D0", T.D0[:, 2 * j:2 * j + 2], T.L1[0:1, 128 * j:128 * j + 128], T.one[0:1, 0:2], True, True)
+        ACT("D0", "wc", T.wc[:], T.D0[:, 0:4:2])
+        for j in (0, 1):
+            ACT("sl wc", "wi", T.wi[:, j::2], T.sl[:, j::2], scale=T.wc[:, j:j + 1])
+
+    def m_src(r, l):
+        if r and l == home(r - 1):
+            return piece(T, "M", 1, r - 1, l, 1), "Mo%d" % (r - 1)
+        return piece(T, "M", 0, r, l, 1), "M%d.%d" % (r, l)
+
+    def m_gather(r, l):
+        b, k = m_src(r, l)
+        ACT(XX + " " + k, "G.%d" % l, tile(T.G, l, 1024), T.X[:].indirect(b))
+
+    def m_float(r, l):
+        b, k = m_src(r, l)
+        CP(k, "Mf.%d" % l, tile(T.Mf, l, 64), b)
+
+    def key_init(B, a, b):
+        MM("irow irow16 xa", B, T[B][:, :, 0:9], T[a][0:1, :], T.xa[0:1, :, 0:9], True, False)
+        MM("one " + b, B, T[B][:, :, 0:9], T.one[0:1, :], T[b][0:1, :, 0:9], False, False)
+
+    def key_out(B, t, k):
+        return T[B][:, 16 * t + k // 8:16 * t + 16:2, k % 8:9:8 - k % 8]
+
+    DB = ("D0", "BK", "D1")
+
+    def m_delta(r, t, c, D):
+        rk = "I nI G.%d G.%d " % (2 * t, 2 * t + 1) + lanes("z%d" % r, (2 * t, 2 * t + 1))
+        for j in range(4):
+            k = 4 * c + j
+            MM(rk, D, tile(T[D], j), T.I[:], T.G[:, 2048 * t + k:2048 * t + 2048:16], True, False)
+            MM(rk, D, tile(T[D], j), T.nI[:], piece(T, "z", 0, r, 2 * t, 2), False, True)
+
+    def m_abs(t, c, D):
+        o = 4096 * t + 2048 + 512 * c
+        ACT(D, "W.m%d%d" % (t, c), T.W[:, o:o + 512], T[D][:], F.Abs, scale=2.0)
+
+    def m_keys(t, c, last):
+        for j in range(4):
+            k = 4 * c + j
+            o = 4096 * t + 2048 + 128 * k
+            MM("Rx W.m%d%d" % (t, c), "BM", key_out("BM", t, k), T.W[:, o:o + 128], T.Rx[:, 48:64], False, last and j == 3)
+
+    def m_chunks(r, todo, last, hooks):
+        n = len(todo)
+        for i in range(-3, n):
+            if i in hooks:
+                hooks[i]()
+            if i >= 0:
+                m_abs(todo[i][0], todo[i][1], DB[i % 3])
+            if i + 3 < n:
+                m_delta(r, todo[i + 3][0], todo[i + 3][1], DB[i % 3])
+            if i >= 0:
+                m_keys(todo[i][0], todo[i][1], last and i == n - 1)
+
+    def z_rep(r, t, ng=0):
+        z = piece(T, "z", 0, r, 2 * t, 2)
+        rk = lanes("z%d" % r, (2 * t, 2 * t + 1))
+        for k in range(16):
+            out = T.ZR[:, 4096 * t + k:4096 * t + 2048:16]
+            if k < ng:
+                SEL(rk, "ZR.%d.%d" % (t, k), out, z, [[0, 128]], A.is_ge, 0, 0)
+            elif k >= 16 - CFG["zs"]:
+                ACT(rk, "ZR.%d.%d" % (t, k), out, z)
+            else:
+                CP(rk, "ZR.%d.%d" % (t, k), out, z)
+
+    def kc(r, t):
+        CP("K " + lanes("c%d" % r, (2 * t, 2 * t + 1)), "kcu%d" % t, tile(T.kcu, t), T.K[:].indirect(piece(T, "c", 0, r, 2 * t, 2)))
+
+    def kc2(r):
+        CP("kcu0 kcu1", "kcf", T.kcf[:], T.kcu[:])
+        TS(lanes("c%d" % r), "c2a", s["c2a"], piece(T, "c", 0, r), 2.0, A.mult)
+        ts("c2", "c2a", 511, A.bitwise_and)
+
+    def x_gather(t):
+        zr = " ".join("ZR.%d.%d" % (t, k) for k in range(16))
+        TT(XX + " kcu%d " % t + zr, "W.x%d" % t, T.W[:, 4096 * t:4096 * t + 2048], T.X[:].indirect(tile(T.kcu, t)), tile(T.ZR, 2 * t, 2048), A.subtract)
+
+    def x_relu(t, n=0, ab=False):
+        if ab:
+            ACT("W.x%d" % t, "R.%d" % t, tile(T.R, t, 2048), T.W[:, 4096 * t:4096 * t + 2048], F.Abs)
+        elif n:
+            ACT("W.x%d" % t, "R.s%d" % t, T.R[:, 2048 * t:2048 * t + n], T.W[:, 4096 * t:4096 * t + n], F.Relu)
+            TS("W.x%d" % t, "R.%d" % t, T.R[:, 2048 * t + n:2048 * t + 2048], T.W[:, 4096 * t + n:4096 * t + 2048], 0.0, A.max)
+        else:
+            TS("W.x%d" % t, "R.%d" % t, tile(T.R, t, 2048), T.W[:, 4096 * t:4096 * t + 2048], 0.0, A.max)
+
+    def x_keys(t, part, last, ab=False):
+        j = 2 if ab else part
+        for k in range(16):
+            src = T.W[:, 4096 * t + k:4096 * t + 2048:16] if part == 0 else T.R[:, 2048 * t + k:2048 * t + 2048:16]
+            MM("Rx " + ("W.x%d" % t if part == 0 else "R.%d R.s%d" % (t, t)), "BX", key_out("BX", t, k), src, tile(T.Rx, j, 16), False, last and k == 15)
+
+    MF = "Mf.0 Mf.1 Mf.2 Mf.3"
+
+    def m_copy():
+        ACT("BM", "tt", T.tt[:], T.BM[:, :, 8])
+        ACT("BM", "kms", T.kms[:], T.BM[:, :, 0:8], F.Identity, bias=-4096 * U)
+
+    def m_side(r):
+        TT("tt", "df", s["df"], T.tt[:, 1::2], T.tt[:, 0::2], A.subtract)
+        TT("tt", "ts", s["ts"], T.tt[:, 0::2], T.tt[:, 1::2], A.add)
+        o = "nf" if r else "thr"
+        ACT("df", o, s[o], s["df"], F.Abs)
+        ts("ts2", "ts", -7.5 * SU, A.add, 3072.0, A.add)
+        if r:
+            tt("thr", "nf", "a8", A.add)
+        SCAN("kms r16", "msn", T.msn[:], T.r16[:], T.kms[:], A.add, A.min)
+        ACT("ts2", "tT", s["tT"], s["ts2"], F.Identity, bias=-3071.0)
+        ts("nthr", "thr", SU, A.max, -1.0, A.mult)
+        ACT("msn", "ek", s["ek"], T.msn[:, 15::16], F.Identity, bias=4096 * U)
+
+    def m_values(r):
+        zl = lanes("z%d" % r)
+        for t in (0, 1):
+            o = tile(T.BB, t)
+            MM("kcf If", "BB", o, tile(T.kcf, t), T.If[:], True, False)
+            MM("Wu " + zl, "BB", o, piece(T, "z", 0, r, 2 * t, 2), T.Wu[:], False, False)
+            MM("onef vrow", "BB", o, T.onef[0:1, :], T.vrow[0:1, :], False, True)
+        ACT("BB", "ry", T.ry[:], T.BB[:, 0:256], F.Identity, bias=1.5 * 2.0 ** 34)
+        ACT("ry", "rr", T.rr[:], T.ry[:], F.Identity, bias=-1.5 * 2.0 ** 34)
+        for t in (0, 1):
+            o = tile(T.BA, t)
+            MM("kcf If", "BA", o, tile(T.kcf, t), T.If[:], True, False)
+            MM("nIf " + MF, "BA", o, tile(T.Mf, t), T.nIf[:], False, True)
+        for t in (0, 1):
+            o = tile(T.BA, 2 + t)
+            MM("kcf If", "BA", o, tile(T.kcf, t), T.If[:], True, False)
+            MM("nIf " + MF, "BA", o, tile(T.Mf, t), T.nIf[:], False, False)
+            MM("Wu " + zl, "BA", o, piece(T, "z", 0, r, 2 * t, 2), T.Wu[:], False, False)
+            MM("onef drow", "BA", o, T.onef[0:1, :], T.drow[0:1, :], False, False)
+            MM("nI rr", "BA", o, T.nI[:], tile(T.rr, t), False, True)
+
+    WALL = "W.x0 W.x1 " + " ".join("W.m%d%d" % (t, c) for t in (0, 1) for c in range(4))
+
+    def choose():
+        ACT("BX", "kxs", T.kxs[:], T.BX[:, :, 0:9])
+        TT("kxs", "sd", s["sd"], T.kxs[:, 17::18], T.kxs[:, 8::18], A.subtract)
+        SCAN("kxs r8", "xs", T.xs[:], T.r8[:], T.kxs[:], A.add, A.min)
+        TT("sd thr", "bad0", T.bad[:, 0::2], s["sd"], s["thr"], A.is_lt)
+        TT("sd nthr", "bad1", T.bad[:, 1::2], s["sd"], s["nthr"], A.is_gt)
+        TT("xs bad0 bad1", "cand", T.cand[:], T.xs[:, 7::9], T.bad[:], A.max)
+        TT("bad0 bad1", "nt", s["nt"], T.bad[:, 0::2], T.bad[:, 1::2], A.min)
+        TT("cand", "m1", s["m1"], T.cand[:, 0::2], T.cand[:, 1::2], A.min)
+        tt("win", "m1", "ek", A.min)
+        ts("wi32", "win", 1 / U, A.mult)
+        TT("win ek", "hz", T.hz[:, 0::4], s["win"], s["ek"], A.is_equal)
+        ts("ix", "wi32", 4095, A.bitwise_and)
+        ACT("bad1", "hz2", T.hz[:, 2::4], T.bad[:, 1::2])
+        TT("ix b16 E", "ex", T.ex[:], s["ix"].indirect(T.b16[:]), T.E[:, 0:256], A.mult)
+        MM("one crow", "BL", T.BL[:, 0:16], T.one[0:1, :], T.crow[0:1, :], True, False)
+        for t in (0, 1):
+            MM("ex sel8", "BL", tile(T.BL, t, 8), tile(T.ex, t), T.sel8[:], False, t == 1)
+
+    def pack(r):
+        TT("nt hz", "hz1", T.hz[:, 1::4], s["nt"], T.hz[:, 0::4], A.is_ge)
+        SCAN("kxs ra", "asn", T.asn[:], T.ra[:], T.kxs[:], A.add, A.max)
+        SCAN("hz hz1 hz2 hm", "hs", T.hs[:], T.hm[:], T.hz[:], A.mult, A.add)
+        TS("asn", "ai", s["ai"], T.asn[:, 16::18], 1 / U, A.mult)
+
+    EX2 = " ".join("ex2.%d" % j for j in range(16))
+
+    def pack2(r):
+        ts("a15", "ai", 15, A.bitwise_and)
+        TT("a15 hs", "P", s["P"], s["a15"], T.hs[:, 3::4], A.add)
+        if CFG["ex2"][r] == "V":
+            TT("P b16 E", EX2, T.ex2[:], s["P"].indirect(T.b16[:]), T.E[:, 0:256], A.mult)
+        else:
+            o = 16 * F16.index("P")
+            for j in range(16):
+                ACT("P E", "ex2.%d" % j, tile(T.ex2, j, 16), T.E[:, 0:16], scale=T.pf[:, o + j:o + j + 1])
+        for t in (0, 1):
+            MM(EX2 + " sel8", "BK", T.BK[:, 8 * t:8 + 8 * t], tile(T.ex2, t), T.sel8[:], True, True)
+        for t in (0, 1):
+            h = block(2 * t, r)
+            o = 16 + 4 * (h % 2)
+            for u in (0, 1):
+                MM(EX2 + " sel8", "BK", T.BK[:, o + 8 * u:o + 8 * u + 4], tile(T.ex2, t), tile(T.sel8, (u + h // 2) % 2, 4), True, True)
+        if r < RO - 1:
+            MM("one arow", "BK", T.BK[:, 32:48], T.one[0:1, :], T.arow[0:1, :], True, False)
+            for t in (0, 1):
+                for u in (0, 1):
+                    MM("aw hz1", "BK", T.BK[:, 32 + 8 * t:40 + 8 * t], T.aw[:], T.hz[:, 32 * u + 1:32 * u + 32:4], False, t + u == 2)
+
+    ZALL = "ZR.z " + " ".join("ZR.%d.%d" % (t, k) for t in (0, 1) for k in range(16))
+
+    def features(r, fill):
+        zo, k = piece(T, "z", 1, r), "zo%d" % r
+        CP("BL", "il", T.il[:], T.BL[:, 0:16])
+        ACT(ZALL + " il", "g1", T.g1[:], T.ZR[:].indirect(T.il[:]), F.Identity, scale=2.0, bias=-0.5)
+        CP("BL", "li.a", T.li[:, 0:16], T.BL[:, 0:16])
+        TT("cand win", "Fw", T.Fw[:, 0::2], T.cand[:, 0::2], s["win"], A.not_equal)
+        TT("cand win", "Fw1", T.Fw[:, 1::2], T.cand[:, 1::2], s["win"], A.not_equal)
+        fill()
+        TT(WALL + " il g1", "sx", T.sx[:], T.W[:].indirect(T.il[:]), T.g1[:], A.add)
+        ACT("sx", "ry", T.ry[:], T.sx[:], F.Identity, bias=1.5 * 2.0 ** 24)
+        ACT("ry", k, zo, T.ry[:], F.Identity, scale=0.5, bias=-0.75 * 2.0 ** 24)
+        MM("Wu " + k, "BL", T.BL[:, 256:512], T.Wu[:], zo, True, False)
+        MM("I um", "BL", T.BL[:, 256:512], T.I[:], T.um[:], False, True)
+        if r == RO - 1:
+            for l in range(N):
+                dma("Y", tile(T.yz, block(l, r), 64), piece(T, "z", 1, r, l, 1), k, "")
+        else:
+            send("z", r + 1, k)
+            l = home(r)
+            ACT(k, "z%d.%d" % (r + 1, l), piece(T, "z", 0, r + 1, l, 1), piece(T, "z", 1, r, l, 1))
+
+    def survivors(part):
+        if part == 0:
+            tt("Tt", "tT", "nt", A.subtract)
+            ACT("BX", "nkx", T.nkx[:], T.BX[:, :, 0:8], scale=-1.0)
+            ACT("Tt b16", "tbc", T.tbc[:], s["Tt"].indirect(T.b16[:]), F.Identity, bias=4096 * U)
+            MM("nIq kms", "D0", T.D0[:, 0:256], T.nIq[:], T.kms[:], True, False)
+            TT("BM tbc", "c2b", T.c2b[:], T.BM[:, :, 0:8], T.tbc[:], A.is_ge)
+            TT("c2b BA", "p2", T.p2[:], T.BA[:, 256:512], T.c2b[:], A.mult)
+        else:
+            for k in range(8):
+                MM("I Fw Fw1", "D0", T.D0[:, k:256:8], T.I[:], T.Fw[:], False, k == 7)
+            TT("D0 nkx", "ltb", T.ltb[:], T.D0[:, 0:256], T.nkx[:], A.is_lt)
+            TT("ltb BA", "p1m", T.p1m[:], T.BA[:, 0:256], T.ltb[:], A.mult)
+
+    def survivors_sum():
+        for t in (0, 1):
+            o = tile(T.BB, 2 + t)
+            MM("If " + MF, "BB", o, T.If[:], tile(T.Mf, t), True, False)
+            MM("If p1m", "BB", o, tile(T.p1m, t), T.If[:], False, False)
+            MM("If p2", "BB", o, tile(T.p2, t), T.If[:], False, True)
+
+    def survivors_out(r):
+        if r == RO - 1:
+            ACT("BB", "Mof", T.Mof[:], T.BB[:, 256:512])
+            for l in range(N):
+                dma("Y", tile(T.yms, block(l, r), 64), tile(T.Mof, l, 64), "Mof", "")
+        else:
+            CP("BB", "Mo%d" % r, piece(T, "M", 1, r), T.BB[:, 256:512])
+            send("M", r + 1, "Mo%d" % r)
+
+    def lists(r):
+        CP("BK", "li.b", T.li[:, 16:48], T.BK[:, 0:32])
+        if r < RO - 1:
+            ACT("BK", "a8", s["a8"], T.BK[:, 32:48])
+        SCAN("BL ru", "us", T.us[:], T.ru[:], T.BL[:, 256:512], A.add, A.max)
+        TS("li.b", "vv", s["vv"], T.li[:, 16:32], 4, A.arith_shift_right, 1023, A.bitwise_and)
+        CP("us", "ui", s["ui"], T.us[:, 15::16])
+        tt("tA", "vv", "c2", A.add)
+        ts("uq", "ui", 7, A.bitwise_and)
+        TS("tA", "tl", T.tl[:], s["tA"], 512.0, A.min)
+        TT("uq o8", "ow", s["ow"], s["uq"], tile(T.o8, r, 16), A.add)
+
+    def own_list():
+        CP("ow", "ol", T.ol[:], s["ow"])
+
+    def names():
+        TS("li.a", "l4.a", T.l4[:, 0:16], T.li[:, 0:16], 7, A.arith_shift_right, 15, A.bitwise_and)
+        TS("li.b", "l4.b", T.l4[:, 16:32], T.li[:, 32:48], 15, A.bitwise_and)
+        CP("l4.a l4.b", "el", T.el[:], T.l4[:])
+        TT("E el " + MF, "EM", T.EM[:], T.E[:, 0:16].indirect(T.el[:, 0:16]), T.Mf[:], A.mult)
+
+    def taxa(r):
+        TT(XX + " ol zo%d" % r, "si", T.si[:], T.X[:].indirect(T.ol[:]), piece(T, "z", 1, r), A.add)
+        TS("si", "sh", T.sh[:], T.si[:], 1, A.arith_shift_right)
+        CP("sh ol", XX, T.X[:].indirect(T.ol[:]), T.sh[:])
+        if r == RO - 1:
+            dma("Y", T.ytx[:, 0:1024], T.X[:, 0:1024], XX, "")
+            dma("C", T.ytx[:, 1024:2048], T.X[:, 1024:2048], XX, "")
+
+    def couplet_numbers(r):
+        tt("tB", "c2", "vv", A.subtract)
+        ts("u9", "ui", 511, A.bitwise_and)
+        ts("tB", "tB", 513.0, A.add)
+        TS("li.b", "im", s["im"], T.li[:, 16:32], 14, A.arith_shift_right)
+        tt("tC", "u9", "tB", A.subtract)
+        tt("tC", "tC", "im", A.mult)
+        tt("tD", "tC", "tB", A.add)
+        CP("tD", "co%d" % r, piece(T, "c", 1, r), s["tD"])
+        send("c", r + 1, "co%d" % r)
+        l = home(r)
+        dma("Y", piece(T, "c", 0, r + 1, l, 1), piece(T, "c", 1, r, l, 1), "co%d" % r, "c%d.%d" % (r + 1, l))
+
+    def k_onehot(qs):
+        for j, wn in enumerate(("E", "H0", "H1")):
+            if qs[j] == "S":
+                ACT("tl " + wn, "oh%d" % j, tile(T.oh, j, 256), T[wn][:].indirect(T.tl[:]))
+            else:
+                CP("tl " + wn, "oh%d" % j, tile(T.oh, j, 256), T[wn][:].indirect(T.tl[:]))
+        for t in (0, 1):
+            MM("oh0 I", "BA", tile(T.BA, 2 + t), tile(T.oh, t), T.I[:], True, True)
+        for t in (0, 1):
+            for a in (0, 1):
+                for hh in (0, 1):
+                    MM("I oh%d" % (hh + 1), "BK", tile(T.BK, 4 * t + 2 * a + hh, 64), tile(T.oh, 2 + 2 * hh + t), tile(T.I, a, 64), True, True)
+
+    def k_old():
+        ACT("K tl", "Kt", T.Kt[:], T.K[:].indirect(T.tl[:]))
+
+    def k_table(r):
+        for t in (0, 1):
+            ACT("BA wc", "L1", tile(T.L1, t), tile(T.BA, 2 + t), scale=tile(T.wc, (r + t) % 2, 1))
+            ACT("BA wi", "L2", tile(T.L2, t), tile(T.BA, 2 + t), scale=tile(T.wi, r + t, 1))
+        ACT("BK", "Oh", T.Oh[:], T.BK[:])
+        MM("one srow", "D1", T.D1[:], T.one[0:1, :], T.srow[0:1, :], True, False)
+        parts = [(l // 2, 64 * (l % 2), 64, block(l, r) // 2) for l in range(N)]
+        todo = [(p, a, u) for p in parts[0::2] + parts[1::2] for a in (0, 1) for u in (0, 1)]
+        for i, ((t, p0, n, hi), a, u) in enumerate(todo):
+            o = 256 * u + 128 * hi
+            L = T["L%d" % (u + 1)]
+            MM("L1 L2 Oh", "D1", T.D1[64 * a:64 * a + 64, o:o + 128], L[p0:p0 + n, 128 * t + 64 * a:128 * t + 64 * a + 64],
+               T.Oh[p0:p0 + n, 256 * t + 128 * a:256 * t + 128 * a + 128], False, i in (len(todo) - 3, len(todo) - 1), i == len(todo) // 2)
+
+    def k_delta(r):
+        for l in range(N):
+            o = tile(T.BA, block(l, r), 64)
+            MM("BOf EM nIq Kt", "BA", o, T.BOf[:], tile(T.EM, l, 64), True, False)
+            MM("BOf EM nIq Kt", "BA", o, T.nIq[:], tile(T.Kt, l, 64), False, True)
+
+    def k_read():
+        ACT("D1", "tb", T.tb[:], T.D1[:])
+        ACT("tb dl", "tg", T.tg[:], T.tb[:].indirect(T.dl[:]))
+        ACT("EA el", "oa", T.oa[:], T.EA[:].indirect(T.el[:, 16:32]))
+
+    def k_write(r):
+        op("V", "tg", "rc", lambda: v.reciprocal(T.rc[:], T.tg[:, 0:64]), "plain", 230 + 6 * 64)
+        TT("BA oa", "Wd", T.Wd[:, 0:256], T.BA[:, 0:256], T.oa[:], A.mult)
+        TT("rc tg", "ra2", T.ra2[:], T.rc[:], T.tg[:, 64:128], A.mult)
+        TT("ra2", "om", T.om[:], T.ra2[:, 0:32], T.ra2[:, 32:64], A.min)
+        TS("om", "oi oi2 oi3", T.oi[:], T.om[:], -0.3, A.add)
+        CP("oi", "wl", T.wl[:], T.oi[:])
+        if r < RO - 1:
+            TT("Wd Wd1 wl K", "K", T.K[:, 0:512], T.Wd[:].indirect(T.wl[:]), T.K[:, 0:512], A.add)
+        else:
+            for h, b in enumerate(("ex", "sx")):
+                TT("Wd Wd1 wl K", b, T[b][:], T.Wd[:].indirect(tile(T.wl, h, 16)), tile(T.K, h, 256), A.add)
+                dma("YS"[h], tile(T.ykt, h, 256), T[b][:], b, "")
+
+    def x_big(r, ta, both, lane):
+        hooks = {0: lambda: m_gather(r, lane), CFG["hv"]: lambda: (consts_scalar() if r == 0 else None, m_values(r))}
+        if not CFG["xabs"]:
+            if r == 0:
+                x_relu(ta)
+            hooks[CFG["h0"]] = lambda: x_keys(ta, 0, False)
+            hooks[CFG["h1"]] = lambda: x_keys(ta, 1, False)
+        m_chunks(r, both, True, hooks)
+        m_copy()
+        if CFG["xabs"]:
+            x_relu(ta, 0, True)
+            x_keys(ta, 1, False, True)
+
+    consts_first()
+    MS("K", T.K[:, 512:528], 0.0)
+    for l in range(N):
+        h = block(l, 0)
+        o = 16 * I16.index("ci") + 4 * h
+        CP("si", "M0.%d" % l, piece(T, "M", 0, 0, l, 1), tile(T.si, h, 64))
+        CP("ci", "c0.%d" % l, piece(T, "c", 0, 0, l, 1), T.pn[:, o:o + 4])
+    CP("Ki", "K", T.K[:, 0:512], T.Ki[:])
+    consts_iota()
+    for r in range(RO):
+        loc = home(r - 1) if r else 0
+        seq = [loc, loc ^ 1, loc ^ 2, loc ^ 3]
+        ta = loc // 2
+        tb = 1 - ta
+        both = [(t, c) for t in (ta, tb) for c in range(4)]
+        key_init("BM", "irow", "mb")
+        key_init("BX", "irw", "xb")
+        if r == 0:
+            z_rep(r, 0)
+            m_gather(r, 0)
+            m_gather(r, 1)
+            kc(r, 0)
+            x_gather(0)
+            m_gather(r, 2)
+            z_rep(r, 1)
+            kc(r, 1)
+            consts_later()
+            for l in range(N):
+                m_float(r, l)
+            kc2(r)
+            x_gather(1)
+            x_big(r, ta, both, 3)
+        else:
+            m_gather(r, seq[0])
+            k_write(r - 1)
+            m_gather(r, seq[1])
+            z_rep(r, ta)
+            kc(r, ta)
+            x_gather(ta)
+            m_gather(r, seq[2])
+            z_rep(r, tb, CFG["zg"])
+            kc(r, tb)
+            for l in seq:
+                m_float(r, l)
+            kc2(r)
+            if not CFG["xabs"]:
+                x_relu(ta)
+            x_gather(tb)
+            x_big(r, ta, both, seq[3])
+        x_keys(tb, 0, False)
+        x_relu(tb, CFG["rs"])
+        x_keys(tb, 1, True)
+        m_side(r)
+        choose()
+        features(r, lambda: pack(r))
+        pack2(r)
+        if r == 0:
+            consts_last()
+        if r < RO - 1:
+            survivors(0)
+            survivors(1)
+            survivors_sum()
+            lists(r)
+            survivors_out(r)
+            own_list()
+            k_onehot(CFG["oh"])
+            couplet_numbers(r)
+            names()
+            k_table(r)
+            k_old()
+            taxa(r)
+            k_delta(r)
+            k_read()
+        else:
+            survivors(0)
+            lists(r)
+            k_onehot(CFG["ohl"])
+            survivors(1)
+            survivors_sum()
+            own_list()
+            names()
+            k_table(r)
+            k_old()
+            survivors_out(r)
+            taxa(r)
+            k_delta(r)
+            k_read()
+    k_write(RO - 1)
+    PLAN["ops"] = [o[:3] + o[4:] for o in ops]
+    for i in issue_order(PLAN["ops"]):
+        ops[i][3]()
+    final["sent"] = sent[0]
+    for n in final:
+        need("C", (n, final[n]))

@@ -1,11 +1,12 @@
 from concourse.bass import DstId, RemoteDMATransfer
-from concourse.mybir import AluOpType as A, AxisListType, ActivationFunctionType as F
+from concourse.mybir import AluOpType as A, ActivationFunctionType as F
 
 N, RO = 4, 3
 H = "float16"
-U = 2.0 ** -24
-SU = 2.0 ** -16
-CFG = {"oh": "SSS", "ohl": "SVS", "zg": 8, "zs": 0, "rs": 640, "h0": 4, "h1": 6, "hv": 5, "xabs": False, "ex2": "VVV"}
+B = 2.0 ** 24
+BIG = 2.0 ** 45
+CFG = {"zr0": ("V" * 16, "V" * 16), "zr": ("S" * 16, "C" * 16, "C" * 6 + "V" * 10), "ex2": "VVV", "mg0": "SSSS", "mg": "SSSS", "rs0": (0, 0), "rs": (0, 0),
+       "rr": "S", "passes": 6, "cy": 0.9e-3, "ga": 1.6, "sem": 0.12, "hop": 2.9, "first": 1.0}
 
 SCRATCH = {}
 
@@ -16,27 +17,30 @@ def _decl(where, dtype, spec):
         SCRATCH[name] = (where, [128] + [int(v) for v in shape.split("x")], dtype)
 
 
-F16 = "df nf thr nthr ts ts2 tT Tt a8 m1 win nt P tA tB tC tD sd ek".split()
-I16 = "wi32 ix ai a15 uq ow c2 c2a u9 im vv ci ui".split()
-_decl("sbuf", "bfloat16", "X:2048 zi:768 zo:768 W:8192 R:4096 G:4096 ZR:8192 "
-      "I:128 nI:128 BO:128 E:528 H0:528 H1:528 EA:16 um:256 Rx:64 Wu:128 irow:128 irw:128 one:128 "
-      "xa:32x16 xb:32x16 xk:32x16 mb:32x16 crow:16 srow:512 arow:16 aw:128 rr:256 hz:64 ltb:256 c2b:256 oa:256 Fw:32 "
-      "oh:768 L1:256 L2:256 Oh:512 t0:512 t1:512 r8:288 r16:256 ra:288 ru:256")
-_decl("sbuf", H, "If:128 nIf:128 BOf:128 onef:128 vrow:128 drow:128 Mf:256 kcf:256 p1m:256 p2:256 EM:256")
-_decl("sbuf", "float32", "K:528 Mof:256 pm:8 sel8:8 hm:64 xs:288 msn:256 kxs:288 "
-      "asn:288 kms:256 tt:32 pf:304 bad:32 cand:32 hs:64 ex:256 ex2:256 nkx:256 tbc:256 g1:256 sx:256 us:256 ry:256 Kt:256 "
-      "nIq:128 Q:256 Wd:272 tb:512 tg:128 rc:64 ra2:64 om:32 wc:2 wi:4 sl:4 s1:16 s2:16")
-_decl("sbuf", "int32", "Ki:512 pn:208 o8:48 si:256 sh:256 li:48 l4:32 oi:32")
-_decl("sbuf", "uint16", "Mu:768 Mo:512 cu:48 co:32 kcu:256 b16:16 dl:8 il:16 ol:16 el:32 tl:16 wl:32")
-_decl("psum", "float32", "BX:32x16 BM:32x16 D0:512 D1:512 BA:512 BB:512 BL:512 BK:512")
+F16 = "df nf thr thq ts tT tr Tt m1 P f16 tA A1 mx".split()
+I16 = "win ix ai a15 ui uq u9 ow c2a c2 li lb im cn ci".split()
+_decl("sbuf", "bfloat16", "X:2048 zz:1536 W:8192 R:4096 G:4096 ZR:4096 Zs:512 Z:3840 Ip:128 "
+      "I:128 nI:128 BI:128 BO:128 E:256 E2:512 H0:512 H1:512 Rx:112 Wu:128 Wz:144 irow:128 irw:128 one:128 sel:8 "
+      "xa:16x17 xb:16x17 ma:32x9 mb:32x9 crow:16 srow:128 aw:128 rr:256 mk:512 oa:256 nk:32 f:32 "
+      "oh:768 Lc:256 Hs:16x64 t0:512 t1:512 t2:256 r8:256 ra:256 r16:256 ex2:256 Q:256 Qa:256 Qb:256 s16:8")
+_decl("sbuf", H, "If:128 nIf:128 hIf:128 BOf:128 onef:128 vrow:128 drow:128 Mf:256 kcf:256 pp:512 EM:256 c2h:16")
+_decl("sbuf", "float32", "K:512 Mof:256 pm:8 sel8:8 xs:256 asn:256 kxs:256 msn:256 kms:256 tt:32 pf:224 q:32 qe:32 ek:32 cand:32 "
+      "ex:256 ry:256 Kt:256 Ka:512 nIq:128 Iq:128 Wd:272 rc:64 ra2:64 om:32 wc:2 wi:4 sl:4 s1:16")
+_decl("sbuf", "int32", "Ki:512 pn:240 o8:48 ms4:4x64 ci4:4x4 si:256 sh:256 hh:256 pi:16 oi:16")
+_decl("sbuf", "uint16", "Mu:768 Mo:512 cu:48 co:32 kcu:256 b16:16 b2:16 il:16 zl:16 ol:16 el:16 al:16 tl:16 wl:32")
+_decl("psum", "float32", "BX:16x17 BM:56x9 DA:16x32 DB:16x32 DC:16x32 BA:512 BB:512 BL:512")
 
 MSGS = [k + str(r) for r in (1, 2) for k in "zMc"]
-SEMAPHORES = ["V", "S", "P", "C", "sent"] + ["d%d" % i for i in range(26)] + [m + "l%d" % l for m in MSGS for l in range(N)]
+SEMAPHORES = ["V", "S", "P", "C", "sent"] + ["d%d" % i for i in range(40)] + [m + "l%d" % l for m in MSGS for l in range(N)]
+ZAT = {(0, 0): 0, (1, 0): 4, (0, 1): 8, (0, 2): 12, (1, 1): 16, (1, 2): 20}
 
 
 def piece(T, kind, side, r, l0=0, n=N):
+    if kind == "z":
+        o = ZAT[side, r] + l0
+        return T.zz[:, 64 * o:64 * (o + n)]
     w = 4 if kind == "c" else 64
-    b = T[{"z": ("zi", "zo"), "M": ("Mu", "Mo"), "c": ("cu", "co")}[kind][side]]
+    b = T[{"M": ("Mu", "Mo"), "c": ("cu", "co")}[kind][side]]
     return b[:, w * (N * r + l0):w * (N * r + l0 + n)]
 
 
@@ -83,28 +87,75 @@ def engine_split(topo, me, rt):
 
 
 PLAN = {}
-ORDER = """2 29 -28 6 -5 1 7 7 -9 7 -2 8 -3 64 2 -62 -3 -10 7 4 -6 30 -32 28 -17 1 1 1 1 1 21 -38 78 -90 7 25 38 2 -67 1 25 2 4 36 1 -9 -27 31 -35 2 90 -59 -1 57 1 3 3 -31 -64 42 -9 57 8 -35 -59 32 4 7 -1 -5 63 -11 1 3 -1 5 4 -61 43 -22 34 38 -126 91 38 -87 53 -61 -2 -30 14 -1 -9 -5 64 24 42 -39 4 31 3 -58 56 -78 -41 -13 14 51 -67 47 34 -24 81 -115 1 117 -62 64 -39 38 -3 5 -81 9 -26 15 9 -2 -51 -13 16 120 -64 -14 83 -92 21 -55 130 -85 -61 41 66 -5 4 38 4 -74 -26 24 77 -41 42 -101 102 1 -37 49 -55 45 -1 -101 103 -78 26 54 -91 4 -62 148 2 14 -166 4 149 1 -149 4 146 10 -8 -53 1 5 58 16 -85 -1 58 11 9 10 -9 8 -48 -26 1 1 1 -8 1 1 7 1 -22 23 1 1 1 1 1 37 1 18 1 8 -48 49 -27 8 -129 101 48 1 -8 15 -6 1 1 -13 1 -11 24 -11 16 13 -48 51 -15 -37 54 -55 39 2 16 -17 -31 27 27 -12 -9 32 -31 -31 50 2 -54 1 33 8 24 1 -23 2 -11 1 1 1 1 10 6 -32 1 32 -6 7 21 -20 1 1 19 -18 1 1 2 -17 20 -17 18 17 -11 -1 6 -10 -186 192 -203 209 -1 12 1 -11 12 -8 -202 186 6 11 -85 82 -1 8 -2 -18 1 18 15 -9 8 -16 23 -14 1 1 7 -6 7 -6 -6 38 -1 2 -26 -6 18 -17 33 3 -15 -3 17 3 -6 2 8 -3 -33 1 38 -8 9 -32 -2 1 30 31 -52 -3 8 13 1 30 -27 4 -1 -36 -2 67 -4 -62 6 -1 60 -2 -45 53 -4 3 -2 1 3 -62 64 -60 59 -60 34 1 -9 37 2 1 -4 6 -66 62 6 -1 -2 4 1 37 -36 1 1 1 1 1 1 1 1 10 -8 9 -89 91 -67 1 1 1 54 -2 11 9 -71 1 1 3 1 1 1 1 1 1 1 1 1 1 1 38 1 17 5 -21 23 1 -7 1 1 1 -12 -7 24 -23 7 1 -7 10 57 -34 -22 23 2 2 2 -16 3 -2 -2 3 -18 1 26 33 -40 1 1 1 1 14 -1 2 -10 11 1 20 -11 -19 33 -1 3 -1 -23 1 -9 10 1 1 1 1 -15 16 -14 32 -31 15 1 1 9 -8 24 -7 6 -7 -15 17 -16 1 1 21 -11 1 6 1 -2 -1 9 10 -2 7 -17 38 1 -28 31 3 -4 -38 1 1 35 -39 13 -8 1 20 -19 5 -4 35 -1 4 4 -3 -33 11 -10 38 -8 6 3 28 -59 -1 -2 4 5 2 -4 8 14 -1 7 -3 29 -2 -62 4 63 -28 24 3 2 -66 -1 10 5 3 52 1 -3 -52 -4 60 -3 4 2 -61 60 2 -29 30 2 -1 3 -42 43 -2 -40 1 42 1 1 2 -1 -44 1 1 53 -9 1 1 1 1 1 1 10 -8 9 -10 11 1 -5 -57 1 2 1 1 1 1 1 1 1 1 1 1 1 1 57 -19 1 19 3 3 -24 23 -4 -11 -7 24 -16 11 -10 1 1 45 -31 1 2 29 -27 28 -26 -5 7 2 1 23 1 -26 3 1 1 -11 -27 39 -10 11 1 1 1 17 1 1 -43 46 14 -48 26 -4 18 1 -28 19 -18 1 27 2 -11 13 1 -2 5 -1 -68 70 1 1 -37 1 1 1 1 1 14 -55 2 -3 75 -11 -4 -1 -2 1 18 2 -1 2"""
+BANK = ("BX", "BM", "DA", "DB", "DC", "BA", "BB", "BL")
 
 
 def issue_order(ops):
-    out = [-1]
-    for d in ORDER.split():
-        out.append(out[-1] + int(d))
-    out = out[1:]
-    if sorted(out) != list(range(len(ops))):
-        return list(range(len(ops)))
-    pos = {i: p for p, i in enumerate(out)}
+    n = len(ops)
+    pre = [dict() for _ in ops]
     wr, rd = {}, {}
-    for i, o in enumerate(ops):
-        for k in o[1] + o[2]:
-            assert pos[wr.get(k, i)] <= pos[i]
-        for k in o[2]:
-            assert all(pos[j] <= pos[i] for j in rd.get(k, []))
-        for k in o[1]:
+    for i, (q, r, w, t, late) in enumerate(ops):
+        for k in r + w:
+            if k in wr:
+                j = wr[k]
+                pre[i][j] = max(pre[i].get(j, 0), ops[j][4].get(k, 0))
+        for k in w:
+            for j in rd.get(k, []):
+                pre[i].setdefault(j, 0)
+        for k in r:
             rd.setdefault(k, []).append(i)
-        for k in o[2]:
+        for k in w:
             wr[k], rd[k] = i, []
-    return out
+    suc = [[] for _ in ops]
+    for i in range(n):
+        pre[i].pop(i, None)
+        for j in pre[i]:
+            suc[j].append(i)
+
+    def gap(j, i):
+        return ops[j][3] + pre[i][j] + (0.0 if ops[j][0] == ops[i][0] == "P" else CFG["sem"])
+    last = [ops[i][3] + max(list(ops[i][4].values()) + [0]) for i in range(n)]
+    banks = [[k for k in BANK if k in o[1] + o[2]] for o in ops]
+
+    def place(rank, back):
+        before, after = (suc, pre) if back else (pre, suc)
+        left = [len(b) for b in before]
+        ready = [i for i in range(n) if not left[i]]
+        t, busy = [0.0] * n, {}
+        while ready:
+            i = min(ready, key=lambda i: rank[i])
+            ready.remove(i)
+            q, d = ops[i][0], ops[i][3]
+            if back:
+                a = max([last[i] - d] + [t[j] + ops[j][3] + gap(i, j) - d for j in suc[i]])
+            else:
+                a = max([0.0] + [t[j] + gap(j, i) for j in pre[i]])
+            taken = sorted(busy.get(q, []) + [(x - CFG["sem"], y + CFG["sem"]) for k in banks[i] for x, y, o in busy.get(k, []) if o != q])
+            for x, y in taken:
+                if x < a + d - 1e-9 and y > a + 1e-9:
+                    a = y
+            t[i] = a
+            busy.setdefault(q, []).append((a, a + d))
+            for k in banks[i]:
+                busy.setdefault(k, []).append((a, a + d, q))
+            for j in after[i]:
+                left[j] -= 1
+                if not left[j]:
+                    ready.append(j)
+        return t
+    tail = [0.0] * n
+    for i in range(n - 1, -1, -1):
+        tail[i] = max([last[i]] + [gap(i, j) + tail[j] for j in suc[i]])
+    rank, best = [-x for x in tail], None
+    for _ in range(CFG["passes"]):
+        t = place(rank, False)
+        span = max(t[i] + last[i] for i in range(n))
+        if best is None or span < best[0]:
+            best = (span, t)
+        u = place([-(t[i] + ops[i][3]) for i in range(n)], True)
+        rank = [-(u[i] + ops[i][3]) for i in range(n)]
+    PLAN["span"] = best[0]
+    return sorted(range(n), key=lambda i: (best[1][i], i))
 
 
 def relay_program(g, core, T, topo):
@@ -134,8 +185,8 @@ def rank_program(g, core, T, topo):
     Qs = {"V": g.vector, "S": g.scalar, "P": g.tensor, "C": g, "Y": g.sync}
     cnt = {"V": 0, "S": 0, "P": 0, "C": 0}
     seen = {q: {} for q in Qs}
+    known = {}
     wr, rd, final, nd, sent = {}, {}, {}, [0], [0]
-    BANK = ("BX", "BM", "D0", "D1", "BA", "BB", "BL", "BK")
     s = {n: T.pf[:, 16 * j:16 * j + 16] for j, n in enumerate(F16)}
     s.update({n: T.pn[:, 16 * j:16 * j + 16] for j, n in enumerate(I16)})
 
@@ -143,6 +194,8 @@ def rank_program(g, core, T, topo):
         if seen[q].get(tok[0], 0) < tok[1]:
             Qs[q].wait_ge(T.sem[tok[0]], tok[1])
             seen[q][tok[0]] = tok[1]
+            for n, c in known.get(tok, {}).items():
+                seen[q][n] = max(seen[q].get(n, 0), c)
 
     def order(q, r, w):
         toks = {}
@@ -153,10 +206,11 @@ def rank_program(g, core, T, topo):
             for t in deps:
                 if not (q == "P" and t[0] == "P"):
                     toks[t[0]] = max(toks.get(t[0], 0), t[1])
-        for n in toks:
+        for n in sorted(toks, key=lambda n: -len(known.get((n, toks[n]), {}))):
             need(q, (n, toks[n]))
 
-    def mark(tok, r, w):
+    def mark(q, tok, r, w):
+        known[tok] = dict(seen[q])
         for k in r:
             rd.setdefault(k, []).append(tok)
         for k in w:
@@ -164,34 +218,33 @@ def rank_program(g, core, T, topo):
         final[tok[0]] = tok[1]
 
     ops = []
+    CY = CFG["cy"]
 
-    def op(q, r, w, f, kind, n):
+    def op(q, r, w, f, t):
         r, w = r.split(), w.split()
+        ww = [k for k in w if k[0] != "~"]
 
         def emit():
-            order(q, r, w)
+            order(q, r, ww)
             cnt[q] += 1
             f().then_inc(T.sem[q], 1)
-            mark((q, cnt[q]), r, w)
+            mark(q, (q, cnt[q]), r, ww)
         if q == "P" and ops[-1][:3] == (q, r, w):
             a = ops.pop()
-            ops.append((q, r, w, lambda: (a[3](), emit()), kind, n + a[5], {}))
-        elif q == "V" and w[0][:2] == "ZR" and int(w[0][5:]) % 4 and ops[-1][:2] == (q, r):
-            a = ops.pop()
-            ops.append((q, r, a[2] + w, lambda: (a[3](), emit()), kind, n + a[5], {}))
+            ops.append((q, r, w, lambda: (a[3](), emit()), t + a[4], a[5]))
         else:
-            ops.append((q, r, w, emit, kind, n, {}))
+            ops.append((q, r, w, emit, t, {k: 0.15 for k in w} if q == "P" else {}))
 
     def dma(q, out, in_, r, w):
-        r, w = r.split(), w.split()
+        r, w = r.split(), w.split() or ["out%d" % len(ops)]
 
         def emit():
             order(q, r, w)
             n = "d%d" % nd[0]
             nd[0] += 1
             Qs[q].dma_start(out, in_).then_inc(T.sem[n], 16)
-            mark((n, 16), r, w)
-        ops.append((q, r, w, emit, "dma", size(out) * (2 if "16" in str(out.dtype) else 4), {}))
+            mark(q, (n, 16), r, w)
+        ops.append((q, r, w, emit, 0.06, {k: 1.8 + size(out) / 2000 for k in w}))
 
     def size(a):
         n = 1
@@ -199,25 +252,23 @@ def rank_program(g, core, T, topo):
             n *= d
         return n
 
-    def kind_of(r, w, out, a, base):
-        if "X.a" in w.split():
-            return "scatter", size(a)
-        if set(r.split()) & set("b16 bH il ol el tl dl wl".split()) or w[:3] == "kcu" or w[:2] == "G." or w[:3] == "W.x":
-            return "gather", size(out)
-        if base == "half":
-            return "plain", size(a) * (0.5 if "16" in str(out.dtype) and "16" in str(a.dtype) else 1)
-        return "plain", size(a) * base
+    def wide(*aps):
+        return 0.5 if all("16" in str(a.dtype) for a in aps) else 1.0
 
     v, sc, pe = g.vector, g.scalar, g.tensor
 
-    def TT(r, w, out, a, b, o):
-        op("V", r, w, lambda: v.tensor_tensor(out, a, b, o), *kind_of(r, w, out, a, 1 if set(r.split()) & set(BANK) else 2))
+    def cost(n, c, ga):
+        return 0.06 + n * CFG["ga"] * ga * CY if ga else max(64, n * c) * CY
 
-    def TS(r, w, out, a, s1, o0, s2=None, o1=None):
+    def TT(r, w, out, a, b, o, ga=0):
+        op("V", r, w, lambda: v.tensor_tensor(out, a, b, o), cost(size(b), 1 if set(r.split()) & set(BANK) else 2, ga))
+
+    def TS(r, w, out, a, s1, o0, s2=None, o1=None, ga=0):
+        t = cost(size(out), wide(out, a), ga)
         if o1 is None:
-            op("V", r, w, lambda: v.tensor_scalar(out, a, s1, None, o0), *kind_of(r, w, out, a, "half"))
+            op("V", r, w, lambda: v.tensor_scalar(out, a, s1, None, o0), t)
         else:
-            op("V", r, w, lambda: v.tensor_scalar(out, a, s1, s2, o0, o1), *kind_of(r, w, out, a, "half"))
+            op("V", r, w, lambda: v.tensor_scalar(out, a, s1, s2, o0, o1), t)
 
     def tt(out, a, b, o):
         TT(a + " " + b, out, s[out], s[a], s[b], o)
@@ -225,37 +276,42 @@ def rank_program(g, core, T, topo):
     def ts(out, a, s1, o0, s2=None, o1=None):
         TS(a, out, s[out], s[a], s1, o0, s2, o1)
 
-    def CP(r, w, out, a):
-        op("V", r, w, lambda: v.tensor_copy(out, a), *kind_of(r, w, out, a, "half"))
+    def CP(r, w, out, a, ga=0):
+        op("V", r, w, lambda: v.tensor_copy(out, a), cost(size(a if ga > 1 else out), wide(out, a), ga))
 
     def MS(w, out, c):
-        op("V", "", w, lambda: v.memset(out, c), *kind_of("", w, out, out, "half"))
+        op("V", "", w, lambda: v.memset(out, c), cost(size(out), wide(out), 0))
 
     def SCAN(r, w, out, d0, d1, o0, o1, init=0.0):
-        op("V", r, w, lambda: v.tensor_tensor_scan(out, d0, d1, init, o0, o1), "plain", size(out))
+        op("V", r, w, lambda: v.tensor_tensor_scan(out, d0, d1, init, o0, o1), cost(size(out), 1, 0))
 
-    def ACT(r, w, out, a, f=F.Copy, **kw):
-        op("S", r, w, lambda: sc.activation(out, a, f, **kw), *kind_of(r, w, out, a, 1))
+    def ACT(r, w, out, a, f=F.Copy, ga=0, **kw):
+        op("S", r, w, lambda: sc.activation(out, a, f, **kw), cost(size(out), 1, ga))
 
-    def MM(r, w, out, l, rh, st, sp, fence=False):
-        def f():
-            if fence:
-                need("P", ("P", cnt["P"] - 1))
-            return pe.matmul(out, l, rh, st, sp)
-        op("P", r, w, f, "mm", max(min(64, size(l)), size(rh)) * (4 if "32" in str(l.dtype) else 1))
+    def MM(r, w, out, l, rh, st, sp):
+        op("P", r, w, lambda: pe.matmul(out, l, rh, st, sp), max(min(64, size(l)), size(rh)) * (4 if "32" in str(l.dtype) else 1) * CY / 2)
 
     def IO(w, out, pat, base=0, cm=0, flt=True):
         if flt:
-            op("C", "", w, lambda: g.iota(out, pat, base, cm, allow_small_or_imprecise_dtypes=True), "pool", size(out))
+            op("C", "", w, lambda: g.iota(out, pat, base, cm, allow_small_or_imprecise_dtypes=True), 0.15 + 2 * CY * size(out))
         else:
-            op("C", "", w, lambda: g.iota(out, pat, base, cm), "pool", size(out))
+            op("C", "", w, lambda: g.iota(out, pat, base, cm), 0.15 + 2 * CY * size(out))
 
     def SEL(r, w, out, a, pat, o, base, cm, fill=0.0):
-        op("C", r, w, lambda: g.affine_select(out, a, pat, o, fill, base, cm), "pool", size(out))
+        op("C", r, w, lambda: g.affine_select(out, a, pat, o, fill, base, cm), 0.2 + 2 * CY * size(out))
+
+    def COPY(q, r, w, out, a, ga=0):
+        if q == "V":
+            CP(r, w, out, a, ga)
+        elif q == "S":
+            ACT(r, w, out, a, F.Copy, ga)
+        else:
+            SEL(r, w, out, a, [[0, size(out)]], A.is_ge, 0, 0)
 
     def send(kind, r, src):
-        hops = {"%s%d.%d" % (kind, r, l): 1 if via is None else 2 for l, dst, via in routes(T, topo, rank, r)}
-        ops.append(("C", [src], list(hops), lambda: send_now(kind, r, src), "send", 0, hops))
+        hop = CFG["hop"] + (CFG["first"] if r == 1 else 0)
+        hops = {"%s%d.%d" % (kind, r, l): hop if via is None else 2 * hop + 0.6 for l, dst, via in routes(T, topo, rank, r)}
+        ops.append(("C", [src], list(hops) + ["sends"], lambda: send_now(kind, r, src), 0.6, hops))
 
     def send_now(kind, r, src):
         m = kind + str(r)
@@ -275,245 +331,239 @@ def rank_program(g, core, T, topo):
                 frm = (rank - h) % N
                 via = [x[2] for x in routes(T, topo, frm, r) if x[0] == l][0]
                 n = len(topo.engines(T.cores[frm] if via is None else via, core))
-                mark((m + "l%d" % l, n), [], ["%s.%d" % (m, l)])
-
-    def lanes(m, ls=range(N)):
-        return " ".join("%s.%d" % (m, l) for l in ls)
+                wr["%s.%d" % (m, l)] = (m + "l%d" % l, n)
+                final[m + "l%d" % l] = n
 
     def tile(b, t, w=128):
         return b[:, w * t:w * t + w]
 
-    dma("Y", T.si[:], T.ms[:], "", "si")
-    dma("S", T.X[:, 0:1024], T.tx[:, 0:1024], "", "X.a")
-    dma("Y", T.X[:, 1024:2048], T.tx[:, 1024:2048], "", "X.b")
+    def at(kind, r, l):
+        if r and l == home(r - 1):
+            return piece(T, kind, 1, r - 1, l, 1), "%so%d" % (kind, r - 1)
+        return piece(T, kind, 0, r, l, 1), "%s%d.%d" % (kind, r, l)
+
+    def zparts(r, t):
+        if r and home(r - 1) // 2 == t:
+            return [(l, 1) + at("z", r, l) for l in (2 * t, 2 * t + 1)]
+        return [(2 * t, 2, piece(T, "z", 0, r, 2 * t, 2), "z%d.%d z%d.%d" % (r, 2 * t, r, 2 * t + 1))]
+
+    XX = "X.0 X.1 X.2 X.3"
+
+    dma("Y", T.ms4[:], T.ms[:], "", "ms4")
+    dma("S", T.X[:, 0:1024], T.tx[:, 0:1024], "", "X.0 X.1")
+    dma("Y", T.X[:, 1024:2048], T.tx[:, 1024:2048], "", "X.2 X.3")
+    dma("S", T.Ki[:], T.kt[:], "", "K")
+    dma("Y", T.ci4[:], T.cp[:], "", "ci4")
     for l in range(N):
         dma("SY"[l // 2], piece(T, "z", 0, 0, l, 1), tile(T.z, block(l, 0), 64), "", "z0.%d" % l)
-    dma("Y", s["ci"], T.cp[:], "", "ci")
-    dma("S", T.Ki[:], T.kt[:], "", "Ki")
-    XX = "X.a X.b"
+    for t in (0, 1):
+        CP("ms4", "M0.%d M0.%d" % (2 * t, 2 * t + 1), piece(T, "M", 0, 0, 2 * t, 2), T.ms4[:, t::2, :])
+        CP("ci4", "c0.%d c0.%d" % (2 * t, 2 * t + 1), piece(T, "c", 0, 0, 2 * t, 2), T.ci4[:, t::2, :])
 
-    def consts_first():
+    def consts():
+        p16 = T.pm[:, 0:1]
         IO("one", T.one[:], [[0, 128]], 1)
         SEL("one", "I", T.I[:], T.one[:], [[-1, 128]], A.is_equal, 0, 1)
-        IO("xk", T.xk[0:32, :, 0:9], [[0, 16], [8, 2], [1, 9]])
-        IO("irow", T.irow[0:32, :], [[1, 128]])
-        IO("irow16", T.irw[0:32, :], [[16, 128]])
         SEL("one", "s1", T.s1[:, 0:8], T.one[:, 0:8], [[-16, 8]], A.is_ge, 0, 1)
         SEL("s1", "sel8", T.sel8[:], T.s1[:, 0:8], [[16, 8]], A.is_ge, 15, -1)
-        IO("sh", T.sh[:, 0:1], [[0, 1]], 0, 1, False)
-        ACT("I", "nI", T.nI[:], T.I[:], scale=-1.0)
-        xk = T.xk[0:32, :, 0:9]
-        ACT("xk", "xb", T.xb[0:32, :, 0:9], xk, scale=U)
-        ACT("xk", "mb", T.mb[0:32, :, 0:9], xk, F.Identity, scale=128 * U, bias=2048 * U)
-        ACT("xk", "xa", T.xa[0:32, :, 0:9], xk, F.Identity, scale=0.0, bias=U)
-        for b, c in (("xa", 0.0), ("xb", -2.0), ("mb", 0.0)):
-            ACT("xk", b, T[b][0:32, :, 8], T.xk[0:32, :, 8], F.Identity, scale=0.0, bias=c)
-        for j, c in enumerate((-1.0, 2.0, 1.0, 0.5)):
-            if j != 2 or CFG["xabs"]:
-                ACT("sel8", "Rx", T.Rx[:, 16 * j:16 * j + 16:2], T.sel8[:], scale=c * 2.0 ** -12)
-                ACT("sel8", "Rx", T.Rx[:, 16 * j + 1:16 * j + 16:2], T.sel8[:], scale=c * SU)
-
-    def consts_iota():
-        IO("t1", T.t1[:], [[0, 32], [1, 16]])
-        SEL("one", "um", T.um[:, 0:128], T.one[:], [[-16, 8], [0, 16]], A.is_ge, 0, 1)
-        SEL("um", "BO", T.BO[:], T.um[:, 0:128], [[16, 8], [0, 16]], A.is_ge, 15, -1)
-        IO("sx", T.sx[0:32, 0:128], [[0, 8], [37, 16]])
-        IO("li.a", T.li[:, 0:16], [[1, 16]], 0, 0, False)
+        IO("irow", T.irow[0:32, :], [[1, 128]])
+        IO("irw", T.irw[0:32, :], [[16, 128]])
+        IO("xb", T.xb[0:32, :, :], [[0, 16], [1, 17]])
+        IO("mb", T.mb[0:32, :, :], [[0, 16], [1024, 2], [128, 9]], 2048)
+        IO("pi", T.pi[:, 0:1], [[0, 1]], 0, 1, False)
+        IO("t2", T.t2[:], [[0, 16], [1, 16]])
+        IO("oi", T.oi[:], [[1, 16]], 0, 0, False)
+        MS("Z.0", T.Z[:, 0:896], 0.0)
+        for a, o in enumerate((896, 2048, 2944)):
+            dma("Y", T.Z[:, o:o + 896], T.Z[:, 0:896], "Z.0", "Z.%d" % (a + 1))
+        dma("Y", T.r16[:], T.Z[:, 0:256], "Z.0", "r16")
+        dma("Y", T.r8[:], T.Z[:, 0:256], "Z.0", "r8")
+        dma("Y", T.Zs[:], T.Z[:, 0:512], "Z.0", "Zs Zs.0 Zs.1 Zs.2 Zs.3")
+        SEL("one", "Ip", T.Ip[:], T.one[:], [[-1, 16], [-16, 8]], A.is_equal, 0, 1)
+        IO("ra", T.ra[:], [[0, 256]], 16)
+        IO("s2", T.Wd[0:32, 0:128], [[0, 8], [37, 16]])
+        IO("t1", T.t1[:], [[0, 64], [1, 8]])
+        IO("t0", T.t0[:], [[0, 2], [1, 32], [0, 8]])
         for r in range(RO):
-            IO("o8", tile(T.o8, r, 16), [[512, 2], [1024, 2], [128, 4]], 512 * r, 0, False)
-        IO("s2", T.s2[:], [[-1, 16]], 14, 0)
-        IO("hz hz1 hz2", T.hz[:], [[0, 64]])
-        IO("crow", T.crow[:], [[4096, 2], [0, 8]])
-        IO("Wd", T.Wd[:, 256:272], [[0, 16]])
-        for b in ("E", "H0", "H1"):
-            IO(b, T[b][:, 512:528], [[0, 16]])
-        for j, c in enumerate((0, 2, 512, 16)):
-            IO("hm", T.hm[:, j::4], [[0, 16]], c)
-        IO("t0", T.t0[:], [[1, 32], [0, 16]])
-        IO("oi", T.oi[:, 0:8], [[64, 8]], 0, 0, False)
-        IO("oi2", T.oi[:, 8:12], [[64, 4]], 0, 1, False)
-        IO("ZR.y", T.ZR[:, 2048:3072], [[0, 1024]])
-        dma("Y", T.ZR[:, 3072:4096], T.ZR[:, 2048:3072], "ZR.y", "ZR.x")
-        dma("Y", T.ZR[:, 6144:8192], T.ZR[:, 2048:4096], "ZR.y ZR.x", "ZR.z")
+            IO("o8", tile(T.o8, r, 16), [[512, 2], [1024, 2], [128, 4]], 512 * r, 8, False)
+        IO("crow", T.crow[0:32, :], [[4096, 2], [0, 8]])
+        IO("Wd1", T.Wd[:, 256:272], [[0, 16]])
+        IO("sl0", T.pi[:, 8:12], [[64, 4]], 0, 1, False)
+        IO("b20", T.pn[:, 0:16], [[0, 8], [-1, 2]], 0, 0, False)
 
-    def consts_later():
-        p16 = T.pm[:, 0:1]
-        TS("sh", "ai", T.pn[:, 32:33], T.sh[:, 0:1], 15, A.bitwise_and)
+        ACT("I", "nI", T.nI[:], T.I[:], scale=-1.0)
+        for b, c, o in (("xa", 1.0, T.xa[0:32, :, :]), ("ma", 1.0, T.ma[0:32, :, :])):
+            MS(b, o, c)
+        for b, c, o in (("xa", 0.0, T.xa[0:32, :, 16]), ("xb", 0.0, T.xb[0:32, :, 16]), ("ma", 0.0, T.ma[0:32, :, 8]), ("mb", -960.0, T.mb[0:32, :, 8])):
+            MS(b, o, c)
+        for h in (0, 1):
+            ACT("sel8", "Rx", T.Rx[:, 16 * h:16 * h + 16:2], T.sel8[:], scale=4096.0)
+            ACT("sel8", "Rx", T.Rx[:, 16 * h + 1:16 * h + 16:2], T.sel8[:], scale=B * (2 * h - 1))
+        ACT("sel8", "Rm", T.Rx[:, 96:112:2], T.sel8[:], scale=2048.0)
+        ACT("sel8", "Rm", T.Rx[:, 97:112:2], T.sel8[:], scale=128.0)
+        ACT("Rx", "Rx1", T.Rx[:, 32:64], T.Rx[:, 0:32], scale=-1.0)
+        ACT("Rx", "Rx2", T.Rx[:, 64:96], T.Rx[:, 0:32], scale=2.0)
+        MS("r16", T.r16[:, 0::16], BIG)
+        MS("r8", T.r8[:, 0::8], BIG)
+        MS("ra", T.ra[:, 0::16], -BIG)
+
+        TS("pi", "pi1", T.pi[:, 1:2], T.pi[:, 0:1], 15, A.bitwise_and)
+        TS("pi", "pi2", T.pi[:, 2:3], T.pi[:, 0:1], 1, A.arith_shift_right, 7, A.bitwise_and)
+        TS("pi", "pi3", T.pi[:, 3:4], T.pi[:, 0:1], 1, A.bitwise_and)
+        TS("pi", "pi4", T.pi[:, 4:5], T.pi[:, 0:1], 64, A.bitwise_and)
+        TS("pi", "pi5", T.pi[:, 5:6], T.pi[:, 0:1], 112, A.bitwise_and)
+        CP("pi1 pi2 pi3 pi4 pi5", "pm", T.pm[:, 0:5], T.pi[:, 1:6])
+        TS("pm", "pm5", T.pm[:, 5:6], p16, 2.0, A.mult, 1.0, A.add)
+        TS("pm", "pm6", T.pm[:, 6:7], p16, 16.0, A.add)
+        TS("pm", "pm7", T.pm[:, 7:8], T.pm[:, 4:5], -8.0, A.mult)
+        TS("t2 pm", "E", T.E[:], T.t2[:], p16, A.is_equal)
+        CP("oi", "b16", T.b16[:], T.oi[:])
+        TS("b20 pm5", "b2 win", T.b2[:], T.pn[:, 0:16], T.pm[:, 5:6], A.add)
         CP("I", "If", T.If[:], T.I[:])
-        CP("ai", "pm", p16, T.pn[:, 32:33])
-        CP("nI", "nIf", T.nIf[:], T.nI[:])
-        TS("t1 pm", "E", T.E[:, 0:512], T.t1[:], p16, A.is_equal)
-        TS("pm", "pm1", T.pm[:, 1:2], p16, 2.0, A.mult, 1.0, A.add)
-        TS("pm", "pm3", T.pm[:, 3:4], p16, 16.0, A.add)
-        TS("pm", "pm4", T.pm[:, 4:5], p16, 8.0, A.mult)
-        TS("sx", "vrow", T.vrow[0:32, :], T.sx[0:32, 0:128], -1023.5, A.add)
-        CP("sx", "drow", T.drow[0:32, :], T.sx[0:32, 0:128])
+        TS("I", "nIf", T.nIf[:], T.I[:], -1.0, A.mult)
+        TS("I", "hIf", T.hIf[:], T.I[:], 0.5, A.mult)
+        TS("s2", "vrow", T.vrow[0:32, :], T.Wd[0:32, 0:128], -1023.5, A.add)
+        CP("s2", "drow Wd", T.drow[0:32, :], T.Wd[0:32, 0:128])
         MS("onef", T.onef[0:32, :], 1.0)
+        ACT("sel8 b16", "BO", T.BO[:], T.sel8[:].indirect(T.b16[:, 0:8]), F.Copy, 1)
         CP("BO", "BOf", T.BOf[:], T.BO[:])
-        CP("li.a", "b16", T.b16[:], T.li[:, 0:16])
-        TS("s2", "s1", T.s1[:], T.s2[:], 0.0, A.is_lt, 16.0, A.mult)
-        TT("s1 s2", "s2", T.s2[:], T.s2[:], T.s1[:], A.add)
-        TS("sh", "a15", T.pn[:, 48:49], T.sh[:, 0:1], 63, A.bitwise_and)
-        TS("sh", "uq", T.pn[:, 64:65], T.sh[:, 0:1], 64, A.bitwise_and)
-        CP("uq", "pm6", T.pm[:, 6:7], T.pn[:, 64:65])
-        TS("oi2 pm6", "oi2", T.oi[:, 8:12], T.oi[:, 8:12], T.pm[:, 6:7], A.add)
-        TS("oi2", "oi3", T.oi[:, 16:20], T.oi[:, 8:12], 255, A.bitwise_and)
-        CP("a15", "pm5", T.pm[:, 5:6], T.pn[:, 48:49])
-        CP("oi3", "sl", T.sl[:], T.oi[:, 16:20])
-        TS("oi pm5", "dl", T.dl[:], T.oi[:, 0:8], T.pm[:, 5:6], A.add)
-        TS("s2 pm", "EA", T.EA[:], T.s2[:], p16, A.is_equal)
-        zero = T.ZR[:, 2048:2336]
-        SEL("ZR.y", "r16", T.r16[:], T.ZR[:, 2048:2304], [[0, 16], [1, 16]], A.not_equal, 0, 0, 4.0)
-        SEL("ZR.y", "r8", T.r8[:], zero, [[0, 32], [1, 9]], A.not_equal, 0, 0, 8.0)
-        SEL("ZR.y", "ra", T.ra[:], zero, [[0, 32], [1, 9]], A.is_equal, -8, 0, 2 * U)
-        SEL("ZR.y", "ru", T.ru[:], T.ZR[:, 2048:2304], [[0, 16], [1, 16]], A.not_equal, 0, 0, -2.0 ** 18)
-        TS("o8 pm4", "o8", T.o8[:], T.o8[:], T.pm[:, 4:5], A.add)
-        TS("o8", "o8", T.o8[:], T.o8[:], 2047, A.bitwise_and)
-        IO("ra", T.ra[:, 0::18], [[0, 16]], -8)
-
-    def consts_scalar():
-        ACT("nI", "nIq", T.nIq[:], T.nI[:])
-        ACT("E BO", "um", T.um[:], T.E[:, 0:256], F.Identity, scale=2.0 ** 17, bias=-2.0 ** 17)
-        ACT("BO pm1", "Wu", T.Wu[:], T.BO[:], scale=T.pm[:, 1:2])
-        ACT("E", "srow", T.srow[0:32, 0:256], T.E[0:32, 0:256], F.Identity, scale=0.0, bias=2.0 ** -125)
-        ACT("E", "srow", T.srow[0:32, 256:512], T.E[0:32, 0:256], F.Identity, scale=0.0, bias=2.0 ** -117)
-        ACT("one", "arow", T.arow[:], T.one[:, 0:16], scale=2048 * SU)
-        ACT("one", "aw", T.aw[:], T.one[:], scale=-8 * SU)
-
-    def consts_last():
-        TS("t0 pm", "H0", T.H0[:, 0:512], T.t0[:], T.pm[:, 0:1], A.is_equal)
-        TS("t0 pm3", "H1", T.H1[:, 0:512], T.t0[:], T.pm[:, 3:4], A.is_equal)
-        MS("t1", T.t1[0:32, 0:128], 0.25)
-        MS("L2", T.L2[0:32, 0:128], 0.0)
-        MS("t1", T.t1[0:32, 5:116:5], 0.5)
-        MS("t1", T.t1[0:32, 0:1], 2.0 ** 58)
-        SCAN("t1 L2", "Q", T.Q[0:32, 0:128], T.t1[0:32, 0:128], T.L2[0:32, 0:128], A.mult, A.add, 2.0 ** 59)
-        for j in range(4):
-            ACT("Q", "L1", T.L1[0:32, 64 * j:64 * j + 64], T.Q[0:32, 64 * (j // 2):64 * (j // 2) + 64])
+        ACT("BO pm5", "Wu", T.Wu[:], T.BO[:], scale=T.pm[:, 5:6])
+        MS("Wz", T.Wz[:], 0.0)
+        ACT("sel8 pm5", "Wz", T.Wz[:, 15:143:16], T.sel8[:], scale=T.pm[:, 5:6])
+        ACT("I", "nIq", T.nIq[:], T.I[:], scale=-1.0)
+        ACT("I", "Iq", T.Iq[:], T.I[:])
+        ACT("I", "BI", T.BI[:], T.I[:], scale=2 * B)
+        ACT("one", "aw", T.aw[:], T.one[:], scale=8 * B)
+        ACT("sel8", "sel", T.sel[:], T.sel8[:])
+        ACT("sel8", "s16", T.s16[:], T.sel8[:], scale=1 / 16)
+        TS("o8 pm7", "o8", T.o8[:], T.o8[:], T.pm[:, 7:8], A.add)
+        TS("o8", "o8", T.o8[:, 0:32], T.o8[:, 0:32], 2047, A.bitwise_and)
+        TS("o8", "o8", T.o8[:, 32:48], T.o8[:, 32:48], 511, A.bitwise_and)
+        TS("t1 pm", "E2", T.E2[:], T.t1[:], T.pm[:, 1:2], A.is_equal)
+        TS("t0 pm", "H0", T.H0[:], T.t0[:], p16, A.is_equal)
+        TS("t0 pm6", "H1", T.H1[:], T.t0[:], T.pm[:, 6:7], A.is_equal)
+        TS("sl0 pm", "sl0", T.pi[:, 8:12], T.pi[:, 8:12], T.pm[:, 3:4], A.add)
+        TS("sl0", "sl1", T.pi[:, 12:16], T.pi[:, 8:12], 255, A.bitwise_and)
+        CP("sl1", "sl", T.sl[:], T.pi[:, 12:16])
+        MS("Qa", T.Qa[0:32, :], 0.25)
+        MS("Qb", T.Qb[0:32, :], 0.0)
+        MS("Qa", T.Qa[0:32, 2::4], 0.5)
+        MS("Qb", T.Qb[0:32, 0::128], 2.0 ** 59)
+        TS("Qb", "Qb", T.Qb[0:32, 0::128], T.Qb[0:32, 0::128], 2.0 ** 59, A.mult)
+        MS("Qa", T.Qa[0:32, 64::128], 2.0 ** -10)
+        MS("Qa", T.Qa[0:32, 0::128], 0.0)
+        SCAN("Qa Qb", "Q", T.Q[0:32, :], T.Qa[0:32, :], T.Qb[0:32, :], A.mult, A.add)
         for j in (0, 1):
-            MM("L1 one", "D0", T.D0[:, 2 * j:2 * j + 2], T.L1[0:1, 128 * j:128 * j + 128], T.one[0:1, 0:2], True, True)
-        ACT("D0", "wc", T.wc[:], T.D0[:, 0:4:2])
+            MM("Q one", "BL", T.BL[:, 2 * j:2 * j + 2], T.Q[0:1, 64 * j:64 * j + 128], T.one[0:1, 0:2], True, True)
+        ACT("BL", "wc", T.wc[:], T.BL[:, 0:4:2])
         for j in (0, 1):
-            ACT("sl wc", "wi", T.wi[:, j::2], T.sl[:, j::2], scale=T.wc[:, j:j + 1])
+            ACT("sl wc", "wi", T.wi[:, 2 * j:2 * j + 2], T.sl[:, 2 * j:2 * j + 2], scale=T.wc[:, j:j + 1])
+        MS("srow", T.srow[0:32, :], 2.0 ** -124)
+        for t in (0, 1):
+            MS("srow", T.srow[0:32, 64 * t + 32:64 * t + 64], 2.0 ** -116)
 
-    def m_src(r, l):
-        if r and l == home(r - 1):
-            return piece(T, "M", 1, r - 1, l, 1), "Mo%d" % (r - 1)
-        return piece(T, "M", 0, r, l, 1), "M%d.%d" % (r, l)
+    def m_gather(q, r, l):
+        b, k = at("M", r, l)
+        COPY(q, XX + " " + k, "G.%d ~g%s" % (l, q), tile(T.G, l, 1024), T.X[:].indirect(b), 1)
 
-    def m_gather(r, l):
-        b, k = m_src(r, l)
-        ACT(XX + " " + k, "G.%d" % l, tile(T.G, l, 1024), T.X[:].indirect(b))
+    def m_float(r):
+        far = 2 * (1 - home(r - 1) // 2) if r else 2
+        for l, n in ([(far, 2), (far ^ 2, 1), (far ^ 3, 1)] if r else [(0, 2), (2, 2)]):
+            if n == 1:
+                b, k = at("M", r, l)
+            else:
+                b, k = piece(T, "M", 0, r, l, 2), "M%d.%d M%d.%d" % (r, l, r, l + 1)
+            CP(k, " ".join("Mf.%d" % j for j in range(l, l + n)), T.Mf[:, 64 * l:64 * (l + n)], b)
 
-    def m_float(r, l):
-        b, k = m_src(r, l)
-        CP(k, "Mf.%d" % l, tile(T.Mf, l, 64), b)
+    def key_init():
+        MM("irow ma", "BM", T.BM[:, 0:32, :], T.irow[0:1, :], T.ma[0:1, :, :], True, False)
+        MM("one mb", "BM", T.BM[:, 0:32, :], T.one[0:1, :], T.mb[0:1, :, :], False, False)
+        MM("irw xa", "BX", T.BX[:], T.irw[0:1, :], T.xa[0:1, :, :], True, False)
+        MM("one xb", "BX", T.BX[:], T.one[0:1, :], T.xb[0:1, :, :], False, False)
 
-    def key_init(B, a, b):
-        MM("irow irow16 xa", B, T[B][:, :, 0:9], T[a][0:1, :], T.xa[0:1, :, 0:9], True, False)
-        MM("one " + b, B, T[B][:, :, 0:9], T.one[0:1, :], T[b][0:1, :, 0:9], False, False)
+    DB = ("DA", "DB", "DC")
 
-    def key_out(B, t, k):
-        return T[B][:, 16 * t + k // 8:16 * t + 16:2, k % 8:9:8 - k % 8]
-
-    DB = ("D0", "BK", "D1")
-
-    def m_delta(r, t, c, D):
-        rk = "I nI G.%d G.%d " % (2 * t, 2 * t + 1) + lanes("z%d" % r, (2 * t, 2 * t + 1))
+    def m_chunk(r, t, c, D, last):
+        zs = zparts(r, t)
+        rk = "I nI G.%d G.%d " % (2 * t, 2 * t + 1) + " ".join(x[3] for x in zs)
         for j in range(4):
             k = 4 * c + j
-            MM(rk, D, tile(T[D], j), T.I[:], T.G[:, 2048 * t + k:2048 * t + 2048:16], True, False)
-            MM(rk, D, tile(T[D], j), T.nI[:], piece(T, "z", 0, r, 2 * t, 2), False, True)
-
-    def m_abs(t, c, D):
+            MM(rk, D, T[D][:, 4 * j:4 * j + 4, :], T.I[:], T.G[:, 2048 * t + k:2048 * t + 2048:16], True, False)
+            for l, n, z, zk in zs:
+                o = 4 * j + 2 * (l % 2)
+                MM(rk, D, T[D][:, o:o + 2 * n, :], T.nI[:], z, False, l + n == 2 * t + 2)
         o = 4096 * t + 2048 + 512 * c
         ACT(D, "W.m%d%d" % (t, c), T.W[:, o:o + 512], T[D][:], F.Abs, scale=2.0)
-
-    def m_keys(t, c, last):
         for j in range(4):
             k = 4 * c + j
-            o = 4096 * t + 2048 + 128 * k
-            MM("Rx W.m%d%d" % (t, c), "BM", key_out("BM", t, k), T.W[:, o:o + 128], T.Rx[:, 48:64], False, last and j == 3)
+            MM("Rm W.m%d%d" % (t, c), "BM", T.BM[:, 16 * t + k // 8:16 * t + 16:2, k % 8:9:8 - k % 8], tile(T.W, o // 128 + j), T.Rx[:, 96:112], False, last and j == 3)
 
-    def m_chunks(r, todo, last, hooks):
-        n = len(todo)
-        for i in range(-3, n):
-            if i in hooks:
-                hooks[i]()
-            if i >= 0:
-                m_abs(todo[i][0], todo[i][1], DB[i % 3])
-            if i + 3 < n:
-                m_delta(r, todo[i + 3][0], todo[i + 3][1], DB[i % 3])
-            if i >= 0:
-                m_keys(todo[i][0], todo[i][1], last and i == n - 1)
+    def zr(l):
+        return " ".join("ZR.%d.%d" % (l, k) for k in range(16))
 
-    def z_rep(r, t, ng=0):
-        z = piece(T, "z", 0, r, 2 * t, 2)
-        rk = lanes("z%d" % r, (2 * t, 2 * t + 1))
+    def z_rep(part, qs):
+        l, n, z, zk = part
         for k in range(16):
-            out = T.ZR[:, 4096 * t + k:4096 * t + 2048:16]
-            if k < ng:
-                SEL(rk, "ZR.%d.%d" % (t, k), out, z, [[0, 128]], A.is_ge, 0, 0)
-            elif k >= 16 - CFG["zs"]:
-                ACT(rk, "ZR.%d.%d" % (t, k), out, z)
-            else:
-                CP(rk, "ZR.%d.%d" % (t, k), out, z)
+            COPY(qs[k], zk, " ".join("ZR.%d.%d" % (j, k) for j in range(l, l + n)), T.ZR[:, 1024 * l + k:1024 * (l + n):16], z)
 
-    def kc(r, t):
-        CP("K " + lanes("c%d" % r, (2 * t, 2 * t + 1)), "kcu%d" % t, tile(T.kcu, t), T.K[:].indirect(piece(T, "c", 0, r, 2 * t, 2)))
+    def z_window(t):
+        COPY("C", " ".join(zr(l) for l in range(N)), "Zs.%d Zs.%d" % (2 * t, 2 * t + 1), T.Zs[:, 256 * t:256 * t + 128], T.ZR[:, 2048 * t:2048 * t + 2048:16])
 
-    def kc2(r):
-        CP("kcu0 kcu1", "kcf", T.kcf[:], T.kcu[:])
-        TS(lanes("c%d" % r), "c2a", s["c2a"], piece(T, "c", 0, r), 2.0, A.mult)
-        ts("c2", "c2a", 511, A.bitwise_and)
+    def kwin(r):
+        return T.K if r else T.Ki
 
-    def x_gather(t):
-        zr = " ".join("ZR.%d.%d" % (t, k) for k in range(16))
-        TT(XX + " kcu%d " % t + zr, "W.x%d" % t, T.W[:, 4096 * t:4096 * t + 2048], T.X[:].indirect(tile(T.kcu, t)), tile(T.ZR, 2 * t, 2048), A.subtract)
+    def kc(r, l):
+        b, k = at("c", r, l)
+        CP("K " + k, "kcu%d" % l, tile(T.kcu, l, 64), kwin(r)[:].indirect(b), 1)
 
-    def x_relu(t, n=0, ab=False):
-        if ab:
-            ACT("W.x%d" % t, "R.%d" % t, tile(T.R, t, 2048), T.W[:, 4096 * t:4096 * t + 2048], F.Abs)
-        elif n:
-            ACT("W.x%d" % t, "R.s%d" % t, T.R[:, 2048 * t:2048 * t + n], T.W[:, 4096 * t:4096 * t + n], F.Relu)
-            TS("W.x%d" % t, "R.%d" % t, T.R[:, 2048 * t + n:2048 * t + 2048], T.W[:, 4096 * t + n:4096 * t + 2048], 0.0, A.max)
-        else:
-            TS("W.x%d" % t, "R.%d" % t, tile(T.R, t, 2048), T.W[:, 4096 * t:4096 * t + 2048], 0.0, A.max)
+    def kc_tile(r, t):
+        CP("K c%d.%d c%d.%d" % (r, 2 * t, r, 2 * t + 1), "kcu%d kcu%d" % (2 * t, 2 * t + 1), tile(T.kcu, t), kwin(r)[:].indirect(piece(T, "c", 0, r, 2 * t, 2)), 1)
 
-    def x_keys(t, part, last, ab=False):
-        j = 2 if ab else part
+    def x_lane(l):
+        o = 4096 * (l // 2) + 1024 * (l % 2)
+        TT(XX + " kcu%d " % l + zr(l), "W.x%d ~x" % l, T.W[:, o:o + 1024], T.X[:].indirect(tile(T.kcu, l, 64)), tile(T.ZR, l, 1024), A.subtract, 1)
+
+    def x_keys(t, src, rk, j, last):
         for k in range(16):
-            src = T.W[:, 4096 * t + k:4096 * t + 2048:16] if part == 0 else T.R[:, 2048 * t + k:2048 * t + 2048:16]
-            MM("Rx " + ("W.x%d" % t if part == 0 else "R.%d R.s%d" % (t, t)), "BX", key_out("BX", t, k), src, tile(T.Rx, j, 16), False, last and k == 15)
+            MM(rk, "BX", T.BX[:, 8 * t:8 * t + 8, k:17:16 - k], src[:, k:2048:16], tile(T.Rx, 2 * j + k // 8, 16), False, last and k == 15)
+
+    def x_tile(t, ns, last):
+        w, rl = T.W[:, 4096 * t:4096 * t + 2048], tile(T.R, t, 2048)
+        x_keys(t, w, "Rx1 W.x%d W.x%d" % (2 * t, 2 * t + 1), 1, False)
+        for l in (0, 1):
+            a, b = 1024 * l, 1024 * l + 1024
+            m = min(max(ns - a, 0), 1024) + a
+            if m > a:
+                ACT("W.x%d" % (2 * t + l), "R.s%d" % (2 * t + l), rl[:, a:m], w[:, a:m], F.Relu)
+            if m < b:
+                TS("W.x%d" % (2 * t + l), "R.%d" % (2 * t + l), rl[:, m:b], w[:, m:b], 0.0, A.max)
+        x_keys(t, rl, "Rx2 " + " ".join("R.%d R.s%d" % (l, l) for l in (2 * t, 2 * t + 1)), 2, last)
 
     MF = "Mf.0 Mf.1 Mf.2 Mf.3"
 
-    def m_copy():
-        ACT("BM", "tt", T.tt[:], T.BM[:, :, 8])
-        ACT("BM", "kms", T.kms[:], T.BM[:, :, 0:8], F.Identity, bias=-4096 * U)
+    def clanes(r):
+        return " ".join("c%d.%d" % (r, l) for l in range(N))
 
-    def m_side(r):
-        TT("tt", "df", s["df"], T.tt[:, 1::2], T.tt[:, 0::2], A.subtract)
-        TT("tt", "ts", s["ts"], T.tt[:, 0::2], T.tt[:, 1::2], A.add)
-        o = "nf" if r else "thr"
-        ACT("df", o, s[o], s["df"], F.Abs)
-        ts("ts2", "ts", -7.5 * SU, A.add, 3072.0, A.add)
-        if r:
-            tt("thr", "nf", "a8", A.add)
-        SCAN("kms r16", "msn", T.msn[:], T.r16[:], T.kms[:], A.add, A.min)
-        ACT("ts2", "tT", s["tT"], s["ts2"], F.Identity, bias=-3071.0)
-        ts("nthr", "thr", SU, A.max, -1.0, A.mult)
-        ACT("msn", "ek", s["ek"], T.msn[:, 15::16], F.Identity, bias=4096 * U)
+    def add_u(r, t, bank, o):
+        for l, n, z, zk in zparts(r, t):
+            MM("Wu " + zk, bank, o[64 * (l % 2):64 * (l % 2 + n), :], z, T.Wu[:], False, False)
 
-    def m_values(r):
-        zl = lanes("z%d" % r)
+    def early(r):
+        CP("kcu0 kcu1 kcu2 kcu3", "kcf", T.kcf[:], T.kcu[:])
+        TS(clanes(r), "c2a", s["c2a"], piece(T, "c", 0, r), 2.0, A.mult)
+        ts("c2", "c2a", 511, A.bitwise_and)
+        TS("c2", "c2h", T.c2h[:], s["c2"], 512.0, A.add)
         for t in (0, 1):
             o = tile(T.BB, t)
             MM("kcf If", "BB", o, tile(T.kcf, t), T.If[:], True, False)
-            MM("Wu " + zl, "BB", o, piece(T, "z", 0, r, 2 * t, 2), T.Wu[:], False, False)
+            add_u(r, t, "BB", o)
             MM("onef vrow", "BB", o, T.onef[0:1, :], T.vrow[0:1, :], False, True)
-        ACT("BB", "ry", T.ry[:], T.BB[:, 0:256], F.Identity, bias=1.5 * 2.0 ** 34)
-        ACT("ry", "rr", T.rr[:], T.ry[:], F.Identity, bias=-1.5 * 2.0 ** 34)
+        C = 1.5 * 2.0 ** 34
+        if CFG["rr"] == "S":
+            ACT("BB", "ry", T.ry[:], T.BB[:, 0:256], F.Identity, bias=C)
+            ACT("ry", "rr", T.rr[:], T.ry[:], F.Identity, bias=-C)
+        else:
+            TS("BB", "rr", T.rr[:], T.BB[:, 0:256], C, A.add, -C, A.add)
         for t in (0, 1):
             o = tile(T.BA, t)
             MM("kcf If", "BA", o, tile(T.kcf, t), T.If[:], True, False)
@@ -522,106 +572,116 @@ def rank_program(g, core, T, topo):
             o = tile(T.BA, 2 + t)
             MM("kcf If", "BA", o, tile(T.kcf, t), T.If[:], True, False)
             MM("nIf " + MF, "BA", o, tile(T.Mf, t), T.nIf[:], False, False)
-            MM("Wu " + zl, "BA", o, piece(T, "z", 0, r, 2 * t, 2), T.Wu[:], False, False)
+            add_u(r, t, "BA", o)
             MM("onef drow", "BA", o, T.onef[0:1, :], T.drow[0:1, :], False, False)
             MM("nI rr", "BA", o, T.nI[:], tile(T.rr, t), False, True)
+        MM("hIf " + MF, "BB", T.BB[:, 256:512], T.hIf[:], T.Mf[:], True, False)
+        MM("hIf kcf", "BB", T.BB[:, 256:512], T.hIf[:], T.kcf[:], False, False)
 
-    WALL = "W.x0 W.x1 " + " ".join("W.m%d%d" % (t, c) for t in (0, 1) for c in range(4))
+    def onehots(r):
+        c = piece(T, "c", 0, r)
+        for j, wn in enumerate(("E2", "H0", "H1")):
+            ACT(clanes(r) + " " + wn, "oh%d" % j, tile(T.oh, j, 256), T[wn][:].indirect(c), F.Copy, 1)
+        for t in (0, 1):
+            MM("oh0 Ip", "DB", T.DB[:, :, 8 * t:8 * t + 8], tile(T.oh, t), T.Ip[:], True, True)
+        ACT("DB", "Lc", T.Lc[:], T.DB[:, :, 0:16])
+        for hh in (0, 1):
+            for t in (0, 1):
+                MM("I oh%d" % (hh + 1), "DA", T.DA[:, 8 * t:8 * t + 8, 16 * hh:16 * hh + 16], tile(T.oh, 2 + 2 * hh + t), T.I[:], True, True)
+        for t in (0, 1):
+            ACT("DA wc", "Hs%d" % t, T.Hs[:, 8 * t:8 * t + 8, 0:32], T.DA[:, 8 * t:8 * t + 8, :], scale=tile(T.wc, (r + t) // 2, 1))
+            ACT("DA wi", "Hu%d" % t, T.Hs[:, 8 * t:8 * t + 8, 32:64], T.DA[:, 8 * t:8 * t + 8, :], scale=tile(T.wi, r + t, 1))
+        MM("one srow", "DC", T.DC[:, 0:4, :], T.one[0:1, :], T.srow[0:1, :], True, False)
 
-    def choose():
-        ACT("BX", "kxs", T.kxs[:], T.BX[:, :, 0:9])
-        TT("kxs", "sd", s["sd"], T.kxs[:, 17::18], T.kxs[:, 8::18], A.subtract)
+    TL, AL, A8 = T.BM[:, 32:48, 0], T.BM[:, 32:48, 1], T.BM[:, 32:48, 2]
+
+    def m_side(r):
+        ACT("BM", "tt", T.tt[:], T.BM[:, 0:32, 8])
+        ACT("BM", "kms", T.kms[:], T.BM[:, 0:32, 0:8], F.Identity, bias=-4096.0)
+        TT("tt", "df", s["df"], T.tt[:, 1::2], T.tt[:, 0::2], A.subtract)
+        TT("tt", "ts", s["ts"], T.tt[:, 0::2], T.tt[:, 1::2], A.add)
+        o = "nf" if r else "thr"
+        ACT("df", o, s[o], s["df"], F.Abs, scale=B / 256)
+        if r:
+            TT("nf BM", "thr", s["thr"], s["nf"], A8, A.add)
+        ts("thq", "thr", B, A.max)
+        ts("tT", "ts", 1.5 * 2.0 ** 35, A.add, -1.5 * 2.0 ** 35, A.add)
+        SCAN("kms r16", "msn", T.msn[:], T.r16[:], T.kms[:], A.add, A.min)
+        for h in (0, 1):
+            ACT("msn", "ek%d" % h, T.ek[:, h::2], T.msn[:, 15::16], F.Identity, bias=4096.0)
+
+    WALL = "W.x0 W.x1 W.x2 W.x3 " + " ".join("W.m%d%d" % (t, c) for t in (0, 1) for c in range(4))
+
+    def choose(r):
+        xm = T.xs[:, 7::8]
+        ACT("BX", "kxs", T.kxs[:], T.BX[:, :, 0:16])
         SCAN("kxs r8", "xs", T.xs[:], T.r8[:], T.kxs[:], A.add, A.min)
-        TT("sd thr", "bad0", T.bad[:, 0::2], s["sd"], s["thr"], A.is_lt)
-        TT("sd nthr", "bad1", T.bad[:, 1::2], s["sd"], s["nthr"], A.is_gt)
-        TT("xs bad0 bad1", "cand", T.cand[:], T.xs[:, 7::9], T.bad[:], A.max)
-        TT("bad0 bad1", "nt", s["nt"], T.bad[:, 0::2], T.bad[:, 1::2], A.min)
+        TT("BX thr", "q0", T.q[:, 0::2], s["thr"], T.BX[:, :, 16], A.subtract)
+        TT("BX thq", "q1", T.q[:, 1::2], s["thq"], T.BX[:, :, 16], A.add)
+        TT("xs q0 q1", "cand", T.cand[:], xm, T.q[:], A.max)
         TT("cand", "m1", s["m1"], T.cand[:, 0::2], T.cand[:, 1::2], A.min)
-        tt("win", "m1", "ek", A.min)
-        ts("wi32", "win", 1 / U, A.mult)
-        TT("win ek", "hz", T.hz[:, 0::4], s["win"], s["ek"], A.is_equal)
-        ts("ix", "wi32", 4095, A.bitwise_and)
-        ACT("bad1", "hz2", T.hz[:, 2::4], T.bad[:, 1::2])
-        TT("ix b16 E", "ex", T.ex[:], s["ix"].indirect(T.b16[:]), T.E[:, 0:256], A.mult)
+        TT("m1 ek0", "win", s["win"], s["m1"], T.ek[:, 0::2], A.min)
+        ts("ix", "win", 4095, A.bitwise_and)
+        TT("ix b16 E", "ex", T.ex[:], s["ix"].indirect(T.b16[:]), T.E[:], A.mult, 1)
         MM("one crow", "BL", T.BL[:, 0:16], T.one[0:1, :], T.crow[0:1, :], True, False)
         for t in (0, 1):
             MM("ex sel8", "BL", tile(T.BL, t, 8), tile(T.ex, t), T.sel8[:], False, t == 1)
-
-    def pack(r):
-        TT("nt hz", "hz1", T.hz[:, 1::4], s["nt"], T.hz[:, 0::4], A.is_ge)
-        SCAN("kxs ra", "asn", T.asn[:], T.ra[:], T.kxs[:], A.add, A.max)
-        SCAN("hz hz1 hz2 hm", "hs", T.hs[:], T.hm[:], T.hz[:], A.mult, A.add)
-        TS("asn", "ai", s["ai"], T.asn[:, 16::18], 1 / U, A.mult)
-
-    EX2 = " ".join("ex2.%d" % j for j in range(16))
-
-    def pack2(r):
-        ts("a15", "ai", 15, A.bitwise_and)
-        TT("a15 hs", "P", s["P"], s["a15"], T.hs[:, 3::4], A.add)
-        if CFG["ex2"][r] == "V":
-            TT("P b16 E", EX2, T.ex2[:], s["P"].indirect(T.b16[:]), T.E[:, 0:256], A.mult)
-        else:
-            o = 16 * F16.index("P")
-            for j in range(16):
-                ACT("P E", "ex2.%d" % j, tile(T.ex2, j, 16), T.E[:, 0:16], scale=T.pf[:, o + j:o + j + 1])
-        for t in (0, 1):
-            MM(EX2 + " sel8", "BK", T.BK[:, 8 * t:8 + 8 * t], tile(T.ex2, t), T.sel8[:], True, True)
-        for t in (0, 1):
-            h = block(2 * t, r)
-            o = 16 + 4 * (h % 2)
-            for u in (0, 1):
-                MM(EX2 + " sel8", "BK", T.BK[:, o + 8 * u:o + 8 * u + 4], tile(T.ex2, t), tile(T.sel8, (u + h // 2) % 2, 4), True, True)
-        if r < RO - 1:
-            MM("one arow", "BK", T.BK[:, 32:48], T.one[0:1, :], T.arow[0:1, :], True, False)
-            for t in (0, 1):
-                for u in (0, 1):
-                    MM("aw hz1", "BK", T.BK[:, 32 + 8 * t:40 + 8 * t], T.aw[:], T.hz[:, 32 * u + 1:32 * u + 32:4], False, t + u == 2)
-
-    ZALL = "ZR.z " + " ".join("ZR.%d.%d" % (t, k) for t in (0, 1) for k in range(16))
-
-    def features(r, fill):
-        zo, k = piece(T, "z", 1, r), "zo%d" % r
         CP("BL", "il", T.il[:], T.BL[:, 0:16])
-        ACT(ZALL + " il", "g1", T.g1[:], T.ZR[:].indirect(T.il[:]), F.Identity, scale=2.0, bias=-0.5)
-        CP("BL", "li.a", T.li[:, 0:16], T.BL[:, 0:16])
-        TT("cand win", "Fw", T.Fw[:, 0::2], T.cand[:, 0::2], s["win"], A.not_equal)
-        TT("cand win", "Fw1", T.Fw[:, 1::2], T.cand[:, 1::2], s["win"], A.not_equal)
-        fill()
-        TT(WALL + " il g1", "sx", T.sx[:], T.W[:].indirect(T.il[:]), T.g1[:], A.add)
-        ACT("sx", "ry", T.ry[:], T.sx[:], F.Identity, bias=1.5 * 2.0 ** 24)
-        ACT("ry", k, zo, T.ry[:], F.Identity, scale=0.5, bias=-0.75 * 2.0 ** 24)
-        MM("Wu " + k, "BL", T.BL[:, 256:512], T.Wu[:], zo, True, False)
-        MM("I um", "BL", T.BL[:, 256:512], T.I[:], T.um[:], False, True)
+        TS("BL", "zl", T.zl[:], T.BL[:, 0:16], 1 / 16, A.mult, -0.47, A.add)
+        TS("BL", "el", T.el[:], T.BL[:, 0:16], 1 / 128, A.mult, -0.496, A.add)
+        if r < RO - 1:
+            CP("BL", "li", s["li"], T.BL[:, 0:16])
+        TT("q0 q1 ek0 ek1", "qe", T.qe[:], T.q[:], T.ek[:], A.max)
+        TT("xs qe", "f", T.f[:], xm, T.qe[:], A.is_gt)
+        TT("cand ek0 ek1", "nk", T.nk[:], T.cand[:], T.ek[:], A.is_gt)
+        SCAN("kxs ra", "asn", T.asn[:], T.ra[:], T.kxs[:], A.add, A.max)
+
+    def features(r):
+        zo, k = piece(T, "z", 1, r), "zo%d" % r
+        TS(WALL + " il", "hh", T.hh[:], T.W[:].indirect(T.il[:]), -0.5, A.add, 0.5, A.mult, 1)
+        TT("Zs Zs.0 Zs.1 Zs.2 Zs.3 zl hh", k, zo, T.Zs[:].indirect(T.zl[:]), T.hh[:], A.add, 1)
+        for j in range(16):
+            MM("Wz " + k, "BL", T.BL[:, 16:32], T.Wz[:, 15 - j:143 - j], zo[:, j::16], j == 0, j == 15)
         if r == RO - 1:
             for l in range(N):
                 dma("Y", tile(T.yz, block(l, r), 64), piece(T, "z", 1, r, l, 1), k, "")
         else:
             send("z", r + 1, k)
-            l = home(r)
-            ACT(k, "z%d.%d" % (r + 1, l), piece(T, "z", 0, r + 1, l, 1), piece(T, "z", 1, r, l, 1))
+        CP("BL", "ui", s["ui"], T.BL[:, 16:32])
+        ts("uq", "ui", 7, A.bitwise_and)
+        TT("uq o8", "ow", s["ow"], s["uq"], tile(T.o8, r, 16), A.add)
+        CP("ow", "ol", T.ol[:], s["ow"])
 
-    def survivors(part):
-        if part == 0:
-            tt("Tt", "tT", "nt", A.subtract)
-            ACT("BX", "nkx", T.nkx[:], T.BX[:, :, 0:8], scale=-1.0)
-            ACT("Tt b16", "tbc", T.tbc[:], s["Tt"].indirect(T.b16[:]), F.Identity, bias=4096 * U)
-            MM("nIq kms", "D0", T.D0[:, 0:256], T.nIq[:], T.kms[:], True, False)
-            TT("BM tbc", "c2b", T.c2b[:], T.BM[:, :, 0:8], T.tbc[:], A.is_ge)
-            TT("c2b BA", "p2", T.p2[:], T.BA[:, 256:512], T.c2b[:], A.mult)
-        else:
-            for k in range(8):
-                MM("I Fw Fw1", "D0", T.D0[:, k:256:8], T.I[:], T.Fw[:], False, k == 7)
-            TT("D0 nkx", "ltb", T.ltb[:], T.D0[:, 0:256], T.nkx[:], A.is_lt)
-            TT("ltb BA", "p1m", T.p1m[:], T.BA[:, 0:256], T.ltb[:], A.mult)
+    def taxa(r):
+        k = "zo%d" % r
+        if r < RO - 1:
+            TT(XX + " ol " + k, "si", T.si[:], T.X[:].indirect(T.ol[:]), piece(T, "z", 1, r), A.add, 1)
+            TS("si", "sh", T.sh[:], T.si[:], 1, A.arith_shift_right)
+            CP("sh ol", XX, T.X[:].indirect(T.ol[:]), T.sh[:], 2.4)
+            return
+        for l in range(N):
+            h = block(l, r)
+            win = tile(T.X, h, 512).indirect(tile(T.ol, l, 4))
+            TT("X.%d ol %s" % (h, k), "si%d" % l, tile(T.si, l, 64), win, piece(T, "z", 1, r, l, 1), A.add, 1)
+            TS("si%d" % l, "sh%d" % l, tile(T.sh, l, 64), tile(T.si, l, 64), 1, A.arith_shift_right)
+            CP("sh%d ol" % l, "X.%d" % h, win, tile(T.sh, l, 64), 2.4)
+            dma("Y", tile(T.ytx, h, 512), tile(T.X, h, 512), "X.%d" % h, "")
 
-    def survivors_sum():
+    def survivors(r):
+        ACT("m1", "tr", s["tr"], s["m1"], F.Identity, scale=-512.0, bias=512 * B)
+        tt("Tt", "tT", "tr", A.max)
+        TT("Tt b16 kms", "mk1", T.mk[:, 256:512], s["Tt"].indirect(T.b16[:]), T.kms[:], A.is_le, 1)
+        TT("mk1 BA", "p2", T.pp[:, 256:512], T.BA[:, 256:512], T.mk[:, 256:512], A.mult)
+        MM("nIq kms", "DB", T.DB[:, :, 16:32], T.nIq[:], T.kms[:], True, False)
+        MM("Iq kxs", "DB", T.DB[:, :, 16:32], T.Iq[:], T.kxs[:], False, False)
+        for k in range(8):
+            MM("BI nk", "DB", T.DB[:, :, 16 + k:32:8], T.BI[:], T.nk[:], False, k == 7)
+        ACT("DB", "mk0", T.mk[:, 0:256], T.DB[:, :, 16:32], F.Sign, scale=-1.0)
+        TT("mk0 BA", "p1", T.pp[:, 0:256], T.BA[:, 0:256], T.mk[:, 0:256], A.mult)
         for t in (0, 1):
-            o = tile(T.BB, 2 + t)
-            MM("If " + MF, "BB", o, T.If[:], tile(T.Mf, t), True, False)
-            MM("If p1m", "BB", o, tile(T.p1m, t), T.If[:], False, False)
-            MM("If p2", "BB", o, tile(T.p2, t), T.If[:], False, True)
-
-    def survivors_out(r):
+            MM("If p2", "BB", tile(T.BB, 2 + t), tile(T.pp, 2 + t), T.If[:], False, False)
+        for t in (0, 1):
+            MM("hIf p1", "BB", tile(T.BB, 2 + t), tile(T.pp, t), T.hIf[:], False, t == 1)
         if r == RO - 1:
             ACT("BB", "Mof", T.Mof[:], T.BB[:, 256:512])
             for l in range(N):
@@ -630,206 +690,115 @@ def rank_program(g, core, T, topo):
             CP("BB", "Mo%d" % r, piece(T, "M", 1, r), T.BB[:, 256:512])
             send("M", r + 1, "Mo%d" % r)
 
-    def lists(r):
-        CP("BK", "li.b", T.li[:, 16:48], T.BK[:, 0:32])
-        if r < RO - 1:
-            ACT("BK", "a8", s["a8"], T.BK[:, 32:48])
-        SCAN("BL ru", "us", T.us[:], T.ru[:], T.BL[:, 256:512], A.add, A.max)
-        TS("li.b", "vv", s["vv"], T.li[:, 16:32], 4, A.arith_shift_right, 1023, A.bitwise_and)
-        CP("us", "ui", s["ui"], T.us[:, 15::16])
-        tt("tA", "vv", "c2", A.add)
-        ts("uq", "ui", 7, A.bitwise_and)
-        TS("tA", "tl", T.tl[:], s["tA"], 512.0, A.min)
-        TT("uq o8", "ow", s["ow"], s["uq"], tile(T.o8, r, 16), A.add)
-
-    def own_list():
-        CP("ow", "ol", T.ol[:], s["ow"])
-
-    def names():
-        TS("li.a", "l4.a", T.l4[:, 0:16], T.li[:, 0:16], 7, A.arith_shift_right, 15, A.bitwise_and)
-        TS("li.b", "l4.b", T.l4[:, 16:32], T.li[:, 32:48], 15, A.bitwise_and)
-        CP("l4.a l4.b", "el", T.el[:], T.l4[:])
-        TT("E el " + MF, "EM", T.EM[:], T.E[:, 0:16].indirect(T.el[:, 0:16]), T.Mf[:], A.mult)
-
-    def taxa(r):
-        TT(XX + " ol zo%d" % r, "si", T.si[:], T.X[:].indirect(T.ol[:]), piece(T, "z", 1, r), A.add)
-        TS("si", "sh", T.sh[:], T.si[:], 1, A.arith_shift_right)
-        CP("sh ol", XX, T.X[:].indirect(T.ol[:]), T.sh[:])
-        if r == RO - 1:
-            dma("Y", T.ytx[:, 0:1024], T.X[:, 0:1024], XX, "")
-            dma("C", T.ytx[:, 1024:2048], T.X[:, 1024:2048], XX, "")
-
     def couplet_numbers(r):
-        tt("tB", "c2", "vv", A.subtract)
+        ts("lb", "li", 3, A.arith_shift_right, 1, A.bitwise_and)
+        ts("im", "li", 1, A.arith_shift_right, 1024, A.bitwise_and)
+        TT("lb c2h", "tA", s["tA"], s["lb"], T.c2h[:], A.add)
+        tt("A1", "tA", "im", A.subtract)
         ts("u9", "ui", 511, A.bitwise_and)
-        ts("tB", "tB", 513.0, A.add)
-        TS("li.b", "im", s["im"], T.li[:, 16:32], 14, A.arith_shift_right)
-        tt("tC", "u9", "tB", A.subtract)
-        tt("tC", "tC", "im", A.mult)
-        tt("tD", "tC", "tB", A.add)
-        CP("tD", "co%d" % r, piece(T, "c", 1, r), s["tD"])
+        tt("cn", "u9", "A1", A.max)
+        ts("c2a", "cn", 511, A.bitwise_and)
+        CP("c2a", "co%d" % r, piece(T, "c", 1, r), s["c2a"])
         send("c", r + 1, "co%d" % r)
         l = home(r)
         dma("Y", piece(T, "c", 0, r + 1, l, 1), piece(T, "c", 1, r, l, 1), "co%d" % r, "c%d.%d" % (r + 1, l))
 
-    def k_onehot(qs):
-        for j, wn in enumerate(("E", "H0", "H1")):
-            if qs[j] == "S":
-                ACT("tl " + wn, "oh%d" % j, tile(T.oh, j, 256), T[wn][:].indirect(T.tl[:]))
-            else:
-                CP("tl " + wn, "oh%d" % j, tile(T.oh, j, 256), T[wn][:].indirect(T.tl[:]))
-        for t in (0, 1):
-            MM("oh0 I", "BA", tile(T.BA, 2 + t), tile(T.oh, t), T.I[:], True, True)
-        for t in (0, 1):
-            for a in (0, 1):
-                for hh in (0, 1):
-                    MM("I oh%d" % (hh + 1), "BK", tile(T.BK, 4 * t + 2 * a + hh, 64), tile(T.oh, 2 + 2 * hh + t), tile(T.I, a, 64), True, True)
-
-    def k_old():
-        ACT("K tl", "Kt", T.Kt[:], T.K[:].indirect(T.tl[:]))
-
     def k_table(r):
+        TT("f b2 Lc", "Z", T.Z[:, 1792:2048], T.f[:].indirect(T.b2[:]), T.Lc[:], A.mult, 1)
         for t in (0, 1):
-            ACT("BA wc", "L1", tile(T.L1, t), tile(T.BA, 2 + t), scale=tile(T.wc, (r + t) % 2, 1))
-            ACT("BA wi", "L2", tile(T.L2, t), tile(T.BA, 2 + t), scale=tile(T.wi, r + t, 1))
-        ACT("BK", "Oh", T.Oh[:], T.BK[:])
-        MM("one srow", "D1", T.D1[:], T.one[0:1, :], T.srow[0:1, :], True, False)
-        parts = [(l // 2, 64 * (l % 2), 64, block(l, r) // 2) for l in range(N)]
-        todo = [(p, a, u) for p in parts[0::2] + parts[1::2] for a in (0, 1) for u in (0, 1)]
-        for i, ((t, p0, n, hi), a, u) in enumerate(todo):
-            o = 256 * u + 128 * hi
-            L = T["L%d" % (u + 1)]
-            MM("L1 L2 Oh", "D1", T.D1[64 * a:64 * a + 64, o:o + 128], L[p0:p0 + n, 128 * t + 64 * a:128 * t + 64 * a + 64],
-               T.Oh[p0:p0 + n, 256 * t + 128 * a:256 * t + 128 * a + 128], False, i in (len(todo) - 3, len(todo) - 1), i == len(todo) // 2)
+            for j in range(8):
+                o = 1792 + 8 * t + j - 256 * j
+                MM("Z Z.0 Z.1 Z.2 Z.3 Hs%d Hu%d" % (t, t), "DC", T.DC[:, 2 * t:2 * t + 2, :], T.Z[:, o:o + 2033:16],
+                   T.Hs[:, 8 * t + j, :], False, t == 1 and j == 7)
+        op("V", "DC", "rc", lambda: v.reciprocal(T.rc[:], T.DC[:, 0:4:2, :]), (230 + 6 * 64) * CY)
+        TT("rc DC", "ra2", T.ra2[:], T.rc[:], T.DC[:, 1:4:2, :], A.mult)
+        TT("ra2", "om", T.om[:], T.ra2[:, 0:32], T.ra2[:, 32:64], A.min)
+        TS("om", "wl", T.wl[:], T.om[:], -0.3, A.add)
 
     def k_delta(r):
+        if r < RO - 1:
+            for t in (0, 1):
+                for u in range(4):
+                    MM("aw f", "BM", T.BM[:, 32 + 8 * t:40 + 8 * t, 2], T.aw[:], T.f[:, 16 * (u // 2) + u % 2:16 * (u // 2) + 16:2], u == 0, u == 3)
+        CP("asn", "ai", s["ai"], T.asn[:, 15::16])
+        ts("a15", "ai", 15, A.bitwise_and)
+        ACT("f", "f16", s["f16"], T.f[:, 0::2], scale=16.0)
+        tt("P", "a15", "f16", A.add)
+        EX2 = " ".join("ex2.%d" % j for j in range(16))
+        if CFG["ex2"][r] == "V":
+            TT("P b16 E", EX2, T.ex2[:], s["P"].indirect(T.b16[:]), T.E[:], A.mult, 1)
+        else:
+            for j in range(16):
+                ACT("P E", "ex2.%d" % j, tile(T.ex2, j, 16), T.E[:, 0:16], scale=s["P"][:, j:j + 1])
+        MM("If c2h", "BM", TL, T.If[:], T.c2h[:], True, False)
+        for t in (0, 1):
+            MM(EX2 + " s16", "BM", T.BM[:, 32 + 8 * t:40 + 8 * t, 0], tile(T.ex2, t), T.s16[:], False, t == 1)
+        for l in range(N):
+            o = 32 + 4 * block(l, r)
+            MM(EX2 + " sel", "BM", T.BM[:, o:o + 4, 1], tile(T.ex2, l // 2), tile(T.sel, l % 2, 4), True, True)
+        TS("BM", "tl", T.tl[:], TL, -512.47, A.add)
+        CP("BM", "al", T.al[:], AL)
+        if r:
+            ACT("K tl", "Kt", T.Kt[:], T.K[:].indirect(T.tl[:]), F.Copy, 1)
+        else:
+            CP("K tl", "Kt", T.Kt[:], T.Ki[:].indirect(T.tl[:]), 1)
+        ACT("E al", "oa", T.oa[:], T.E[:].indirect(T.al[:]), F.Copy, 1)
+        TT("E el " + MF, "EM", T.EM[:], T.E[:].indirect(T.el[:]), T.Mf[:], A.mult, 1)
         for l in range(N):
             o = tile(T.BA, block(l, r), 64)
             MM("BOf EM nIq Kt", "BA", o, T.BOf[:], tile(T.EM, l, 64), True, False)
             MM("BOf EM nIq Kt", "BA", o, T.nIq[:], tile(T.Kt, l, 64), False, True)
-
-    def k_read():
-        ACT("D1", "tb", T.tb[:], T.D1[:])
-        ACT("tb dl", "tg", T.tg[:], T.tb[:].indirect(T.dl[:]))
-        ACT("EA el", "oa", T.oa[:], T.EA[:].indirect(T.el[:, 16:32]))
+        TT("BA oa", "Wd", T.Wd[:, 0:256], T.BA[:, 0:256], T.oa[:], A.mult)
 
     def k_write(r):
-        op("V", "tg", "rc", lambda: v.reciprocal(T.rc[:], T.tg[:, 0:64]), "plain", 230 + 6 * 64)
-        TT("BA oa", "Wd", T.Wd[:, 0:256], T.BA[:, 0:256], T.oa[:], A.mult)
-        TT("rc tg", "ra2", T.ra2[:], T.rc[:], T.tg[:, 64:128], A.mult)
-        TT("ra2", "om", T.om[:], T.ra2[:, 0:32], T.ra2[:, 32:64], A.min)
-        TS("om", "oi oi2 oi3", T.oi[:], T.om[:], -0.3, A.add)
-        CP("oi", "wl", T.wl[:], T.oi[:])
         if r < RO - 1:
-            TT("Wd Wd1 wl K", "K", T.K[:, 0:512], T.Wd[:].indirect(T.wl[:]), T.K[:, 0:512], A.add)
+            TT("Wd Wd1 wl K", "K", T.K[:], T.Wd[:].indirect(T.wl[:]), kwin(r)[:], A.add, 1)
         else:
-            for h, b in enumerate(("ex", "sx")):
-                TT("Wd Wd1 wl K", b, T[b][:], T.Wd[:].indirect(tile(T.wl, h, 16)), tile(T.K, h, 256), A.add)
-                dma("YS"[h], tile(T.ykt, h, 256), T[b][:], b, "")
+            for h in (0, 1):
+                TT("Wd Wd1 wl K", "Ka%d" % h, tile(T.Ka, h, 256), T.Wd[:].indirect(tile(T.wl, h, 16)), tile(T.K, h, 256), A.add, 1)
+                dma("YS"[h], tile(T.ykt, h, 256), tile(T.Ka, h, 256), "Ka%d" % h, "")
 
-    def x_big(r, ta, both, lane):
-        hooks = {0: lambda: m_gather(r, lane), CFG["hv"]: lambda: (consts_scalar() if r == 0 else None, m_values(r))}
-        if not CFG["xabs"]:
-            if r == 0:
-                x_relu(ta)
-            hooks[CFG["h0"]] = lambda: x_keys(ta, 0, False)
-            hooks[CFG["h1"]] = lambda: x_keys(ta, 1, False)
-        m_chunks(r, both, True, hooks)
-        m_copy()
-        if CFG["xabs"]:
-            x_relu(ta, 0, True)
-            x_keys(ta, 1, False, True)
-
-    consts_first()
-    MS("K", T.K[:, 512:528], 0.0)
-    for l in range(N):
-        h = block(l, 0)
-        o = 16 * I16.index("ci") + 4 * h
-        CP("si", "M0.%d" % l, piece(T, "M", 0, 0, l, 1), tile(T.si, h, 64))
-        CP("ci", "c0.%d" % l, piece(T, "c", 0, 0, l, 1), T.pn[:, o:o + 4])
-    CP("Ki", "K", T.K[:, 0:512], T.Ki[:])
-    consts_iota()
+    consts()
     for r in range(RO):
         loc = home(r - 1) if r else 0
-        seq = [loc, loc ^ 1, loc ^ 2, loc ^ 3]
-        ta = loc // 2
-        tb = 1 - ta
-        both = [(t, c) for t in (ta, tb) for c in range(4)]
-        key_init("BM", "irow", "mb")
-        key_init("BX", "irw", "xb")
-        if r == 0:
-            z_rep(r, 0)
-            m_gather(r, 0)
-            m_gather(r, 1)
-            kc(r, 0)
-            x_gather(0)
-            m_gather(r, 2)
-            z_rep(r, 1)
-            kc(r, 1)
-            consts_later()
-            for l in range(N):
-                m_float(r, l)
-            kc2(r)
-            x_gather(1)
-            x_big(r, ta, both, 3)
+        ta, tb = loc // 2, 1 - loc // 2
+        sfx = "" if r else "0"
+        key_init()
+        for j, l in enumerate((loc, loc ^ 1, loc ^ 2, loc ^ 3)):
+            m_gather(CFG["mg" + sfx][j], r, l)
+        parts = sorted(zparts(r, ta), key=lambda x: x[0] != loc) + zparts(r, tb)
+        for part, qs in zip(parts, CFG["zr" + sfx]):
+            z_rep(part, qs)
+        for t in (0, 1):
+            z_window(t)
+        if r:
+            kc(r, loc)
+            kc(r, loc ^ 1)
         else:
-            m_gather(r, seq[0])
-            k_write(r - 1)
-            m_gather(r, seq[1])
-            z_rep(r, ta)
-            kc(r, ta)
-            x_gather(ta)
-            m_gather(r, seq[2])
-            z_rep(r, tb, CFG["zg"])
-            kc(r, tb)
-            for l in seq:
-                m_float(r, l)
-            kc2(r)
-            if not CFG["xabs"]:
-                x_relu(ta)
-            x_gather(tb)
-            x_big(r, ta, both, seq[3])
-        x_keys(tb, 0, False)
-        x_relu(tb, CFG["rs"])
-        x_keys(tb, 1, True)
+            kc_tile(r, ta)
+        kc_tile(r, tb)
+        m_float(r)
+        for i, (t, c) in enumerate([(t, c) for t in (ta, tb) for c in range(4)]):
+            m_chunk(r, t, c, DB[i % 3], i == 7)
+        for l in (loc, loc ^ 1, loc ^ 2, loc ^ 3):
+            x_lane(l)
+        for j, t in enumerate((ta, tb)):
+            x_tile(t, CFG["rs" + sfx][j], j == 1)
+        early(r)
         m_side(r)
-        choose()
-        features(r, lambda: pack(r))
-        pack2(r)
-        if r == 0:
-            consts_last()
+        onehots(r)
+        choose(r)
+        features(r)
+        survivors(r)
+        k_table(r)
+        k_delta(r)
         if r < RO - 1:
-            survivors(0)
-            survivors(1)
-            survivors_sum()
-            lists(r)
-            survivors_out(r)
-            own_list()
-            k_onehot(CFG["oh"])
             couplet_numbers(r)
-            names()
-            k_table(r)
-            k_old()
-            taxa(r)
-            k_delta(r)
-            k_read()
-        else:
-            survivors(0)
-            lists(r)
-            k_onehot(CFG["ohl"])
-            survivors(1)
-            survivors_sum()
-            own_list()
-            names()
-            k_table(r)
-            k_old()
-            survivors_out(r)
-            taxa(r)
-            k_delta(r)
-            k_read()
-    k_write(RO - 1)
-    PLAN["ops"] = [o[:3] + o[4:] for o in ops]
-    for i in issue_order(PLAN["ops"]):
+        taxa(r)
+        k_write(r)
+    if "order" not in PLAN:
+        PLAN["order"] = issue_order([o[:3] + o[4:] for o in ops])
+    for i in PLAN["order"]:
         ops[i][3]()
     final["sent"] = sent[0]
     for n in final:

from concourse.bass import DstId, RemoteDMATransfer
from concourse.mybir import AluOpType as A, ActivationFunctionType as F

N, RO = 4, 3
H = "float16"
B = 2.0 ** 24
BIG = 2.0 ** 45
CFG = {"zr0": ("V" * 16, "V" * 16), "zr": ("S" * 16, "C" * 16, "C" * 6 + "V" * 10), "ex2": "VVV", "mg0": "SSSS", "mg": "SSSS", "rs0": (0, 0), "rs": (0, 0),
       "rr": "S", "passes": 6, "cy": 0.9e-3, "ga": 1.6, "sem": 0.12, "hop": 2.9, "first": 1.0}

SCRATCH = {}


def _decl(where, dtype, spec):
    for item in spec.split():
        name, shape = item.split(":")
        SCRATCH[name] = (where, [128] + [int(v) for v in shape.split("x")], dtype)


F16 = "df nf thr thq ts tT tr Tt m1 P f16 tA A1 mx".split()
I16 = "win ix ai a15 ui uq u9 ow c2a c2 li lb im cn ci".split()
_decl("sbuf", "bfloat16", "X:2048 zz:1536 W:8192 R:4096 G:4096 ZR:4096 Zs:512 Z:3840 Ip:128 "
      "I:128 nI:128 BI:128 BO:128 E:256 E2:512 H0:512 H1:512 Rx:112 Wu:128 Wz:144 irow:128 irw:128 one:128 sel:8 "
      "xa:16x17 xb:16x17 ma:32x9 mb:32x9 crow:16 srow:128 aw:128 rr:256 mk:512 oa:256 nk:32 f:32 "
      "oh:768 Lc:256 Hs:16x64 t0:512 t1:512 t2:256 r8:256 ra:256 r16:256 ex2:256 Q:256 Qa:256 Qb:256 s16:8")
_decl("sbuf", H, "If:128 nIf:128 hIf:128 BOf:128 onef:128 vrow:128 drow:128 Mf:256 kcf:256 pp:512 EM:256 c2h:16")
_decl("sbuf", "float32", "K:512 Mof:256 pm:8 sel8:8 xs:256 asn:256 kxs:256 msn:256 kms:256 tt:32 pf:224 q:32 qe:32 ek:32 cand:32 "
      "ex:256 ry:256 Kt:256 Ka:512 nIq:128 Iq:128 Wd:272 rc:64 ra2:64 om:32 wc:2 wi:4 sl:4 s1:16")
_decl("sbuf", "int32", "Ki:512 pn:240 o8:48 ms4:4x64 ci4:4x4 si:256 sh:256 hh:256 pi:16 oi:16")
_decl("sbuf", "uint16", "Mu:768 Mo:512 cu:48 co:32 kcu:256 b16:16 b2:16 il:16 zl:16 ol:16 el:16 al:16 tl:16 wl:32")
_decl("psum", "float32", "BX:16x17 BM:56x9 DA:16x32 DB:16x32 DC:16x32 BA:512 BB:512 BL:512")

MSGS = [k + str(r) for r in (1, 2) for k in "zMc"]
SEMAPHORES = ["V", "S", "P", "C", "sent"] + ["d%d" % i for i in range(40)] + [m + "l%d" % l for m in MSGS for l in range(N)]
ZAT = {(0, 0): 0, (1, 0): 4, (0, 1): 8, (0, 2): 12, (1, 1): 16, (1, 2): 20}


def piece(T, kind, side, r, l0=0, n=N):
    if kind == "z":
        o = ZAT[side, r] + l0
        return T.zz[:, 64 * o:64 * (o + n)]
    w = 4 if kind == "c" else 64
    b = T[{"M": ("Mu", "Mo"), "c": ("cu", "co")}[kind][side]]
    return b[:, w * (N * r + l0):w * (N * r + l0 + n)]


def block(l, r):
    return (l // 2 + 2 * (l % 2) + r) % N


def home(r):
    return [l for l in range(N) if block(l, r) == 0][0]


def routes(T, topo, rank, r):
    me, out, used = T.cores[rank], [], []
    for l in range(N):
        h = block(l, r - 1)
        if h == 0:
            continue
        dst = T.cores[(rank + h) % N]
        if topo.may_write(me, dst):
            out.append((l, dst, None))
            continue
        can = [c for c in topo.cores_of(me) if c != me and T.rank_of(c) is None and topo.may_write(c, dst) and c not in used]
        can.sort(key=lambda c: topo.die(c) != topo.die(me))
        used.append(can[0])
        out.append((l, dst, can[0]))
    return out


def engine_split(topo, me, rt):
    off = 0
    for l, dst, via in rt:
        if via is None:
            off |= topo.mask(me, dst)
    vias = [x[0] for x in rt if x[2] is not None]
    res = {}
    for l, dst, via in rt:
        if via is None:
            res[l] = topo.engines(me, dst)
        else:
            free = [e for e in topo.engines(me, via) if not off >> e & 1]
            n = len(free) // len(vias)
            res[l] = free[vias.index(l) * n:(vias.index(l) + 1) * n]
    return res


PLAN = {}
BANK = ("BX", "BM", "DA", "DB", "DC", "BA", "BB", "BL")


def issue_order(ops):
    n = len(ops)
    pre = [dict() for _ in ops]
    wr, rd = {}, {}
    for i, (q, r, w, t, late) in enumerate(ops):
        for k in r + w:
            if k in wr:
                j = wr[k]
                pre[i][j] = max(pre[i].get(j, 0), ops[j][4].get(k, 0))
        for k in w:
            for j in rd.get(k, []):
                pre[i].setdefault(j, 0)
        for k in r:
            rd.setdefault(k, []).append(i)
        for k in w:
            wr[k], rd[k] = i, []
    suc = [[] for _ in ops]
    for i in range(n):
        pre[i].pop(i, None)
        for j in pre[i]:
            suc[j].append(i)

    def gap(j, i):
        return ops[j][3] + pre[i][j] + (0.0 if ops[j][0] == ops[i][0] == "P" else CFG["sem"])
    last = [ops[i][3] + max(list(ops[i][4].values()) + [0]) for i in range(n)]
    banks = [[k for k in BANK if k in o[1] + o[2]] for o in ops]

    def place(rank, back):
        before, after = (suc, pre) if back else (pre, suc)
        left = [len(b) for b in before]
        ready = [i for i in range(n) if not left[i]]
        t, busy = [0.0] * n, {}
        while ready:
            i = min(ready, key=lambda i: rank[i])
            ready.remove(i)
            q, d = ops[i][0], ops[i][3]
            if back:
                a = max([last[i] - d] + [t[j] + ops[j][3] + gap(i, j) - d for j in suc[i]])
            else:
                a = max([0.0] + [t[j] + gap(j, i) for j in pre[i]])
            taken = sorted(busy.get(q, []) + [(x - CFG["sem"], y + CFG["sem"]) for k in banks[i] for x, y, o in busy.get(k, []) if o != q])
            for x, y in taken:
                if x < a + d - 1e-9 and y > a + 1e-9:
                    a = y
            t[i] = a
            busy.setdefault(q, []).append((a, a + d))
            for k in banks[i]:
                busy.setdefault(k, []).append((a, a + d, q))
            for j in after[i]:
                left[j] -= 1
                if not left[j]:
                    ready.append(j)
        return t
    tail = [0.0] * n
    for i in range(n - 1, -1, -1):
        tail[i] = max([last[i]] + [gap(i, j) + tail[j] for j in suc[i]])
    rank, best = [-x for x in tail], None
    for _ in range(CFG["passes"]):
        t = place(rank, False)
        span = max(t[i] + last[i] for i in range(n))
        if best is None or span < best[0]:
            best = (span, t)
        u = place([-(t[i] + ops[i][3]) for i in range(n)], True)
        rank = [-(u[i] + ops[i][3]) for i in range(n)]
    PLAN["span"] = best[0]
    return sorted(range(n), key=lambda i: (best[1][i], i))


def relay_program(g, core, T, topo):
    total = 0
    for m in MSGS:
        for rank in range(N):
            rt = routes(T, topo, rank, int(m[1]))
            sp = engine_split(topo, T.cores[rank], rt)
            for l, dst, via in rt:
                if via != core:
                    continue
                sem = T.sem[m + "l%d" % l]
                g.wait_ge(sem, len(sp[l]))
                rid, pid = topo.addr(dst, core)
                ap = piece(T, m[0], 0, int(m[1]), l, 1)
                g.remote_dma(ap, ap, sem, T.sem.sent, pid, rid, topo.mask(core, dst))
                total += len(topo.engines(core, dst))
    if total:
        g.wait_ge(T.sem.sent, total)


def rank_program(g, core, T, topo):
    rank = T.rank_of(core)
    if rank is None:
        relay_program(g, core, T, topo)
        return
    Qs = {"V": g.vector, "S": g.scalar, "P": g.tensor, "C": g, "Y": g.sync}
    cnt = {"V": 0, "S": 0, "P": 0, "C": 0}
    seen = {q: {} for q in Qs}
    known = {}
    wr, rd, final, nd, sent = {}, {}, {}, [0], [0]
    s = {n: T.pf[:, 16 * j:16 * j + 16] for j, n in enumerate(F16)}
    s.update({n: T.pn[:, 16 * j:16 * j + 16] for j, n in enumerate(I16)})

    def need(q, tok):
        if seen[q].get(tok[0], 0) < tok[1]:
            Qs[q].wait_ge(T.sem[tok[0]], tok[1])
            seen[q][tok[0]] = tok[1]
            for n, c in known.get(tok, {}).items():
                seen[q][n] = max(seen[q].get(n, 0), c)

    def order(q, r, w):
        toks = {}
        for k in r + w:
            deps = [wr[k]] if k in wr else []
            if k in w or k in BANK:
                deps = deps + [t for t in rd.get(k, []) if k in w or t[0] != q]
            for t in deps:
                if not (q == "P" and t[0] == "P"):
                    toks[t[0]] = max(toks.get(t[0], 0), t[1])
        for n in sorted(toks, key=lambda n: -len(known.get((n, toks[n]), {}))):
            need(q, (n, toks[n]))

    def mark(q, tok, r, w):
        known[tok] = dict(seen[q])
        for k in r:
            rd.setdefault(k, []).append(tok)
        for k in w:
            wr[k], rd[k] = tok, []
        final[tok[0]] = tok[1]

    ops = []
    CY = CFG["cy"]

    def op(q, r, w, f, t):
        r, w = r.split(), w.split()
        ww = [k for k in w if k[0] != "~"]

        def emit():
            order(q, r, ww)
            cnt[q] += 1
            f().then_inc(T.sem[q], 1)
            mark(q, (q, cnt[q]), r, ww)
        if q == "P" and ops[-1][:3] == (q, r, w):
            a = ops.pop()
            ops.append((q, r, w, lambda: (a[3](), emit()), t + a[4], a[5]))
        else:
            ops.append((q, r, w, emit, t, {k: 0.15 for k in w} if q == "P" else {}))

    def dma(q, out, in_, r, w):
        r, w = r.split(), w.split() or ["out%d" % len(ops)]

        def emit():
            order(q, r, w)
            n = "d%d" % nd[0]
            nd[0] += 1
            Qs[q].dma_start(out, in_).then_inc(T.sem[n], 16)
            mark(q, (n, 16), r, w)
        ops.append((q, r, w, emit, 0.06, {k: 1.8 + size(out) / 2000 for k in w}))

    def size(a):
        n = 1
        for d in a.shape[1:]:
            n *= d
        return n

    def wide(*aps):
        return 0.5 if all("16" in str(a.dtype) for a in aps) else 1.0

    v, sc, pe = g.vector, g.scalar, g.tensor

    def cost(n, c, ga):
        return 0.06 + n * CFG["ga"] * ga * CY if ga else max(64, n * c) * CY

    def TT(r, w, out, a, b, o, ga=0):
        op("V", r, w, lambda: v.tensor_tensor(out, a, b, o), cost(size(b), 1 if set(r.split()) & set(BANK) else 2, ga))

    def TS(r, w, out, a, s1, o0, s2=None, o1=None, ga=0):
        t = cost(size(out), wide(out, a), ga)
        if o1 is None:
            op("V", r, w, lambda: v.tensor_scalar(out, a, s1, None, o0), t)
        else:
            op("V", r, w, lambda: v.tensor_scalar(out, a, s1, s2, o0, o1), t)

    def tt(out, a, b, o):
        TT(a + " " + b, out, s[out], s[a], s[b], o)

    def ts(out, a, s1, o0, s2=None, o1=None):
        TS(a, out, s[out], s[a], s1, o0, s2, o1)

    def CP(r, w, out, a, ga=0):
        op("V", r, w, lambda: v.tensor_copy(out, a), cost(size(a if ga > 1 else out), wide(out, a), ga))

    def MS(w, out, c):
        op("V", "", w, lambda: v.memset(out, c), cost(size(out), wide(out), 0))

    def SCAN(r, w, out, d0, d1, o0, o1, init=0.0):
        op("V", r, w, lambda: v.tensor_tensor_scan(out, d0, d1, init, o0, o1), cost(size(out), 1, 0))

    def ACT(r, w, out, a, f=F.Copy, ga=0, **kw):
        op("S", r, w, lambda: sc.activation(out, a, f, **kw), cost(size(out), 1, ga))

    def MM(r, w, out, l, rh, st, sp):
        op("P", r, w, lambda: pe.matmul(out, l, rh, st, sp), max(min(64, size(l)), size(rh)) * (4 if "32" in str(l.dtype) else 1) * CY / 2)

    def IO(w, out, pat, base=0, cm=0, flt=True):
        if flt:
            op("C", "", w, lambda: g.iota(out, pat, base, cm, allow_small_or_imprecise_dtypes=True), 0.15 + 2 * CY * size(out))
        else:
            op("C", "", w, lambda: g.iota(out, pat, base, cm), 0.15 + 2 * CY * size(out))

    def SEL(r, w, out, a, pat, o, base, cm, fill=0.0):
        op("C", r, w, lambda: g.affine_select(out, a, pat, o, fill, base, cm), 0.2 + 2 * CY * size(out))

    def COPY(q, r, w, out, a, ga=0):
        if q == "V":
            CP(r, w, out, a, ga)
        elif q == "S":
            ACT(r, w, out, a, F.Copy, ga)
        else:
            SEL(r, w, out, a, [[0, size(out)]], A.is_ge, 0, 0)

    def send(kind, r, src):
        hop = CFG["hop"] + (CFG["first"] if r == 1 else 0)
        hops = {"%s%d.%d" % (kind, r, l): hop if via is None else 2 * hop + 0.6 for l, dst, via in routes(T, topo, rank, r)}
        ops.append(("C", [src], list(hops) + ["sends"], lambda: send_now(kind, r, src), 0.6, hops))

    def send_now(kind, r, src):
        m = kind + str(r)
        rt = routes(T, topo, rank, r)
        sp = engine_split(topo, core, rt)
        order("C", [src], [])
        trs = []
        for l, dst, via in rt:
            rid, pid = topo.addr(dst if via is None else via, core)
            trs.append(RemoteDMATransfer(dst_ids=[DstId(rid=rid, pnc=pid)], dma_engine_mask=sum(1 << e for e in sp[l]),
                                         remote_sem=T.sem[m + "l%d" % l], src=piece(T, kind, 1, r - 1, l, 1), dst=piece(T, kind, 0, r, l, 1)))
            sent[0] += len(sp[l])
        g.remote_dma_fused(trs, local_sem=T.sem.sent)
        for l in range(N):
            h = block(l, r - 1)
            if h:
                frm = (rank - h) % N
                via = [x[2] for x in routes(T, topo, frm, r) if x[0] == l][0]
                n = len(topo.engines(T.cores[frm] if via is None else via, core))
                wr["%s.%d" % (m, l)] = (m + "l%d" % l, n)
                final[m + "l%d" % l] = n

    def tile(b, t, w=128):
        return b[:, w * t:w * t + w]

    def at(kind, r, l):
        if r and l == home(r - 1):
            return piece(T, kind, 1, r - 1, l, 1), "%so%d" % (kind, r - 1)
        return piece(T, kind, 0, r, l, 1), "%s%d.%d" % (kind, r, l)

    def zparts(r, t):
        if r and home(r - 1) // 2 == t:
            return [(l, 1) + at("z", r, l) for l in (2 * t, 2 * t + 1)]
        return [(2 * t, 2, piece(T, "z", 0, r, 2 * t, 2), "z%d.%d z%d.%d" % (r, 2 * t, r, 2 * t + 1))]

    XX = "X.0 X.1 X.2 X.3"

    dma("Y", T.ms4[:], T.ms[:], "", "ms4")
    dma("S", T.X[:, 0:1024], T.tx[:, 0:1024], "", "X.0 X.1")
    dma("Y", T.X[:, 1024:2048], T.tx[:, 1024:2048], "", "X.2 X.3")
    dma("S", T.Ki[:], T.kt[:], "", "K")
    dma("Y", T.ci4[:], T.cp[:], "", "ci4")
    for l in range(N):
        dma("SY"[l // 2], piece(T, "z", 0, 0, l, 1), tile(T.z, block(l, 0), 64), "", "z0.%d" % l)
    for t in (0, 1):
        CP("ms4", "M0.%d M0.%d" % (2 * t, 2 * t + 1), piece(T, "M", 0, 0, 2 * t, 2), T.ms4[:, t::2, :])
        CP("ci4", "c0.%d c0.%d" % (2 * t, 2 * t + 1), piece(T, "c", 0, 0, 2 * t, 2), T.ci4[:, t::2, :])

    def consts():
        p16 = T.pm[:, 0:1]
        IO("one", T.one[:], [[0, 128]], 1)
        SEL("one", "I", T.I[:], T.one[:], [[-1, 128]], A.is_equal, 0, 1)
        SEL("one", "s1", T.s1[:, 0:8], T.one[:, 0:8], [[-16, 8]], A.is_ge, 0, 1)
        SEL("s1", "sel8", T.sel8[:], T.s1[:, 0:8], [[16, 8]], A.is_ge, 15, -1)
        IO("irow", T.irow[0:32, :], [[1, 128]])
        IO("irw", T.irw[0:32, :], [[16, 128]])
        IO("xb", T.xb[0:32, :, :], [[0, 16], [1, 17]])
        IO("mb", T.mb[0:32, :, :], [[0, 16], [1024, 2], [128, 9]], 2048)
        IO("pi", T.pi[:, 0:1], [[0, 1]], 0, 1, False)
        IO("t2", T.t2[:], [[0, 16], [1, 16]])
        IO("oi", T.oi[:], [[1, 16]], 0, 0, False)
        MS("Z.0", T.Z[:, 0:896], 0.0)
        for a, o in enumerate((896, 2048, 2944)):
            dma("Y", T.Z[:, o:o + 896], T.Z[:, 0:896], "Z.0", "Z.%d" % (a + 1))
        dma("Y", T.r16[:], T.Z[:, 0:256], "Z.0", "r16")
        dma("Y", T.r8[:], T.Z[:, 0:256], "Z.0", "r8")
        dma("Y", T.Zs[:], T.Z[:, 0:512], "Z.0", "Zs Zs.0 Zs.1 Zs.2 Zs.3")
        SEL("one", "Ip", T.Ip[:], T.one[:], [[-1, 16], [-16, 8]], A.is_equal, 0, 1)
        IO("ra", T.ra[:], [[0, 256]], 16)
        IO("s2", T.Wd[0:32, 0:128], [[0, 8], [37, 16]])
        IO("t1", T.t1[:], [[0, 64], [1, 8]])
        IO("t0", T.t0[:], [[0, 2], [1, 32], [0, 8]])
        for r in range(RO):
            IO("o8", tile(T.o8, r, 16), [[512, 2], [1024, 2], [128, 4]], 512 * r, 8, False)
        IO("crow", T.crow[0:32, :], [[4096, 2], [0, 8]])
        IO("Wd1", T.Wd[:, 256:272], [[0, 16]])
        IO("sl0", T.pi[:, 8:12], [[64, 4]], 0, 1, False)
        IO("b20", T.pn[:, 0:16], [[0, 8], [-1, 2]], 0, 0, False)

        ACT("I", "nI", T.nI[:], T.I[:], scale=-1.0)
        for b, c, o in (("xa", 1.0, T.xa[0:32, :, :]), ("ma", 1.0, T.ma[0:32, :, :])):
            MS(b, o, c)
        for b, c, o in (("xa", 0.0, T.xa[0:32, :, 16]), ("xb", 0.0, T.xb[0:32, :, 16]), ("ma", 0.0, T.ma[0:32, :, 8]), ("mb", -960.0, T.mb[0:32, :, 8])):
            MS(b, o, c)
        for h in (0, 1):
            ACT("sel8", "Rx", T.Rx[:, 16 * h:16 * h + 16:2], T.sel8[:], scale=4096.0)
            ACT("sel8", "Rx", T.Rx[:, 16 * h + 1:16 * h + 16:2], T.sel8[:], scale=B * (2 * h - 1))
        ACT("sel8", "Rm", T.Rx[:, 96:112:2], T.sel8[:], scale=2048.0)
        ACT("sel8", "Rm", T.Rx[:, 97:112:2], T.sel8[:], scale=128.0)
        ACT("Rx", "Rx1", T.Rx[:, 32:64], T.Rx[:, 0:32], scale=-1.0)
        ACT("Rx", "Rx2", T.Rx[:, 64:96], T.Rx[:, 0:32], scale=2.0)
        MS("r16", T.r16[:, 0::16], BIG)
        MS("r8", T.r8[:, 0::8], BIG)
        MS("ra", T.ra[:, 0::16], -BIG)

        TS("pi", "pi1", T.pi[:, 1:2], T.pi[:, 0:1], 15, A.bitwise_and)
        TS("pi", "pi2", T.pi[:, 2:3], T.pi[:, 0:1], 1, A.arith_shift_right, 7, A.bitwise_and)
        TS("pi", "pi3", T.pi[:, 3:4], T.pi[:, 0:1], 1, A.bitwise_and)
        TS("pi", "pi4", T.pi[:, 4:5], T.pi[:, 0:1], 64, A.bitwise_and)
        TS("pi", "pi5", T.pi[:, 5:6], T.pi[:, 0:1], 112, A.bitwise_and)
        CP("pi1 pi2 pi3 pi4 pi5", "pm", T.pm[:, 0:5], T.pi[:, 1:6])
        TS("pm", "pm5", T.pm[:, 5:6], p16, 2.0, A.mult, 1.0, A.add)
        TS("pm", "pm6", T.pm[:, 6:7], p16, 16.0, A.add)
        TS("pm", "pm7", T.pm[:, 7:8], T.pm[:, 4:5], -8.0, A.mult)
        TS("t2 pm", "E", T.E[:], T.t2[:], p16, A.is_equal)
        CP("oi", "b16", T.b16[:], T.oi[:])
        TS("b20 pm5", "b2 win", T.b2[:], T.pn[:, 0:16], T.pm[:, 5:6], A.add)
        CP("I", "If", T.If[:], T.I[:])
        TS("I", "nIf", T.nIf[:], T.I[:], -1.0, A.mult)
        TS("I", "hIf", T.hIf[:], T.I[:], 0.5, A.mult)
        TS("s2", "vrow", T.vrow[0:32, :], T.Wd[0:32, 0:128], -1023.5, A.add)
        CP("s2", "drow Wd", T.drow[0:32, :], T.Wd[0:32, 0:128])
        MS("onef", T.onef[0:32, :], 1.0)
        ACT("sel8 b16", "BO", T.BO[:], T.sel8[:].indirect(T.b16[:, 0:8]), F.Copy, 1)
        CP("BO", "BOf", T.BOf[:], T.BO[:])
        ACT("BO pm5", "Wu", T.Wu[:], T.BO[:], scale=T.pm[:, 5:6])
        MS("Wz", T.Wz[:], 0.0)
        ACT("sel8 pm5", "Wz", T.Wz[:, 15:143:16], T.sel8[:], scale=T.pm[:, 5:6])
        ACT("I", "nIq", T.nIq[:], T.I[:], scale=-1.0)
        ACT("I", "Iq", T.Iq[:], T.I[:])
        ACT("I", "BI", T.BI[:], T.I[:], scale=2 * B)
        ACT("one", "aw", T.aw[:], T.one[:], scale=8 * B)
        ACT("sel8", "sel", T.sel[:], T.sel8[:])
        ACT("sel8", "s16", T.s16[:], T.sel8[:], scale=1 / 16)
        TS("o8 pm7", "o8", T.o8[:], T.o8[:], T.pm[:, 7:8], A.add)
        TS("o8", "o8", T.o8[:, 0:32], T.o8[:, 0:32], 2047, A.bitwise_and)
        TS("o8", "o8", T.o8[:, 32:48], T.o8[:, 32:48], 511, A.bitwise_and)
        TS("t1 pm", "E2", T.E2[:], T.t1[:], T.pm[:, 1:2], A.is_equal)
        TS("t0 pm", "H0", T.H0[:], T.t0[:], p16, A.is_equal)
        TS("t0 pm6", "H1", T.H1[:], T.t0[:], T.pm[:, 6:7], A.is_equal)
        TS("sl0 pm", "sl0", T.pi[:, 8:12], T.pi[:, 8:12], T.pm[:, 3:4], A.add)
        TS("sl0", "sl1", T.pi[:, 12:16], T.pi[:, 8:12], 255, A.bitwise_and)
        CP("sl1", "sl", T.sl[:], T.pi[:, 12:16])
        MS("Qa", T.Qa[0:32, :], 0.25)
        MS("Qb", T.Qb[0:32, :], 0.0)
        MS("Qa", T.Qa[0:32, 2::4], 0.5)
        MS("Qb", T.Qb[0:32, 0::128], 2.0 ** 59)
        TS("Qb", "Qb", T.Qb[0:32, 0::128], T.Qb[0:32, 0::128], 2.0 ** 59, A.mult)
        MS("Qa", T.Qa[0:32, 64::128], 2.0 ** -10)
        MS("Qa", T.Qa[0:32, 0::128], 0.0)
        SCAN("Qa Qb", "Q", T.Q[0:32, :], T.Qa[0:32, :], T.Qb[0:32, :], A.mult, A.add)
        for j in (0, 1):
            MM("Q one", "BL", T.BL[:, 2 * j:2 * j + 2], T.Q[0:1, 64 * j:64 * j + 128], T.one[0:1, 0:2], True, True)
        ACT("BL", "wc", T.wc[:], T.BL[:, 0:4:2])
        for j in (0, 1):
            ACT("sl wc", "wi", T.wi[:, 2 * j:2 * j + 2], T.sl[:, 2 * j:2 * j + 2], scale=T.wc[:, j:j + 1])
        MS("srow", T.srow[0:32, :], 2.0 ** -124)
        for t in (0, 1):
            MS("srow", T.srow[0:32, 64 * t + 32:64 * t + 64], 2.0 ** -116)

    def m_gather(q, r, l):
        b, k = at("M", r, l)
        COPY(q, XX + " " + k, "G.%d ~g%s" % (l, q), tile(T.G, l, 1024), T.X[:].indirect(b), 1)

    def m_float(r):
        far = 2 * (1 - home(r - 1) // 2) if r else 2
        for l, n in ([(far, 2), (far ^ 2, 1), (far ^ 3, 1)] if r else [(0, 2), (2, 2)]):
            if n == 1:
                b, k = at("M", r, l)
            else:
                b, k = piece(T, "M", 0, r, l, 2), "M%d.%d M%d.%d" % (r, l, r, l + 1)
            CP(k, " ".join("Mf.%d" % j for j in range(l, l + n)), T.Mf[:, 64 * l:64 * (l + n)], b)

    def key_init():
        MM("irow ma", "BM", T.BM[:, 0:32, :], T.irow[0:1, :], T.ma[0:1, :, :], True, False)
        MM("one mb", "BM", T.BM[:, 0:32, :], T.one[0:1, :], T.mb[0:1, :, :], False, False)
        MM("irw xa", "BX", T.BX[:], T.irw[0:1, :], T.xa[0:1, :, :], True, False)
        MM("one xb", "BX", T.BX[:], T.one[0:1, :], T.xb[0:1, :, :], False, False)

    DB = ("DA", "DB", "DC")

    def m_chunk(r, t, c, D, last):
        zs = zparts(r, t)
        rk = "I nI G.%d G.%d " % (2 * t, 2 * t + 1) + " ".join(x[3] for x in zs)
        for j in range(4):
            k = 4 * c + j
            MM(rk, D, T[D][:, 4 * j:4 * j + 4, :], T.I[:], T.G[:, 2048 * t + k:2048 * t + 2048:16], True, False)
            for l, n, z, zk in zs:
                o = 4 * j + 2 * (l % 2)
                MM(rk, D, T[D][:, o:o + 2 * n, :], T.nI[:], z, False, l + n == 2 * t + 2)
        o = 4096 * t + 2048 + 512 * c
        ACT(D, "W.m%d%d" % (t, c), T.W[:, o:o + 512], T[D][:], F.Abs, scale=2.0)
        for j in range(4):
            k = 4 * c + j
            MM("Rm W.m%d%d" % (t, c), "BM", T.BM[:, 16 * t + k // 8:16 * t + 16:2, k % 8:9:8 - k % 8], tile(T.W, o // 128 + j), T.Rx[:, 96:112], False, last and j == 3)

    def zr(l):
        return " ".join("ZR.%d.%d" % (l, k) for k in range(16))

    def z_rep(part, qs):
        l, n, z, zk = part
        for k in range(16):
            COPY(qs[k], zk, " ".join("ZR.%d.%d" % (j, k) for j in range(l, l + n)), T.ZR[:, 1024 * l + k:1024 * (l + n):16], z)

    def z_window(t):
        COPY("C", " ".join(zr(l) for l in range(N)), "Zs.%d Zs.%d" % (2 * t, 2 * t + 1), T.Zs[:, 256 * t:256 * t + 128], T.ZR[:, 2048 * t:2048 * t + 2048:16])

    def kwin(r):
        return T.K if r else T.Ki

    def kc(r, l):
        b, k = at("c", r, l)
        CP("K " + k, "kcu%d" % l, tile(T.kcu, l, 64), kwin(r)[:].indirect(b), 1)

    def kc_tile(r, t):
        CP("K c%d.%d c%d.%d" % (r, 2 * t, r, 2 * t + 1), "kcu%d kcu%d" % (2 * t, 2 * t + 1), tile(T.kcu, t), kwin(r)[:].indirect(piece(T, "c", 0, r, 2 * t, 2)), 1)

    def x_lane(l):
        o = 4096 * (l // 2) + 1024 * (l % 2)
        TT(XX + " kcu%d " % l + zr(l), "W.x%d ~x" % l, T.W[:, o:o + 1024], T.X[:].indirect(tile(T.kcu, l, 64)), tile(T.ZR, l, 1024), A.subtract, 1)

    def x_keys(t, src, rk, j, last):
        for k in range(16):
            MM(rk, "BX", T.BX[:, 8 * t:8 * t + 8, k:17:16 - k], src[:, k:2048:16], tile(T.Rx, 2 * j + k // 8, 16), False, last and k == 15)

    def x_tile(t, ns, last):
        w, rl = T.W[:, 4096 * t:4096 * t + 2048], tile(T.R, t, 2048)
        x_keys(t, w, "Rx1 W.x%d W.x%d" % (2 * t, 2 * t + 1), 1, False)
        for l in (0, 1):
            a, b = 1024 * l, 1024 * l + 1024
            m = min(max(ns - a, 0), 1024) + a
            if m > a:
                ACT("W.x%d" % (2 * t + l), "R.s%d" % (2 * t + l), rl[:, a:m], w[:, a:m], F.Relu)
            if m < b:
                TS("W.x%d" % (2 * t + l), "R.%d" % (2 * t + l), rl[:, m:b], w[:, m:b], 0.0, A.max)
        x_keys(t, rl, "Rx2 " + " ".join("R.%d R.s%d" % (l, l) for l in (2 * t, 2 * t + 1)), 2, last)

    MF = "Mf.0 Mf.1 Mf.2 Mf.3"

    def clanes(r):
        return " ".join("c%d.%d" % (r, l) for l in range(N))

    def add_u(r, t, bank, o):
        for l, n, z, zk in zparts(r, t):
            MM("Wu " + zk, bank, o[64 * (l % 2):64 * (l % 2 + n), :], z, T.Wu[:], False, False)

    def early(r):
        CP("kcu0 kcu1 kcu2 kcu3", "kcf", T.kcf[:], T.kcu[:])
        TS(clanes(r), "c2a", s["c2a"], piece(T, "c", 0, r), 2.0, A.mult)
        ts("c2", "c2a", 511, A.bitwise_and)
        TS("c2", "c2h", T.c2h[:], s["c2"], 512.0, A.add)
        for t in (0, 1):
            o = tile(T.BB, t)
            MM("kcf If", "BB", o, tile(T.kcf, t), T.If[:], True, False)
            add_u(r, t, "BB", o)
            MM("onef vrow", "BB", o, T.onef[0:1, :], T.vrow[0:1, :], False, True)
        C = 1.5 * 2.0 ** 34
        if CFG["rr"] == "S":
            ACT("BB", "ry", T.ry[:], T.BB[:, 0:256], F.Identity, bias=C)
            ACT("ry", "rr", T.rr[:], T.ry[:], F.Identity, bias=-C)
        else:
            TS("BB", "rr", T.rr[:], T.BB[:, 0:256], C, A.add, -C, A.add)
        for t in (0, 1):
            o = tile(T.BA, t)
            MM("kcf If", "BA", o, tile(T.kcf, t), T.If[:], True, False)
            MM("nIf " + MF, "BA", o, tile(T.Mf, t), T.nIf[:], False, True)
        for t in (0, 1):
            o = tile(T.BA, 2 + t)
            MM("kcf If", "BA", o, tile(T.kcf, t), T.If[:], True, False)
            MM("nIf " + MF, "BA", o, tile(T.Mf, t), T.nIf[:], False, False)
            add_u(r, t, "BA", o)
            MM("onef drow", "BA", o, T.onef[0:1, :], T.drow[0:1, :], False, False)
            MM("nI rr", "BA", o, T.nI[:], tile(T.rr, t), False, True)
        MM("hIf " + MF, "BB", T.BB[:, 256:512], T.hIf[:], T.Mf[:], True, False)
        MM("hIf kcf", "BB", T.BB[:, 256:512], T.hIf[:], T.kcf[:], False, False)

    def onehots(r):
        c = piece(T, "c", 0, r)
        for j, wn in enumerate(("E2", "H0", "H1")):
            ACT(clanes(r) + " " + wn, "oh%d" % j, tile(T.oh, j, 256), T[wn][:].indirect(c), F.Copy, 1)
        for t in (0, 1):
            MM("oh0 Ip", "DB", T.DB[:, :, 8 * t:8 * t + 8], tile(T.oh, t), T.Ip[:], True, True)
        ACT("DB", "Lc", T.Lc[:], T.DB[:, :, 0:16])
        for hh in (0, 1):
            for t in (0, 1):
                MM("I oh%d" % (hh + 1), "DA", T.DA[:, 8 * t:8 * t + 8, 16 * hh:16 * hh + 16], tile(T.oh, 2 + 2 * hh + t), T.I[:], True, True)
        for t in (0, 1):
            ACT("DA wc", "Hs%d" % t, T.Hs[:, 8 * t:8 * t + 8, 0:32], T.DA[:, 8 * t:8 * t + 8, :], scale=tile(T.wc, (r + t) // 2, 1))
            ACT("DA wi", "Hu%d" % t, T.Hs[:, 8 * t:8 * t + 8, 32:64], T.DA[:, 8 * t:8 * t + 8, :], scale=tile(T.wi, r + t, 1))
        MM("one srow", "DC", T.DC[:, 0:4, :], T.one[0:1, :], T.srow[0:1, :], True, False)

    TL, AL, A8 = T.BM[:, 32:48, 0], T.BM[:, 32:48, 1], T.BM[:, 32:48, 2]

    def m_side(r):
        ACT("BM", "tt", T.tt[:], T.BM[:, 0:32, 8])
        ACT("BM", "kms", T.kms[:], T.BM[:, 0:32, 0:8], F.Identity, bias=-4096.0)
        TT("tt", "df", s["df"], T.tt[:, 1::2], T.tt[:, 0::2], A.subtract)
        TT("tt", "ts", s["ts"], T.tt[:, 0::2], T.tt[:, 1::2], A.add)
        o = "nf" if r else "thr"
        ACT("df", o, s[o], s["df"], F.Abs, scale=B / 256)
        if r:
            TT("nf BM", "thr", s["thr"], s["nf"], A8, A.add)
        ts("thq", "thr", B, A.max)
        ts("tT", "ts", 1.5 * 2.0 ** 35, A.add, -1.5 * 2.0 ** 35, A.add)
        SCAN("kms r16", "msn", T.msn[:], T.r16[:], T.kms[:], A.add, A.min)
        for h in (0, 1):
            ACT("msn", "ek%d" % h, T.ek[:, h::2], T.msn[:, 15::16], F.Identity, bias=4096.0)

    WALL = "W.x0 W.x1 W.x2 W.x3 " + " ".join("W.m%d%d" % (t, c) for t in (0, 1) for c in range(4))

    def choose(r):
        xm = T.xs[:, 7::8]
        ACT("BX", "kxs", T.kxs[:], T.BX[:, :, 0:16])
        SCAN("kxs r8", "xs", T.xs[:], T.r8[:], T.kxs[:], A.add, A.min)
        TT("BX thr", "q0", T.q[:, 0::2], s["thr"], T.BX[:, :, 16], A.subtract)
        TT("BX thq", "q1", T.q[:, 1::2], s["thq"], T.BX[:, :, 16], A.add)
        TT("xs q0 q1", "cand", T.cand[:], xm, T.q[:], A.max)
        TT("cand", "m1", s["m1"], T.cand[:, 0::2], T.cand[:, 1::2], A.min)
        TT("m1 ek0", "win", s["win"], s["m1"], T.ek[:, 0::2], A.min)
        ts("ix", "win", 4095, A.bitwise_and)
        TT("ix b16 E", "ex", T.ex[:], s["ix"].indirect(T.b16[:]), T.E[:], A.mult, 1)
        MM("one crow", "BL", T.BL[:, 0:16], T.one[0:1, :], T.crow[0:1, :], True, False)
        for t in (0, 1):
            MM("ex sel8", "BL", tile(T.BL, t, 8), tile(T.ex, t), T.sel8[:], False, t == 1)
        CP("BL", "il", T.il[:], T.BL[:, 0:16])
        TS("BL", "zl", T.zl[:], T.BL[:, 0:16], 1 / 16, A.mult, -0.47, A.add)
        TS("BL", "el", T.el[:], T.BL[:, 0:16], 1 / 128, A.mult, -0.496, A.add)
        if r < RO - 1:
            CP("BL", "li", s["li"], T.BL[:, 0:16])
        TT("q0 q1 ek0 ek1", "qe", T.qe[:], T.q[:], T.ek[:], A.max)
        TT("xs qe", "f", T.f[:], xm, T.qe[:], A.is_gt)
        TT("cand ek0 ek1", "nk", T.nk[:], T.cand[:], T.ek[:], A.is_gt)
        SCAN("kxs ra", "asn", T.asn[:], T.ra[:], T.kxs[:], A.add, A.max)

    def features(r):
        zo, k = piece(T, "z", 1, r), "zo%d" % r
        TS(WALL + " il", "hh", T.hh[:], T.W[:].indirect(T.il[:]), -0.5, A.add, 0.5, A.mult, 1)
        TT("Zs Zs.0 Zs.1 Zs.2 Zs.3 zl hh", k, zo, T.Zs[:].indirect(T.zl[:]), T.hh[:], A.add, 1)
        for j in range(16):
            MM("Wz " + k, "BL", T.BL[:, 16:32], T.Wz[:, 15 - j:143 - j], zo[:, j::16], j == 0, j == 15)
        if r == RO - 1:
            for l in range(N):
                dma("Y", tile(T.yz, block(l, r), 64), piece(T, "z", 1, r, l, 1), k, "")
        else:
            send("z", r + 1, k)
        CP("BL", "ui", s["ui"], T.BL[:, 16:32])
        ts("uq", "ui", 7, A.bitwise_and)
        TT("uq o8", "ow", s["ow"], s["uq"], tile(T.o8, r, 16), A.add)
        CP("ow", "ol", T.ol[:], s["ow"])

    def taxa(r):
        k = "zo%d" % r
        if r < RO - 1:
            TT(XX + " ol " + k, "si", T.si[:], T.X[:].indirect(T.ol[:]), piece(T, "z", 1, r), A.add, 1)
            TS("si", "sh", T.sh[:], T.si[:], 1, A.arith_shift_right)
            CP("sh ol", XX, T.X[:].indirect(T.ol[:]), T.sh[:], 2.4)
            return
        for l in range(N):
            h = block(l, r)
            win = tile(T.X, h, 512).indirect(tile(T.ol, l, 4))
            TT("X.%d ol %s" % (h, k), "si%d" % l, tile(T.si, l, 64), win, piece(T, "z", 1, r, l, 1), A.add, 1)
            TS("si%d" % l, "sh%d" % l, tile(T.sh, l, 64), tile(T.si, l, 64), 1, A.arith_shift_right)
            CP("sh%d ol" % l, "X.%d" % h, win, tile(T.sh, l, 64), 2.4)
            dma("Y", tile(T.ytx, h, 512), tile(T.X, h, 512), "X.%d" % h, "")

    def survivors(r):
        ACT("m1", "tr", s["tr"], s["m1"], F.Identity, scale=-512.0, bias=512 * B)
        tt("Tt", "tT", "tr", A.max)
        TT("Tt b16 kms", "mk1", T.mk[:, 256:512], s["Tt"].indirect(T.b16[:]), T.kms[:], A.is_le, 1)
        TT("mk1 BA", "p2", T.pp[:, 256:512], T.BA[:, 256:512], T.mk[:, 256:512], A.mult)
        MM("nIq kms", "DB", T.DB[:, :, 16:32], T.nIq[:], T.kms[:], True, False)
        MM("Iq kxs", "DB", T.DB[:, :, 16:32], T.Iq[:], T.kxs[:], False, False)
        for k in range(8):
            MM("BI nk", "DB", T.DB[:, :, 16 + k:32:8], T.BI[:], T.nk[:], False, k == 7)
        ACT("DB", "mk0", T.mk[:, 0:256], T.DB[:, :, 16:32], F.Sign, scale=-1.0)
        TT("mk0 BA", "p1", T.pp[:, 0:256], T.BA[:, 0:256], T.mk[:, 0:256], A.mult)
        for t in (0, 1):
            MM("If p2", "BB", tile(T.BB, 2 + t), tile(T.pp, 2 + t), T.If[:], False, False)
        for t in (0, 1):
            MM("hIf p1", "BB", tile(T.BB, 2 + t), tile(T.pp, t), T.hIf[:], False, t == 1)
        if r == RO - 1:
            ACT("BB", "Mof", T.Mof[:], T.BB[:, 256:512])
            for l in range(N):
                dma("Y", tile(T.yms, block(l, r), 64), tile(T.Mof, l, 64), "Mof", "")
        else:
            CP("BB", "Mo%d" % r, piece(T, "M", 1, r), T.BB[:, 256:512])
            send("M", r + 1, "Mo%d" % r)

    def couplet_numbers(r):
        ts("lb", "li", 3, A.arith_shift_right, 1, A.bitwise_and)
        ts("im", "li", 1, A.arith_shift_right, 1024, A.bitwise_and)
        TT("lb c2h", "tA", s["tA"], s["lb"], T.c2h[:], A.add)
        tt("A1", "tA", "im", A.subtract)
        ts("u9", "ui", 511, A.bitwise_and)
        tt("cn", "u9", "A1", A.max)
        ts("c2a", "cn", 511, A.bitwise_and)
        CP("c2a", "co%d" % r, piece(T, "c", 1, r), s["c2a"])
        send("c", r + 1, "co%d" % r)
        l = home(r)
        dma("Y", piece(T, "c", 0, r + 1, l, 1), piece(T, "c", 1, r, l, 1), "co%d" % r, "c%d.%d" % (r + 1, l))

    def k_table(r):
        TT("f b2 Lc", "Z", T.Z[:, 1792:2048], T.f[:].indirect(T.b2[:]), T.Lc[:], A.mult, 1)
        for t in (0, 1):
            for j in range(8):
                o = 1792 + 8 * t + j - 256 * j
                MM("Z Z.0 Z.1 Z.2 Z.3 Hs%d Hu%d" % (t, t), "DC", T.DC[:, 2 * t:2 * t + 2, :], T.Z[:, o:o + 2033:16],
                   T.Hs[:, 8 * t + j, :], False, t == 1 and j == 7)
        op("V", "DC", "rc", lambda: v.reciprocal(T.rc[:], T.DC[:, 0:4:2, :]), (230 + 6 * 64) * CY)
        TT("rc DC", "ra2", T.ra2[:], T.rc[:], T.DC[:, 1:4:2, :], A.mult)
        TT("ra2", "om", T.om[:], T.ra2[:, 0:32], T.ra2[:, 32:64], A.min)
        TS("om", "wl", T.wl[:], T.om[:], -0.3, A.add)

    def k_delta(r):
        if r < RO - 1:
            for t in (0, 1):
                for u in range(4):
                    MM("aw f", "BM", T.BM[:, 32 + 8 * t:40 + 8 * t, 2], T.aw[:], T.f[:, 16 * (u // 2) + u % 2:16 * (u // 2) + 16:2], u == 0, u == 3)
        CP("asn", "ai", s["ai"], T.asn[:, 15::16])
        ts("a15", "ai", 15, A.bitwise_and)
        ACT("f", "f16", s["f16"], T.f[:, 0::2], scale=16.0)
        tt("P", "a15", "f16", A.add)
        EX2 = " ".join("ex2.%d" % j for j in range(16))
        if CFG["ex2"][r] == "V":
            TT("P b16 E", EX2, T.ex2[:], s["P"].indirect(T.b16[:]), T.E[:], A.mult, 1)
        else:
            for j in range(16):
                ACT("P E", "ex2.%d" % j, tile(T.ex2, j, 16), T.E[:, 0:16], scale=s["P"][:, j:j + 1])
        MM("If c2h", "BM", TL, T.If[:], T.c2h[:], True, False)
        for t in (0, 1):
            MM(EX2 + " s16", "BM", T.BM[:, 32 + 8 * t:40 + 8 * t, 0], tile(T.ex2, t), T.s16[:], False, t == 1)
        for l in range(N):
            o = 32 + 4 * block(l, r)
            MM(EX2 + " sel", "BM", T.BM[:, o:o + 4, 1], tile(T.ex2, l // 2), tile(T.sel, l % 2, 4), True, True)
        TS("BM", "tl", T.tl[:], TL, -512.47, A.add)
        CP("BM", "al", T.al[:], AL)
        if r:
            ACT("K tl", "Kt", T.Kt[:], T.K[:].indirect(T.tl[:]), F.Copy, 1)
        else:
            CP("K tl", "Kt", T.Kt[:], T.Ki[:].indirect(T.tl[:]), 1)
        ACT("E al", "oa", T.oa[:], T.E[:].indirect(T.al[:]), F.Copy, 1)
        TT("E el " + MF, "EM", T.EM[:], T.E[:].indirect(T.el[:]), T.Mf[:], A.mult, 1)
        for l in range(N):
            o = tile(T.BA, block(l, r), 64)
            MM("BOf EM nIq Kt", "BA", o, T.BOf[:], tile(T.EM, l, 64), True, False)
            MM("BOf EM nIq Kt", "BA", o, T.nIq[:], tile(T.Kt, l, 64), False, True)
        TT("BA oa", "Wd", T.Wd[:, 0:256], T.BA[:, 0:256], T.oa[:], A.mult)

    def k_write(r):
        if r < RO - 1:
            TT("Wd Wd1 wl K", "K", T.K[:], T.Wd[:].indirect(T.wl[:]), kwin(r)[:], A.add, 1)
        else:
            for h in (0, 1):
                TT("Wd Wd1 wl K", "Ka%d" % h, tile(T.Ka, h, 256), T.Wd[:].indirect(tile(T.wl, h, 16)), tile(T.K, h, 256), A.add, 1)
                dma("YS"[h], tile(T.ykt, h, 256), tile(T.Ka, h, 256), "Ka%d" % h, "")

    consts()
    for r in range(RO):
        loc = home(r - 1) if r else 0
        ta, tb = loc // 2, 1 - loc // 2
        sfx = "" if r else "0"
        key_init()
        for j, l in enumerate((loc, loc ^ 1, loc ^ 2, loc ^ 3)):
            m_gather(CFG["mg" + sfx][j], r, l)
        parts = sorted(zparts(r, ta), key=lambda x: x[0] != loc) + zparts(r, tb)
        for part, qs in zip(parts, CFG["zr" + sfx]):
            z_rep(part, qs)
        for t in (0, 1):
            z_window(t)
        if r:
            kc(r, loc)
            kc(r, loc ^ 1)
        else:
            kc_tile(r, ta)
        kc_tile(r, tb)
        m_float(r)
        for i, (t, c) in enumerate([(t, c) for t in (ta, tb) for c in range(4)]):
            m_chunk(r, t, c, DB[i % 3], i == 7)
        for l in (loc, loc ^ 1, loc ^ 2, loc ^ 3):
            x_lane(l)
        for j, t in enumerate((ta, tb)):
            x_tile(t, CFG["rs" + sfx][j], j == 1)
        early(r)
        m_side(r)
        onehots(r)
        choose(r)
        features(r)
        survivors(r)
        k_table(r)
        k_delta(r)
        if r < RO - 1:
            couplet_numbers(r)
        taxa(r)
        k_write(r)
    if "order" not in PLAN:
        PLAN["order"] = issue_order([o[:3] + o[4:] for o in ops])
    for i in PLAN["order"]:
        ops[i][3]()
    final["sent"] = sent[0]
    for n in final:
        need("C", (n, final[n]))
